import numpy as np, ml_dtypes
CORES = [25,29,65,69,153,157,193,197]
N = 8
BF = ml_dtypes.bfloat16
W, I, B, S, RO, H = 4096, 256, 16, 5, 3, 9
def some(rng, k):
    o = np.argsort(rng.random(k.shape[:-1] + (16,) + k.shape[-1:]), axis=-2)
    return np.where(o < k[..., None, :], 0, 255)
def parts(rng):
    x = rng.integers(0, 256, (N, 8, 16, W)); w = rng.integers(0, 16, (N, 8, 16, 1)); c = rng.integers(0, 128, (N, 8, 16, I))
    l = rng.integers(1, 5, (N, 8, 16, I)); s = rng.integers(0, W, (N, 8, 16, I))
    v = rng.choice(np.array([96, 176, 208, 224, 236, 244, 252]), (N, 8, 1, I))
    return x, w, c, l, s, np.clip(v + rng.integers(-12, 13, (N, 8, 16, I)), 0, 255)
def small(a):
    return np.ascontiguousarray(a.reshape(N, 128, -1)).astype(np.float32).astype(BF)
def pack(x, w, c, l, s, fl):
    return {"x": small(x), "wt": small(w), "ch": small(c), "sp": small(l), "st": np.ascontiguousarray(s.reshape(N, 128, I)).astype(np.int32), "fl": small(fl)}
def setup_inputs(rng):
    return pack(*parts(rng))
def setup_inputs_spread(rng):
    x, w, c, l, s, fl = parts(rng)
    x = (np.exp2(8 * rng.random((N, 8, 1, W))) * rng.random(x.shape)).astype(np.int64)
    w = np.where(rng.random(w.shape) < 0.4, 0, w)
    c = np.where(rng.random((N, 8, 1, I)) < 0.5, c, np.exp2(7 * rng.random(c.shape)).astype(np.int64) - 1)
    l = rng.choice(np.array([1, 1, 1, 2, 3, 4]), l.shape)
    fl = (np.exp2(8 * rng.random((N, 8, 1, I))) * (0.5 + 0.5 * rng.random(fl.shape))).astype(np.int64)
    return pack(x, w, c, l, s, fl)
def setup_inputs_ends(rng):
    x, w, c, l, s, fl = parts(rng)
    d = rng.choice(np.array([0.04, 0.1, 0.3, 0.5]), (N, 8, 1, 1)); d[:, 7] = 0.5
    e = 255 * (rng.random(x.shape) < d); k = rng.random((N, 8, 1, W)); full = np.where(np.arange(8) == 7, 0.3, 0.03).reshape(1, 8, 1, 1)
    e = np.where(k < full, 255, np.where(k > 0.85, 0, e)); x = np.where((k > 0.5) & (k < 0.6), x, e)
    w = 15 * rng.integers(0, 2, w.shape); w[:, 7] = 15; w[:, 1] = 0; w[:, 0, 0] = 0; w[:, 0, 15] = 15
    b = rng.random((N, 8, 1, I)); c = np.where(b < 0.15, 127, np.where(b > 0.85, 0, 127 * rng.integers(0, 2, c.shape)))
    l = 1 + 3 * rng.integers(0, 2, l.shape); s = np.where(rng.random(s.shape) < 0.25, s, (W - 1) * rng.integers(0, 2, s.shape))
    fl = some(rng, rng.integers(0, 17, (N, 8, I))); fl[N - 2:] = some(rng, rng.integers(H, 17, (2, 8, I)))
    x[N - 2, 6, H - 1:] = 0; fl[N - 2, 6, :, I - 1] = np.where(np.arange(16) < H - 1, 0, 255)
    l[N - 1, 7, :, :2] = 4; s[N - 1, 7, :, :2] = W - 1
    l[N - 1, 7, 13:, I - 1] = np.array([1, 4, 4]); s[N - 1, 7, 13:, I - 1] = np.array([(0 - 613) & (W - 1), (W - 1 - 2452) & (W - 1), W - 1])
    c[N - 1, 7, 0, :2] = 127; c[N - 1, 7, 0, I - 1] = 127
    x[:, 7, :, (W - 1 + 2452) & (W - 1)] = 255; x[:, 7, :, W - 1] = 255; x[:, 7, 15] = 255
    return pack(x, w, c, l, s, fl)
def setup_inputs_corners(rng):
    x, w, c, l, s, fl = parts(rng); q = rng.permutation(N); ar = np.arange(16)[:, None]
    w[:, 0] = 0; b = rng.integers(0, 4, (N, 1, I)); c[:, 0] = np.where(b == 0, 3, np.where(b == 1, 0, np.where(b == 2, 127, c[:, 0])))
    x[:, 1] = np.minimum(x[:, 1], 254); fl[:, 1] = some(rng, rng.choice(np.array([0, H - 1, H, 16]), (N, I)))
    v = rng.integers(1, 255, (N, 16, 1)); x[:, 2] = v; fl[:, 2] = v + np.minimum(some(rng, rng.choice(np.array([H - 1, H, 16]), (N, I))), 1)
    w[:, 3] = 0; w[:, 3, 0] = 1; x[:, 3, 0, ::2] = 255; fl[:, 3] = fl[:, 3] // 2
    b = rng.integers(0, 4, (N, 1, I)); l[:, 4] = np.where(b == 0, 4, np.where(b == 1, 1, np.where(b == 2, 1 + 3 * (ar == 15), 1 + 3 * (ar & 1)))); fl[:, 4] = fl[:, 4] // 2
    e = (W - 1) * rng.integers(0, 2, (N, 16, I)); s[:, 5] = np.where(rng.random((N, 16, I)) < 0.5, e, (e - 613 * l[:, 5]) & (W - 1))
    w[:, 6] = 15; x[:, 6] = rng.integers(224, 256, (N, 16, W)); c[:, 6] = rng.choice(np.array([0, 126, 127]), (N, 16, I))
    x[q[0]] = np.minimum(x[q[0]], 254); fl[q[0]] = some(rng, np.full((8, I), H - 1))
    fl[q[1]] = some(rng, rng.integers(H, 17, (8, I))); fl[q[2]] = some(rng, rng.integers(H, 17, (8, I)))
    x[q[2], 7] = np.minimum(x[q[2], 7], 254); fl[q[2], 7, :, I - 1] = some(rng, np.full(1, H - 1))[:, 0]
    return pack(x, w, c, l, s, fl)
def setup_inputs_crowd(rng):
    x, w, c, l, s, fl = parts(rng); q = rng.permutation(N)
    s[:, :7] = rng.integers(0, W, (N, 7, 1, 1)); l[:, :7] = rng.integers(1, 5, (N, 7, 1, 1)); c[:, :7] = rng.integers(0, 128, (N, 7, 16, 1))
    s[:, 4:7, 15, I - 1] = rng.integers(0, W, (N, 3)); c[:, 4:7, :, I - 1] = rng.integers(0, 128, (N, 3, 16))
    fl = some(rng, rng.integers(H, 17, (N, 8, I)))
    for a in q[:N // 2]:
        x[a, 7] = np.minimum(x[a, 7], 254); fl[a, 7, :, I - 1] = some(rng, np.full(1, H - 1))[:, 0]
    return pack(x, w, c, l, s, fl)
def setup_inputs_late(rng):
    x, w, c, l, s, fl = parts(rng); q = rng.permutation(N); a, b = int(q[0]), int(q[1])
    x[a] = np.minimum(x[a], 254); fl[a] = some(rng, np.full((8, I), H - 1)); fl[b] = some(rng, rng.integers(H, 17, (8, I)))
    for r, g, low in ((a, 7, 8), (b, 0, 0)):
        hot = B * int(rng.integers(8, I)); w[r, g] = 0
        x[r, g] = rng.integers(0, 101, (16, W)); x[r, g, :, hot] = rng.integers(200, 255, 16)
        fl[r, g, :, low:] = rng.integers(110, 151, (16, I - low))
        l[r, g] = 1; s[r, g] = (hot - 613) & (W - 1)
        if g == 7: l[(a - 2) % N, 7] = 1; s[(a - 2) % N, 7] = (hot - 613) & (W - 1)
    s[(a - 1) % N, 7] = (16 * rng.integers(0, W // 16, (16, I)) - (I - 8)) & (W - 1)
    l[(b - 1) % N, 0] = 1; s[(b - 1) % N, 0] = W - 613 - 8 * I
    c[(b - 1) % N, 0] = 16 * rng.integers(0, 8, (16, I)) + 4 * rng.integers(1, 4, (16, I))
    return pack(x, w, c, l, s, fl)
def check_inputs(d):
    bad = []
    for k, lo, hi in (("x", 0, 255), ("wt", 0, 15), ("ch", 0, 127), ("sp", 1, 4), ("st", 0, W - 1), ("fl", 0, 255)):
        v = np.asarray(d[k]).astype(np.float64)
        if not (np.all(v >= lo) and np.all(v <= hi)): bad.append("range of " + k)
        if np.any(v != np.floor(v)): bad.append("whole numbers of " + k)
    return bad
def reference(x, wt, ch, sp, st, fl):
    X, Q, C, L, Z, F = [v.astype(np.float32).astype(np.int32).reshape(N, 8, 16, -1) for v in (x, wt, ch, sp, st, fl)]
    A = [0] * N; row = np.arange(16)[:, None]
    for t in range(RO):
        if t > 0: C, L, Z = np.roll(C, 1, axis=0), np.roll(L, 1, axis=0), np.roll(Z, 1, axis=0)
        for a in range(N):
            l = L[a]
            at = np.arange(16)[None, :, None, None]; at = at + np.where(at >= row[None, None], l[:, None], 0)
            e = np.take_along_axis(np.concatenate([C[a], np.zeros((8, 4, I), np.int32)], axis=1)[:, :, None, :], at, 1)
            e = np.concatenate([e, np.zeros((8, 1, 16, I), np.int32)], axis=1)
            s = (Z[a] + 613 * l + A[a]) & (W - 1); p = np.zeros((8, 16, I), np.int64); V = np.zeros((8, 16, 16, I), np.int32); log = []
            for k in range(S):
                z = np.take_along_axis(X[a], s.reshape(8, 1, 16 * I), 2).reshape(8, 16, 16, I)
                V = np.maximum(V, z); c = np.take_along_axis(e, np.minimum(p, 16)[:, None], 1)[:, 0].astype(np.int64)
                u = np.add.reduce(Q[a][..., None] * z, axis=1).astype(np.int64)
                n = 1 + (((u >> 3) + c) & 3); log.append((p, n))
                s = (((u * (2 * c + 1)) >> 3) + 37 * u + c) & (W - 1); p = p + n
            fails = np.add.reduce((V >= F[a][:, :, None, :]).astype(np.int32), axis=1) >= H
            best = np.argmax(np.where(fails, 16 * l + 15 - row[None], 0 - 1), axis=1)[:, None, :]; ok = np.any(fails, axis=1)[:, None, :]
            nl = np.ones((8, 16, I), np.int64)
            for p, n in log: nl = np.where(row[None] == np.take_along_axis(p, best, 1), np.take_along_axis(n, best, 1), nl)
            v = np.take_along_axis(V, best[:, None], 2)[:, :, 0]
            C[a] = np.where(ok, np.take_along_axis(e[:, :16], best[:, None], 2)[:, :, 0], C[a]); L[a] = np.where(ok, nl, l)
            to = B * np.arange(I)[None, None, :] + (np.add.reduce(Q[a] * v, axis=1)[:, None, :] & (B - 1))
            to = np.broadcast_to(to, (8, 16, I)); np.put_along_axis(X[a], to, np.where(ok, v, np.take_along_axis(X[a], to, 2)), 2)
            F[a] = np.where(ok, (F[a] + v) >> 1, F[a]); A[a] = int(np.sum(ok))
    sums = np.add.reduce(X.reshape(N, 128, I, B), axis=3)
    return {"yc": C.reshape(N, 128, I).astype(np.float32).astype(BF), "yl": L.reshape(N, 128, I).astype(np.float32).astype(BF),
            "yf": F.reshape(N, 128, I).astype(np.float32).astype(BF), "ys": sums.astype(np.float32)}

@@ -1,0 +1,542 @@
+from concourse.mybir import AluOpType as OP, AxisListType, ActivationFunctionType as AF
+
+SLOTS = ["I", "B1", "ON", "LT", "LE", "S1", "S2", "S3", "S4", "E0", "E1", "E2", "E3", "I32", "I512", "I101", "I64", "mI",
+         "I16", "mB1", "mI4", "mB8", "BD32", "B512", "BX32", "BW", "BQ0", "T0", "T1", "T2", "T3", "DG0", "DG3"]
+SLOTS += ["L%d" % e for e in range(15)]
+SLOT = {n: j for j, n in enumerate(SLOTS)}
+BUF = {"bfloat16": "xt_8192 zz_20480 vs_20480 mk5_5120 wl_2064 cl_2064 mo_2064 ff_256 wtb_16 onef_16 e16_16 tmpm_128 k107_128 km1_128 kmh_128 kd_128 junk_128",
+       "float32": "sd_16 jio_16 jt_16 co_24 b8f_8 c80_8 c16_16 ac_16 ysb_256", "int32": "sti_256 tmi_256 tmj_256"}
+BUFH = {"bfloat16": "h0_512 h1_2048 h2_2048 h3_2048 t0_512 dt_2048 sc_2048 rd_640 hn_640 scn_640 gg_1024 c5_128 pt_896 pp_256 "
+                    "msk_256 w3_128 fl_128 fw_128 cand_128 win_128 vsel_128 z4_128 wx_640 ax_384 ex_512 m4_128 t4_128 n4m_128",
+        "float32": "nk_8 f1_128", "int32": "s32_128 x32_128 r32_128 n32_128 nn_128 n4_128 n5_128 o32_8 q32_8", "uint16": "offs_128 ofs_8 of2_8"}
+
+
+def _bufs():
+    out = {"mats": ("sbuf", [128, len(SLOTS) * 128], "bfloat16")}
+    for table, hs in ((BUF, ("",)), (BUFH, ("a", "b"))):
+        for dt, names in table.items():
+            for s in names.split():
+                nm, n = s.split("_")
+                for h in hs:
+                    out[nm + h] = ("sbuf", [128, int(n)], dt)
+    for t in range(3):
+        out["rec%d" % t] = ("sbuf", [128, 1024], "bfloat16")
+        out["nr%d" % t] = ("sbuf", [128, 512], "bfloat16")
+    for h in "ab":
+        out["pu" + h] = out["pm" + h] = ("psum", [128, 512], "float32")
+        out["pd" + h] = ("psum", [128, 1024], "float32")
+    return out
+
+
+SCRATCH = _bufs()
+MSG = [("st", 1), ("st", 2)] + [(k + h, t) for t in (1, 2) for h in "ab" for k in "cl"]
+COLS = {"st": (512, 1024), "ca": (0, 128), "cb": (128, 256), "la": (256, 384), "lb": (384, 512)}
+SEMAPHORES = ["e_v", "e_s", "e_t", "e_g"] + ["ld_" + n for n in ("st", "sp", "wt", "x", "ch", "fl")] + ["o_c", "o_l", "o_f", "o_s"]
+SEMAPHORES += [p + "%s%d" % m for m in MSG for p in ("a_", "b_")]
+KEEP = []
+
+
+def nbits(m):
+    return bin(m).count("1")
+
+
+def relays(src, dst, topo):
+    if topo.may_write(src, dst):
+        return []
+    own = [c for c in topo.cores_of(src) if c != src and topo.may_write(c, dst)]
+    return sorted(own, key=lambda c: (topo.die(c) != topo.die(src), c))
+
+
+def via(msg, src, dst, topo):
+    own = relays(src, dst, topo)
+    return own[(msg[0][-1] == "a") % len(own)] if own else None
+
+
+def cv(n, k):
+    return 55 + max(64, n * k) * 0.95
+
+
+def cs(n, k=1):
+    return 65 + n * k * 0.95
+
+
+def order(nodes):
+    n = len(nodes)
+    pred, succ, lw, rd = [[] for _ in range(n)], [[] for _ in range(n)], {}, {}
+    for j, (alts, r, w, _) in enumerate(nodes):
+        ws = w + [t for t in r if t[0] == "#"]
+        ps = set()
+        for t in r + ws:
+            ps.update(lw.get(t, []) if t[0] != "+" else rd.get(t[1:], []))
+        for t in ws:
+            ps.update(rd.get(t, []))
+        for t in r:
+            rd.setdefault(t, []).append(j)
+        for t in ws:
+            if t[0] == "+":
+                lw.setdefault(t[1:], []).append(j)
+            else:
+                lw[t], rd[t] = [j], []
+        pred[j] = sorted(ps - {j})
+        for p in pred[j]:
+            succ[p].append(j)
+    prio = [0.0] * n
+    for j in range(n - 1, -1, -1):
+        prio[j] = nodes[j][0][0][1] + 80 + max([prio[x] for x in succ[j]] + [0])
+    for j in range(n):
+        if any(t[-1] == "a" for t in nodes[j][2]):
+            prio[j] += 3000
+    left = [len(p) for p in pred]
+    ready = [j for j in range(n) if not left[j]]
+    free, end, qof, out = {}, [0.0] * n, [None] * n, []
+    while ready:
+        c = []
+        for j in ready:
+            best = None
+            for a, alt in enumerate(nodes[j][0]):
+                q, cost = alt[0], alt[1]
+                s = free.get(q, 0.0) if q != "n" else 0.0
+                for p in pred[j]:
+                    s = max(s, end[p] + (20 if qof[p] == q else 80))
+                if best is None or s + cost < best[0]:
+                    best = (s + cost, s, a, q)
+            c.append((best, j))
+        e, j = min(c, key=lambda x: (x[0][1], -prio[x[1]]))
+        t0, q0 = e[1], e[3]
+        e, j = max([x for x in c if x[0][3] == q0 and x[0][1] <= t0 + 30], key=lambda x: (prio[x[1]], -x[1]))
+        fin, s, a, q = e
+        ready.remove(j)
+        end[j], qof[j] = fin, q
+        free[q] = s + 70 if nodes[j][3] == "dma" else fin
+        out.append((s, j, a))
+        for x in succ[j]:
+            left[x] -= 1
+            if not left[x]:
+                ready.append(x)
+    return out
+
+
+def rank_program(g, core, T, topo):
+    N = len(T.cores)
+    rank = T.rank_of(core)
+
+    def put(msg, src_ap, dst):
+        a, b = COLS[msg[0]]
+        rid, pid = topo.addr(dst, core)
+        m = topo.mask(core, dst)
+        g.remote_dma(T["rec%d" % msg[1]][:, a:b], src_ap, T.sem["a_%s%d" % msg], T.sem["b_%s%d" % msg], pid, rid, m)
+        return nbits(m)
+
+    if rank is None:
+        for r in range(N):
+            src, dst = T.cores[r], T.cores[(r + 1) % N]
+            sent = []
+            for msg in [x for x in MSG if via(x, src, dst, topo) == core]:
+                a, b = COLS[msg[0]]
+                g.wait_ge(T.sem["a_%s%d" % msg], nbits(topo.mask(src, core)))
+                sent.append((msg, put(msg, T["rec%d" % msg[1]][:, a:b], dst)))
+            for msg, n in sent:
+                g.wait_ge(T.sem["b_%s%d" % msg], n)
+        return
+
+    nxt, prv = T.cores[(rank + 1) % N], T.cores[(rank - 1) % N]
+    nodes = []
+
+    def add(alts, r, w, kind="op"):
+        nodes.append((alts, list(r), list(w), kind))
+
+    def vop(meth, cost, r, w, *a):
+        add([("v", cost, lambda: {"tt": g.vector.tensor_tensor, "ts": g.vector.tensor_scalar, "tc": g.vector.tensor_copy, "ms": g.vector.memset,
+                                  "sc": g.vector.tensor_tensor_scan, "tr": g.vector.tensor_reduce}[meth](*a))], r, w)
+
+    def tt(out, a, b, op, r, w, c=128):
+        vop("tt", cv(c, 1), r, w, out, a, b, op)
+
+    def ts(out, a, s1, s2, o1, o2, r, w, c=64):
+        vop("ts", cv(c, 1), r, w, *((out, a, s1, s2, o1) if o2 is None else (out, a, s1, s2, o1, o2)))
+
+    def tc(out, a, r, w, c=128):
+        vop("tc", cv(c, 1), r, w, out, a)
+
+    def ms(ap, val, w, c=64):
+        vop("ms", cv(c, 1), [], w, ap, val)
+
+    def scan(out, a, b, o1, r, w, n):
+        vop("sc", cv(n, 0.5), r, w, out, a, b, 0.0, OP.mult, o1)
+
+    def act(out, in_, func, r, w, n=128, k=1, **kw):
+        add([("s", cs(n, k), lambda: g.scalar.activation(out, in_, func, **kw))], r, w)
+
+    def flex(out, in_, func, r, w, n, v, **kw):
+        add([("s", cs(n), lambda: g.scalar.activation(out, in_, func, **kw)),
+             ("v", cv(n, 1), lambda: g.vector.tensor_scalar(out, in_, *v) if v else g.vector.tensor_copy(out, in_))], r, w)
+
+    def gp(meth, r, w, *a, **kw):
+        add([("g", 350, lambda: {"iota": g.iota, "sel": g.affine_select}[meth](*a, **kw))], r, w)
+
+    def fill(nm, n, v, tag):
+        add([("g", 150 + n * 1.9, lambda: g.iota(T[nm][:], [[0, n]], v, 0, allow_small_or_imprecise_dtypes=True))], [], [tag])
+
+    def cpy(out, in_, r, w):
+        add([("g", 420, lambda: g.affine_select(out, in_, [[0, 128]], OP.is_ge, 0.0, 1, 0))], r, w)
+
+    def MM(r, w, items, ns):
+        def f():
+            for o, l, x, s0, s1 in items:
+                i = g.tensor.matmul(o, l, x, s0, s1)
+            return i
+        add([("t", 60 + 0.45 * max(64, ns) * len(items), f)], r, w)
+
+    def grp(out, pairs):
+        return [(out, l, x, j == 0, j == len(pairs) - 1) for j, (l, x) in enumerate(pairs)]
+
+    def M(n):
+        return T.mats[:, SLOT[n] * 128:SLOT[n] * 128 + 128]
+
+    def WM(n, m):
+        return T[n][:, 128 * m:128 * m + 128]
+
+    def dma(q, sem, out, in_, r, w, cost=2600):
+        add([(q, cost, lambda: {"y": g.sync, "s": g.scalar}[q].dma_start(out, in_))], r, w, ("dma", sem, 16))
+
+    dma("s", "ld_st", T.sti[:], T.st[:], [], ["sti"])
+    dma("s", "ld_sp", T.rec0[:, 256:512], T.sp[:], [], ["l0a", "l0b"])
+    dma("s", "ld_wt", T.wtb[:, 0:1], T.wt[:], [], ["wtb"])
+    dma("y", "ld_x", T.xt[:, 0:4096], T.x[:], [], ["x"], 8000)
+    dma("s", "ld_ch", T.rec0[:, 0:256], T.ch[:], [], ["c0a", "c0b"])
+    dma("s", "ld_fl", T.ff[:], T.fl[:], [], ["ffa", "ffb"])
+    ms(M("ON"), 1.0, ["ON"]); ms(T.onef[:], 1.0, ["onef"]); ms(T.wl[:], 0.0, ["wl0"], 1032)
+    for nm in ("h1a", "h1b", "h2a", "h2b"):
+        fill(nm, 2048, 1, nm)
+    fill("mk5", 5120, 1, "mk5"); fill("cl", 2064, 0, "cl0"); fill("mo", 2064, 0, "mo0")
+    for nm, st in (("jio", [[1, 16]]), ("c80", [[1280, 8]]), ("c16", [[256, 16]])):
+        gp("iota", [], [nm], T[nm][:], st, 0, 0, allow_small_or_imprecise_dtypes=True)
+    gp("sel", ["ON"], ["I"], M("I"), M("ON"), [[-1, 128]], OP.is_equal, 0.0, 0, 1)
+    gp("sel", ["ON"], ["tmpm"], T.tmpm[:], M("ON"), [[-16, 8], [0, 16]], OP.is_ge, 0.0, 0, 1)
+    gp("sel", ["tmpm"], ["B1"], M("B1"), T.tmpm[:], [[16, 8], [0, 16]], OP.is_ge, 0.0, 15, -1)
+    gp("sel", ["B1"], ["LT"], M("LT"), M("B1"), [[1, 128]], OP.is_gt, 0.0, 0, -1)
+    gp("sel", ["B1"], ["LE"], M("LE"), M("B1"), [[1, 128]], OP.is_ge, 0.0, 0, -1)
+    for d in (1, 2, 3, 4):
+        gp("sel", ["B1"], ["S%d" % d], M("S%d" % d), M("B1"), [[-1, 128]], OP.is_equal, 0.0, -d, 1)
+    ts(T.tmi[:], T.sti[:], 6, None, OP.arith_shift_right, None, ["sti"], ["tmi"], 256)
+    ts(T.tmj[:], T.sti[:], 63, None, OP.bitwise_and, None, ["sti"], ["tmj"], 256)
+    tc(T.rec0[:, 512:768], T.tmi[:], ["tmi"], ["+s0"], 256)
+    tc(T.rec0[:, 768:1024], T.tmj[:], ["tmj"], ["+s0"], 256)
+    tt(T.junk[:, 0:64], T.mats[:, 0:64], T.mats[:, 64:128], OP.add, ["I"], ["f64"])
+    tt(T.junk[:, 64:96], T.junk[:, 0:32], T.junk[:, 32:64], OP.add, ["f64"], ["f32"])
+    tt(T.e16[:], T.junk[:, 64:80], T.junk[:, 80:96], OP.add, ["f32"], ["e16"])
+    tt(T.jt[:], T.e16[:], T.jio[:], OP.mult, ["e16", "jio"], ["jt"])
+    co = lambda j: T.co[:, j:j + 1]
+    vop("tr", 120, ["jt"], ["co0"], co(0), T.jt[:], AxisListType.X, OP.add)
+    for k in (1, 2, 3):
+        ts(co(k), co(0), float(-k), None, OP.add, None, ["co0"], ["co%d" % k])
+        ts(co(4 + k), co(0), -1.0, float(k), OP.mult, OP.add, ["co0"], ["co%d" % (4 + k)])
+    ts(co(4), co(0), 28.0, None, OP.add, None, ["co0"], ["co4"])
+    ts(co(8), co(0), 5.0, 4.0, OP.mult, OP.add, ["co0"], ["co8"])
+    ts(co(9), T.wtb[:, 0:1], 64.0, None, OP.mult, None, ["wtb"], ["co9"])
+    ts(co(10), co(0), 80.0, None, OP.mult, None, ["co0"], ["co10"])
+    ts(co(11), co(0), 16.0, None, OP.mult, None, ["co0"], ["co11"])
+    ts(co(12), T.e16[:, 0:1], 1.0, None, OP.mult, None, ["e16"], ["co12"])
+    ts(co(14), T.e16[:, 4:5], 0.03125, None, OP.mult, None, ["e16"], ["co14"])
+    ts(co(13), T.e16[:, 0:1], -1.0, 1.0, OP.mult, OP.add, ["e16"], ["co13"])
+    ts(T.c80[:], T.c80[:], co(10), None, OP.add, None, ["co10", "c80"], ["c80"])
+    ts(T.c16[:], T.c16[:], co(11), None, OP.add, None, ["co11", "c16"], ["c16"])
+    b8 = SLOT["B1"] * 128
+    tc(T.b8f[:], T.mats[:, b8:b8 + 113:16], ["B1"], ["b8f"])
+    for gi in range(8):
+        colb = T.b8f[:, gi:gi + 1]
+        sl = slice(16 * gi, 16 * gi + 129 * 15 + 1, 129)
+        ts(T.wl[:, sl], T.onef[:], co(9), colb, OP.mult, OP.mult, ["onef", "co9", "b8f", "wl0"], ["+wl"])
+        ts(T.cl[:, sl], T.onef[:], colb, None, OP.mult, None, ["onef", "b8f", "cl0"], ["+cl"])
+        ts(T.mo[:, sl], T.onef[:], co(8), colb, OP.mult, OP.mult, ["onef", "co8", "b8f", "mo0"], ["+mo"])
+    tt(T.jt[:, 1:15], T.e16[:, 1:15], T.e16[:, 2:16], OP.subtract, ["e16", "co0"], ["+jd"])
+    tc(T.jt[:, 15:16], T.e16[:, 15:16], ["e16", "co0"], ["+jd"])
+    tc(T.jt[:, 0:1], T.e16[:, 0:1], ["e16", "co0"], ["+jd"])
+    ts(T.sd[:], T.jt[:], 0.03125, None, OP.mult, None, ["jd"], ["sd"])
+
+    def mat(dst, src, f, r2=()):
+        add([("v", cv(64, 1), lambda: g.vector.tensor_scalar(M(dst), M(src), f, None, OP.mult)),
+             ("s", cs(128), lambda: g.scalar.activation(M(dst), M(src), AF.Copy, scale=f))], [src] + list(r2), [dst])
+
+    for nm, f in (("I512", 512.0), ("I101", 101.0), ("I64", 64.0), ("I32", 32.0), ("mI", -1.0), ("I16", 16.0), ("mI4", -4.0)):
+        mat(nm, "I", f)
+    mat("T0", "B1", T.sd[:, 0:1], ["sd"])
+    for e in range(4):
+        nm = "T%d" % e
+        if e:
+            ms(M(nm), 0.0, [nm])
+        o = SLOT[nm] * 128
+        ts(T.mats[:, o:o + 113:16], T.mats[:, b8:b8 + 113:16], T.sd[:, e + 1:e + 2] if e < 3 else co(14), None, OP.mult, None, ["B1", "sd", "co14"], [nm])
+    mat("DG0", "I", co(13), ["co13"]); mat("DG3", "I", co(12), ["co12"])
+    for nm, v in (("kd", -215.0 / 64), ("k107", 107.5), ("km1", -1.0), ("kmh", -0.5)):
+        ms(T[nm][:], v, [nm])
+    for e in range(15):
+        mat("L%d" % e, "B1", T.sd[:, e + 1:e + 2], ["sd"])
+    for nm, f in (("mB1", -1.0), ("mB8", -8.0), ("BD32", 0.03125), ("B512", 512.0), ("BX32", 32.0)):
+        mat(nm, "B1", f)
+    mat("BW", "B1", co(9), ["co9"])
+    for d in range(4):
+        s0 = "S%d" % d if d else "I"
+        tt(M("E%d" % d), M(s0), M("S%d" % (d + 1)), OP.subtract, [s0, "S%d" % (d + 1)], ["E%d" % d], 256)
+    ms(M("BQ0"), 0.0, ["BQ0"])
+    o = SLOT["BQ0"] * 128
+    tc(T.mats[:, o:o + 113:16], T.mats[:, b8:b8 + 113:16], ["B1"], ["BQ0"])
+    ms(T.mk5[:, 0:5120:5], 0.0, ["mk5"], 1024)
+    ms(T.ac[:, 0:1], 0.0, ["ac0"])
+    for h in "ab":
+        ms(T["msk" + h][:], 0.0, ["mskz" + h], 128); ms(T["h0" + h][:], 0.0, ["h0z" + h], 256); ms(T["hn" + h][:], 0.0, ["hnz" + h], 320)
+        for k in (1, 2, 3):
+            for e in range(k):
+                ms(T["h%d%s" % (k, h)][:, e:2048:16], 0.0, ["h%d%s" % (k, h)])
+
+    sends = []
+
+    def send(msg, ap, tags):
+        def f():
+            sends.append(("b_%s%d" % msg, put(msg, ap, via(msg, core, nxt, topo) or nxt)))
+        add([("g", 1500, f)], tags, ["sent%s%d" % msg], ("send",))
+        tag = {"st": "s%d", "ca": "c%da", "cb": "c%db", "la": "l%da", "lb": "l%db"}[msg[0]] % msg[1]
+        add([("n", 3500, None)], ["sent%s%d" % msg], [tag], ("arr", "a_%s%d" % msg, nbits(topo.mask(via(msg, prv, core, topo) or prv, core))))
+
+    send(("st", 1), T.rec0[:, 512:1024], ["s0"])
+
+    def places(t, h):
+        R, b, pm = T["rec%d" % t], 128 * (h == "b"), T["pm" + h]
+        L = R[:, 256 + b:384 + b]
+        MM(["I512", "I101", "I64", "I", "l%d" % t + h, "s%d" % t], ["#pm" + h],
+           grp(pm[:, 384:512], [(M("I512"), L), (M("I101"), L), (M("I64"), R[:, 512 + b:640 + b]), (M("I"), R[:, 768 + b:896 + b])]), 128)
+        ts(T["s32" + h][:], pm[:, 384:512], T.ac[:, 4 * t:4 * t + 1], None, OP.add, None, ["#pm" + h, "ac%d" % t], ["s32" + h], 128)
+        ts(T["r32" + h][:], T["s32" + h][:], 4095, None, OP.bitwise_and, None, ["s32" + h], ["r32" + h], 128)
+        tc(T["offs" + h][:], T["r32" + h][:], ["r32" + h], ["off" + h])
+
+    def gather(k, h):
+        w = 64 if k == 4 else 128
+        for s in range(128 // w):
+            c0 = 128 * (h == "b") + w * s
+            act(T.zz[:, 80 * c0 + k:80 * (c0 + w) - 4 + k:5], T.xt[:, 0:4096].indirect(T["offs" + h][:, w * s:w * s + w]), AF.Copy,
+                ["x", "off" + h], ["z%d%s%d" % (k, h, s)], 16 * w, 1.5)
+
+    def stream(t, h):
+        b = 128 * (h == "b")
+        R = T["rec%d" % t]
+        C, L = R[:, b:b + 128], R[:, 256 + b:384 + b]
+        cg, lg = "c%d" % t + h, "l%d" % t + h
+        X = lambda nm: T[nm + h]
+        pu, pm, pd = X("pu"), X("pm"), X("pd")
+        PU, PM, D0, D1 = "#pu" + h, "#pm" + h, "#pd0" + h, "#pd1" + h
+        g_ = lambda *n: [x + h for x in n]
+        win, wx = X("win"), X("wx")
+
+        for e in range(4):
+            MM(["T%d" % e, "DG0", "DG3", "kd", cg], [D0],
+               grp(pd[:, e:509 + e:4], [(M("T%d" % e), C)] + ([(M("DG%d" % e), T.kd[:])] if e in (0, 3) else [])), 128)
+        flex(X("t0")[:], pd[:, 0:512], AF.Copy, [D0], g_("t0"), 512, None)
+        ppv = X("pp")[:, 1:256:2]
+        pts = [X("pt")[:, 256 * j + 1:256 * j + 256:2] for j in range(3)] + [X("pt")[:, 768:896]]
+        for j in range(3):
+            cpy(X("pt")[:, 256 * j:256 * j + 255:2], L, [lg], ["lp%d%s" % (j + 1, h)])
+        ts(ppv, L, -1.0, co(12), OP.add, OP.mult, [lg, "co12"], g_("pp"))
+        for e in (1, 2, 3):
+            ts(X("h0")[:, e:512:4], ppv, float(e), None, OP.is_lt, None, g_("pp", "h0z"), ["+h0" + h])
+        scan(X("sc")[:, 0:512], X("h0")[:], X("t0")[:], OP.add, g_("h0", "t0"), g_("sc"), 512)
+
+        def c512(y, ys):
+            o, i = X("c5")[:], X("sc")[:, y:y + 127 * ys + 1:ys]
+            add([("s", cs(128), lambda: g.scalar.activation(o, i, AF.Identity, scale=16384.0, bias=55040.0)),
+                 ("v", cv(64, 1), lambda: g.vector.tensor_scalar(o, i, 16384.0, 55040.0, OP.mult, OP.add))], g_("sc"), g_("c5"))
+            return i
+
+        mv = c512(3, 4)
+        for n in (0, 1):
+            it = []
+            for hb in (0, 1):
+                r0 = b + 64 * n + 32 * hb
+                for e in range(16):
+                    it += grp(pd[:, 512 * hb + e:512 * hb + e + 497:16], [(M("L%d" % e), R[:, r0:r0 + 32]) if e < 15 else (M("I"), T.kd[:, 0:32])])
+            MM(["L%d" % e for e in range(15)] + ["I", "kd", cg], [D0, D1], it, 32)
+            for hb in (0, 1):
+                c0 = 1024 * n + 512 * hb
+                flex(X("dt")[:, c0:c0 + 512], pd[:, 512 * hb:512 * hb + 512], AF.Copy, [D1 if hb else D0], ["dt%d%s" % (2 * n + hb, h)], 512, None)
+        MM(["E0", "E1", "E2", "E3", "S4", cg], [D0, D1], [x for d in range(5) for x in grp(pd[:, 128 * d:128 * d + 128], [(M("E%d" % d if d < 4 else "S4"), C)])], 128)
+        for d in range(5):
+            flex(X("rd")[:, d:640:5], pd[:, 128 * d:128 * d + 128], AF.Copy, [D1 if d == 4 else D0], ["rd%d%s" % (d, h)], 128, None)
+        act(X("w3")[:], L, AF.Sigmoid, [lg], g_("w3"), scale=3.4657359027997265, bias=-41.58883083359672)
+
+        zb = 80 * b
+        for k in range(4):
+            kk = k + 1
+            gather(k, h)
+            U, U2 = pu[:, 0:128], pd[:, 0:128]
+            zt = ["wl", "z%d%s0" % (k, h)]
+            us = [(WM("wl", m), T.zz[:, zb + 5 * m + k:zb + 5 * m + k + 80 * 127 + 1:80]) for m in range(16)]
+            MM(zt, [PU], grp(U, us), 128)
+            tt(X("x32")[:], U, mv, OP.mult, [PU] + g_("sc"), g_("x32"))
+            tt(X("n32")[:], U, X("c5")[:], OP.add, [PU] + g_("c5"), g_("n32"))
+            MM(["I32", "I", "k107"] + zt + g_("sc"), [D0], grp(U2, [(M("I32"), mv), (M("I"), T.k107[:])] + us), 128)
+            ts(X("s32")[:], X("x32")[:], 3, 4095, OP.arith_shift_right, OP.bitwise_and, g_("x32"), g_("s32"), 128)
+            tt(X("r32")[:], X("s32")[:], U2, OP.add, [D0] + g_("s32"), g_("r32"))
+            ts(X("s32")[:], X("r32")[:], 4095, None, OP.bitwise_and, None, g_("r32"), g_("s32"), 128)
+            tc(X("offs")[:], X("s32")[:], g_("s32"), ["off" + h])
+            P = pts[k]
+            tp = "p%d%s" % (kk, h)
+            ts(X("nn")[:], X("n32")[:], 9, 3, OP.arith_shift_right, OP.bitwise_and, g_("n32"), g_("nn"), 128)
+            if k == 0:
+                tc(P, X("nn")[:], g_("nn"), [tp])
+            else:
+                tt(P, X("nn")[:], pm[:, 128:256], OP.add, [PM] + g_("nn"), [tp])
+            if k < 3:
+                MM(["I", tp], [PM], grp(pm[:, 128:256], [(M("I"), P)]), 128)
+                ts(X("msk")[:, 1:256:2], P, co(kk), None, OP.is_ge, None, [tp, "co%d" % kk] + g_("mskz"), g_("msk"))
+                scan(X("pp")[:], X("msk")[:], X("pt")[:, 256 * k:256 * kk], OP.add, [tp, "lp%d%s" % (kk, h)] + g_("msk", "mskz"), g_("pp"), 256)
+                hn = "h%d" % kk
+                hts = []
+                for q in range(kk + 1, {1: 9, 2: 13, 3: 17}[kk]):
+                    hts.append("%s%s_%d" % (hn, h, q))
+
+                    def mk(o, i, d):
+                        return [("v", cv(64, 1), lambda: g.vector.tensor_scalar(o, i, float(d), None, OP.is_lt)),
+                                ("s", cs(128), lambda: g.scalar.activation(o, i, AF.Sigmoid, scale=-200.0, bias=200.0 * d - 100.0))]
+                    add(mk(X(hn)[:, q - 1:2048:16], ppv, q - kk), g_("pp", hn), [hts[-1]])
+                scan(X("sc")[:], X(hn)[:], X("dt")[:], OP.add, hts + g_(hn) + ["dt%d%s" % (n, h) for n in range(4)], g_("sc"), 2048)
+                mv = c512(15, 16)
+        gather(4, h)
+        yield
+        for s in (0, 1):
+            o = zb + 5120 * s
+            scan(T.vs[:, o:o + 5120], T.mk5[:], T.zz[:, o:o + 5120], OP.max, ["mk5", "z4%s%d" % (h, s)] + ["z%d%s0" % (k, h) for k in range(4)], ["vs%d%s" % (s, h)], 5120)
+            it = []
+            for m in range(16):
+                it += grp(pd[:, 64 * m:64 * m + 64], [(M("I"), T.vs[:, o + 5 * m + 4:o + 5 * m + 4 + 80 * 63 + 1:80]), (M("mI"), T.ff[:, b + 64 * s:b + 64 * s + 64])])
+            MM(["I", "mI", "vs%d%s" % (s, h), "ff" + h], [D0, D1], it, 64)
+            act(X("gg")[:], pd[:], AF.Sign, [D0, D1], g_("gg"), 1024, bias=0.5)
+            MM(["cl"] + g_("gg"), [PM], grp(pm[:, 64 * s:64 * s + 64], [(WM("cl", m), X("gg")[:, 64 * m:64 * m + 64]) for m in range(16)]), 64)
+        cpy(T.vs[:, zb:zb + 10240:80], T.ff[:, b:b + 128], ["ff" + h, "vs0" + h, "vs1" + h], ["vs0" + h, "vs1" + h])
+        flex(X("fl")[:], pm[:, 0:128], AF.Sigmoid, [PM], g_("fl"), 128, (1.0, None, OP.is_ge), scale=200.0, bias=-100.0)
+        tt(X("fw")[:], X("fl")[:], X("w3")[:], OP.mult, g_("fl", "w3"), g_("fw"), 256)
+        MM(["BD32"] + g_("fw"), [PU], grp(pu[:, 0:128], [(M("BD32"), X("fw")[:])]), 128)
+        tt(X("cand")[:], X("fw")[:], pu[:, 0:128], OP.is_gt, [PU] + g_("fw"), g_("cand"))
+        MM(["LT"] + g_("cand"), [PU], grp(pu[:, 128:256], [(M("LT"), X("cand")[:])]), 128)
+        tt(win[:], X("cand")[:], pu[:, 128:256], OP.is_gt, [PU] + g_("cand"), g_("win"))
+        if h == "b" and t < 2:
+            MM(["ON", "wina", "winb"], [PM], grp(pm[:, 384:512], [(M("ON"), T.wina[:]), (M("ON"), T.winb[:])]), 128)
+            act(T.junk[:], pm[:, 384:512], AF.Copy, [PM], ["f64", "f32", "ac%d" % (t + 1)], accum_out=T.ac[:, 4 * t + 4:4 * t + 5])
+        MM(["mo"] + g_("win"), [PU], grp(pu[:, 0:8], [(WM("mo", a), win[:, a:128:16]) for a in range(16)]), 8)
+        tt(X("o32")[:], pu[:, 0:8], T.c80[:], OP.add, [PU, "c80"], g_("o32"))
+        ts(X("nk")[:], pu[:, 0:8], 1.0, 4096.0, OP.is_lt, OP.mult, [PU], g_("nk"))
+        tc(X("ofs")[:], X("o32")[:], g_("o32"), g_("ofs"), 64)
+        tc(X("vsel")[:], T.vs[:, zb:zb + 10240].indirect(X("ofs")[:]), ["vs0" + h, "vs1" + h] + g_("ofs"), g_("vsel"), 192)
+        MM(["wl"] + g_("vsel"), [PU], grp(pu[:, 8:16], [(WM("wl", a), X("vsel")[:, a:128:16]) for a in range(16)]), 8)
+        tt(X("nk")[:], X("nk")[:], T.c16[:, b // 16:b // 16 + 8], OP.add, ["c16"] + g_("nk"), g_("nk"))
+        tc(X("q32")[:], pu[:, 8:16], [PU], g_("q32"), 64)
+        ts(X("o32")[:], X("q32")[:], 6, 15, OP.arith_shift_right, OP.bitwise_and, g_("q32"), g_("o32"))
+        tt(X("q32")[:], X("o32")[:], X("nk")[:], OP.add, g_("o32", "nk"), g_("q32"))
+        tc(X("of2")[:], X("q32")[:], g_("q32"), g_("of2"), 64)
+        tc(T.xt[:].indirect(X("of2")[:]), X("vsel")[:], g_("of2", "vsel"), ["x"], 512)
+        MM(["I", "I16", lg, "p1" + h, "p2" + h, "p3" + h, "p4" + h] + g_("win"), [D0, D1],
+           [x for j in range(5) for x in grp(pd[:, 128 * j:128 * j + 128], [(M("I"), pts[j - 1] if j else L), (M("I16"), win[:])])], 128)
+        flex(wx[:], pd[:, 0:640], AF.Relu, [D0, D1], g_("wx"), 640, (-16.0, 0.0, OP.add, OP.max), bias=-16.0)
+        MM(["LE"] + g_("wx"), [PU], grp(pu[:, 128:256], [(M("LE"), wx[:, 0:128])]), 128)
+        for d in (1, 2, 3, 4):
+            flex(X("hn")[:, d:640:5], pu[:, 128:256], AF.Sigmoid, [PU, "hnz" + h], ["+hn" + h], 128, (float(d), None, OP.is_lt), scale=-200.0, bias=200.0 * d - 100.0)
+        scan(X("scn")[:], X("hn")[:], X("rd")[:], OP.add, g_("hn") + ["rd%d%s" % (d, h) for d in range(5)], g_("scn"), 640)
+        NRt = T["nr%d" % t]
+        flex(NRt[:, b:b + 128], X("scn")[:, 4:640:5], AF.Copy, g_("scn"), ["nc%d%s" % (t, h)], 64, None)
+        if t < 2:
+            send(("c" + h, t + 1), NRt[:, b:b + 128], ["nc%d%s" % (t, h)])
+        MM(["B1", "BX32"] + g_("wx", "win"), [D0], [x for j in (1, 2, 3, 4) for x in grp(pd[:, 128 * j - 128:128 * j],
+           [(M("B1"), wx[:, 128 * j:128 * j + 128])] + ([(M("BX32"), win[:])] if j == 4 else []))], 128)
+        ts(X("m4")[:], pd[:, 384:512], co(4), None, OP.is_equal, None, [D0, "co4"], g_("m4"), 128)
+        for j in (1, 2, 3):
+            act(X("ax")[:, 128 * j - 128:128 * j], pd[:, 128 * j - 128:128 * j], AF.Abs, [D0, "co%d" % (4 + j)], ["+ax" + h], bias=co(4 + j))
+        tc(X("z4")[:], T.zz[:, zb:zb + 10240].indirect(X("ofs")[:]), g_("ofs") + ["z4%s1" % h] + ["z%d%s0" % (k, h) for k in range(5)], g_("z4"), 192)
+        tt(X("t4")[:], X("m4")[:], X("scn")[:, 4:640:5], OP.mult, g_("m4", "scn"), g_("t4"), 256)
+        MM(["BW", "B512"] + g_("z4", "t4"), [PU], grp(pu[:, 0:128], [(M("BW"), X("z4")[:]), (M("B512"), X("t4")[:])]), 128)
+        tc(X("n4")[:], pu[:, 0:128], [PU], g_("n4"))
+        ts(X("n5")[:], X("n4")[:], 9, 3, OP.arith_shift_right, OP.bitwise_and, g_("n4"), g_("n5"), 128)
+        tt(X("n4m")[:], X("n5")[:], X("m4")[:], OP.mult, g_("n5", "m4"), g_("n4m"), 256)
+        it = []
+        for j in (1, 2, 3):
+            it += grp(pd[:, 384 + 128 * j:512 + 128 * j], [(M("B1"), wx[:, 128 * j + 128:128 * j + 256]), (M("mB1"), wx[:, 128 * j:128 * j + 128]), (M("mI4"), X("ax")[:, 128 * j - 128:128 * j])])
+        it += grp(pd[:, 896:1024], [(M("I"), L), (M("mB8"), win[:]), (M("I"), T.km1[:])])
+        MM(["B1", "mB1", "mI4", "mB8", "I", "km1", lg] + g_("wx", "ax", "win"), [D1], it, 128)
+        flex(X("ex")[:], pd[:, 512:1024], AF.Relu, [D1], g_("ex"), 512, (0.0, None, OP.max))
+        MM(["BQ0", "I"] + g_("wx", "ex", "n4m"), [PU],
+           grp(pu[:, 256:384], [(M("BQ0"), wx[:, 128:256])] + [(M("I"), X("ex")[:, 128 * j:128 * j + 128]) for j in range(4)] + [(M("I"), X("n4m")[:])]), 128)
+        flex(NRt[:, 256 + b:384 + b], pu[:, 256:384], AF.Identity, [PU], ["nl%d%s" % (t, h)], 128, (1.0, None, OP.add), bias=1.0)
+        if t < 2:
+            send(("l" + h, t + 1), NRt[:, 256 + b:384 + b], ["nl%d%s" % (t, h)])
+        MM(["I", "kmh", "ff" + h] + g_("vsel"), [PM], grp(pm[:, 384:512], [(M("I"), T.ff[:, b:b + 128]), (M("I"), X("vsel")[:]), (M("I"), T.kmh[:])]), 128)
+        act(X("f1")[:], pm[:, 384:512], AF.Identity, [PM], g_("f1"), scale=0.5, bias=12582912.0)
+        act(T.ff[:, b:b + 128], X("f1")[:], AF.Identity, g_("f1"), ["ff" + h], bias=-12582912.0)
+
+    for t in range(3):
+        for h in "ab":
+            places(t, h)
+        if t == 1:
+            send(("st", 2), T.rec1[:, 512:1024], ["s1"])
+        for part in [stream(t, h) for h in "ab"] * 2:
+            next(part, None)
+    for hb in (0, 1):
+        MM(["I", "x"], ["#pu" + "ab"[hb]], grp(T["pu" + "ab"[hb]][:, 0:128], [(M("I"), T.xt[:, 2048 * hb + a:2048 * hb + 2048:16]) for a in range(16)]), 128)
+        act(T.ysb[:, 128 * hb:128 * hb + 128], T["pu" + "ab"[hb]][:, 0:128], AF.Copy, ["#pu" + "ab"[hb]], ["ysb%d" % hb])
+    dma("y", "o_c", T.yc[:], T.nr2[:, 0:256], ["nc2a", "nc2b"], [])
+    dma("y", "o_l", T.yl[:], T.nr2[:, 256:512], ["nl2a", "nl2b"], [])
+    dma("y", "o_f", T.yf[:], T.ff[:], ["ffa", "ffb"], [])
+    dma("y", "o_s", T.ys[:], T.ysb[:], ["ysb0", "ysb1"], [])
+
+    Q = {"v": g.vector, "s": g.scalar, "t": g.tensor, "g": g, "y": g.sync}
+    cnt = {"v": 0, "s": 0, "t": 0, "g": 0}
+    known = {q: {} for q in Q}
+    lw, rd, bank = {}, {}, {}
+    if not KEEP:
+        KEEP.append(order([(n[0], n[1], n[2], n[3][0]) for n in nodes]))
+    for _, j, a in KEEP[0]:
+        (q, _, f), (_, r, w, kind) = nodes[j][0][a], nodes[j]
+        if kind[0] == "arr":
+            for t in w:
+                lw[t], rd[t] = [(kind[1], kind[2], {})], []
+            continue
+        own, evs = "e_" + q, []
+        for t in r + w:
+            if t[0] == "#":
+                evs += [e for e in bank.get(t, {}).values() if e[0] != own]
+            elif t[0] == "+":
+                evs += rd.get(t[1:], [])
+            else:
+                evs += lw.get(t, []) + (rd.get(t, []) if t in w else [])
+        best = {}
+        for sem, val, clk in evs:
+            if known[q].get(sem, 0) < val and (sem not in best or best[sem][0] < val):
+                best[sem] = (val, clk)
+        for sem, (val, clk) in best.items():
+            if not any(o != sem and best[o][1].get(sem, 0) >= val for o in best):
+                Q[q].wait_ge(T.sem[sem], val)
+        for sem, (val, clk) in best.items():
+            for k, x in list(clk.items()) + [(sem, val)]:
+                known[q][k] = max(known[q].get(k, 0), x)
+        if kind[0] == "send":
+            f()
+            ev = (sends[-1][0], sends[-1][1], dict(known[q]))
+        elif kind[0] == "dma":
+            f().then_inc(T.sem[kind[1]], 16)
+            ev = (kind[1], 16, dict(known[q]))
+        else:
+            cnt[q] += 1
+            f().then_inc(T.sem[own], 1)
+            ev = (own, cnt[q], dict(known[q]))
+            ev[2][own] = cnt[q]
+        for t in set(r + w):
+            if t[0] == "#":
+                bank.setdefault(t, {})[ev[0]] = ev
+            elif t[0] == "+":
+                lw.setdefault(t[1:], []).append(ev)
+            elif t in w:
+                lw[t], rd[t] = [ev], []
+            else:
+                rd[t] = [e for e in rd.get(t, []) if e[0] != ev[0]] + [ev]
+    for q in ("v", "s", "t", "g"):
+        g.wait_ge(T.sem["e_" + q], cnt[q])
+    for s in ("o_c", "o_l", "o_f", "o_s"):
+        g.wait_ge(T.sem[s], 16)
+    for s, n in sends:
+        g.wait_ge(T.sem[s], n)

@@ -1,39 +1,52 @@
+import numpy as np
 from concourse.mybir import AluOpType as OP, AxisListType, ActivationFunctionType as AF
 
-SLOTS = ["I", "B1", "ON", "LT", "LE", "S1", "S2", "S3", "S4", "E0", "E1", "E2", "E3", "I32", "I512", "I101", "I64", "mI",
-         "I16", "mB1", "mI4", "mB8", "BD32", "B512", "BX32", "BW", "BQ0", "T0", "T1", "T2", "T3", "DG0", "DG3"]
-SLOTS += ["L%d" % e for e in range(15)]
+CH = {"a": (0, 128), "b": (128, 128)}
+NW = {1: 4, 2: 6, 3: 7}
+FIRST = sorted({k + 2 * a for k in NW for a in range(NW[k])})
+DIAG = {"I": 1, "mI": -1, "I512": 512, "I101": 101, "I64": 64, "I32": 32, "mI4": -4, "mI128": -128, "mI256": -256, "Ih": 0.5}
+DIAG.update({"K%d" % a: (4 * a - 11) * 2048 for a in range(7)})
+BLOCK = {"mB1": -1, "mB8": -8, "BH": 0.5, "B8": 8, "BX32": 32, "BX2": 2, "BX3": 3}
+ROWS = {"CU": (-32768, 4, 2.0 ** -9), "CL": (2048, 56, 7 / 64), "CF": (-98304, -1024, -61)}
+SLOTS = ["B1", "ON", "LE", "S1", "S2", "S3", "S4", "BW", "BQ0", "BR0", "BR1"] + list(DIAG) + list(BLOCK) + list(ROWS)
+SLOTS += ["W%d" % e for e in FIRST] + ["LE%d" % d for d in (1, 2, 3, 4)]
 SLOT = {n: j for j, n in enumerate(SLOTS)}
-BUF = {"bfloat16": "xt_8192 zz_20480 vs_20480 mk5_5120 wl_2064 cl_2064 mo_2064 ff_256 wtb_16 onef_16 e16_16 tmpm_128 k107_128 km1_128 kmh_128 kd_128 junk_128",
-       "float32": "sd_16 jio_16 jt_16 co_24 b8f_8 c80_8 c16_16 ac_16 ysb_256", "int32": "sti_256 tmi_256 tmj_256"}
-BUFH = {"bfloat16": "h0_512 h1_2048 h2_2048 h3_2048 t0_512 dt_2048 sc_2048 rd_640 hn_640 scn_640 gg_1024 c5_128 pt_896 pp_256 "
-                    "msk_256 w3_128 fl_128 fw_128 cand_128 win_128 vsel_128 z4_128 wx_640 ax_384 ex_512 m4_128 t4_128 n4m_128",
-        "float32": "nk_8 f1_128", "int32": "s32_128 x32_128 r32_128 n32_128 nn_128 n4_128 n5_128 o32_8 q32_8", "uint16": "offs_128 ofs_8 of2_8"}
+BUF = {"bfloat16": "xt_8192 mk4_2048 wl_2064 cl_2064 ff_256 wtb_16 onef_16 e16_16 tmpm_128 km1_128 km6_128 kmh_128 kmx_128 q2_256 junk_128 c16_32",
+       "float32": "sd_16 jio_16 jt_16 co_24 b8f_8 bw8_8 bc8_8 ct_16 ac_16 ysb_256 q4_512 q5_640 q6_768 q7_896", "int32": "sti_256 tmi_256 tmj_256"}
+BUFH = {"bfloat16": "zz_4096 vs_4112 pt_448 pp_128 msk_128 y8_64 rr_64 ax0_64 sel_64 gg_1024 w3_64 fw_128 win_128 vsel_64 z4_64 wx_320 ax_192 ex_256 t4_64 n4m_64",
+        "float32": "f1_64 c8f_64 sc_448 sn_320", "int32": "s32_64 x32_64 r32_64 n32_64 nn_64 xi_64 c8_64 n4_64 n5_64 o32_4 q32_4", "uint16": "offs_64 ofs_4 of2_4"}
+SIZE = {s.split("_")[0]: int(s.split("_")[1]) for names in BUFH.values() for s in names.split()}
+LAG = {"a": 0, "b": 0.5}
+VG = ["0b0"]
+SW = 32
+BIAS, PASSES = 0.3, 12
+ARR, MMF, PEC, CYC, FV, SAME, CROSS = 4000, 3, 0.38, 0.87, 30, 90, 220
+NOISE, SCALES = 1000, [{}, {"n": 1.8}, {"v": 1.1, "s": 1.2}]
 
 
 def _bufs():
     out = {"mats": ("sbuf", [128, len(SLOTS) * 128], "bfloat16")}
-    for table, hs in ((BUF, ("",)), (BUFH, ("a", "b"))):
+    for table, k in ((BUF, 1), (BUFH, 4)):
         for dt, names in table.items():
             for s in names.split():
                 nm, n = s.split("_")
-                for h in hs:
-                    out[nm + h] = ("sbuf", [128, int(n)], dt)
+                out[nm] = ("sbuf", [128, int(n) * k], dt)
     for t in range(3):
         out["rec%d" % t] = ("sbuf", [128, 1024], "bfloat16")
         out["nr%d" % t] = ("sbuf", [128, 512], "bfloat16")
-    for h in "ab":
-        out["pu" + h] = out["pm" + h] = ("psum", [128, 512], "float32")
-        out["pd" + h] = ("psum", [128, 1024], "float32")
+    for h, (_, n) in CH.items():
+        out["pd" + h] = ("psum", [128, 16 * n], "float32")
     return out
 
 
 SCRATCH = _bufs()
-MSG = [("st", 1), ("st", 2)] + [(k + h, t) for t in (1, 2) for h in "ab" for k in "cl"]
-COLS = {"st": (512, 1024), "ca": (0, 128), "cb": (128, 256), "la": (256, 384), "lb": (384, 512)}
+MSG = [("s", 1), ("s", 2)] + [(k + h, t) for t in (1, 2) for h in CH for k in "cl"]
+COLS = {k + h: (2 * b + n * j, 2 * b + n * j + n) for h, (b, n) in CH.items() for j, k in enumerate("cl")}
+COLS["s"] = (512, 1024)
 SEMAPHORES = ["e_v", "e_s", "e_t", "e_g"] + ["ld_" + n for n in ("st", "sp", "wt", "x", "ch", "fl")] + ["o_c", "o_l", "o_f", "o_s"]
 SEMAPHORES += [p + "%s%d" % m for m in MSG for p in ("a_", "b_")]
 KEEP = []
+LN2 = 0.6931471805599453
 
 
 def nbits(m):
@@ -49,18 +62,18 @@ def relays(src, dst, topo):
 
 def via(msg, src, dst, topo):
     own = relays(src, dst, topo)
-    return own[(msg[0][-1] == "a") % len(own)] if own else None
+    return own[(msg[0][0] == "l") % len(own)] if own else None
 
 
 def cv(n, k):
-    return 55 + max(64, n * k) * 0.95
+    return FV + max(64, n * k) * CYC
 
 
 def cs(n, k=1):
-    return 65 + n * k * 0.95
+    return 65 + n * k * CYC
 
 
-def order(nodes):
+def order(nodes, after):
     n = len(nodes)
     pred, succ, lw, rd = [[] for _ in range(n)], [[] for _ in range(n)], {}, {}
     for j, (alts, r, w, _) in enumerate(nodes):
@@ -77,43 +90,72 @@ def order(nodes):
                 lw.setdefault(t[1:], []).append(j)
             else:
                 lw[t], rd[t] = [j], []
-        pred[j] = sorted(ps - {j})
+        pred[j] = ps - {j}
+    for p, j in after:
+        pred[j].add(p)
+    for j in range(n):
         for p in pred[j]:
             succ[p].append(j)
-    prio = [0.0] * n
-    for j in range(n - 1, -1, -1):
-        prio[j] = nodes[j][0][0][1] + 80 + max([prio[x] for x in succ[j]] + [0])
-    for j in range(n):
-        if any(t[-1] == "a" for t in nodes[j][2]):
-            prio[j] += 3000
-    left = [len(p) for p in pred]
-    ready = [j for j in range(n) if not left[j]]
-    free, end, qof, out = {}, [0.0] * n, [None] * n, []
-    while ready:
-        c = []
-        for j in ready:
+    prio, left = [0.0] * n, [len(x) for x in succ]
+    todo = [j for j in range(n) if not left[j]]
+    for j in todo:
+        prio[j] = nodes[j][0][0][1] + CROSS + max([prio[x] for x in succ[j]] + [0])
+        for p in pred[j]:
+            left[p] -= 1
+            if not left[p]:
+                todo.append(p)
+
+    def place(pred, succ, prio):
+        left = [len(p) for p in pred]
+        ready = [j for j in range(n) if not left[j]]
+        busy, start, end, alt = {}, [0.0] * n, [0.0] * n, [0] * n
+        while ready:
+            j = max(ready, key=lambda x: prio[x])
+            ready.remove(j)
             best = None
-            for a, alt in enumerate(nodes[j][0]):
-                q, cost = alt[0], alt[1]
-                s = free.get(q, 0.0) if q != "n" else 0.0
-                for p in pred[j]:
-                    s = max(s, end[p] + (20 if qof[p] == q else 80))
-                if best is None or s + cost < best[0]:
-                    best = (s + cost, s, a, q)
-            c.append((best, j))
-        e, j = min(c, key=lambda x: (x[0][1], -prio[x[1]]))
-        t0, q0 = e[1], e[3]
-        e, j = max([x for x in c if x[0][3] == q0 and x[0][1] <= t0 + 30], key=lambda x: (prio[x[1]], -x[1]))
-        fin, s, a, q = e
-        ready.remove(j)
-        end[j], qof[j] = fin, q
-        free[q] = s + 70 if nodes[j][3] == "dma" else fin
-        out.append((s, j, a))
-        for x in succ[j]:
-            left[x] -= 1
-            if not left[x]:
-                ready.append(x)
-    return out
+            for a, (q, cost) in enumerate(x[:2] for x in nodes[j][0]):
+                s = max([end[p] + (SAME if nodes[p][0][alt[p]][0] == q else CROSS) for p in pred[j]] + [0.0])
+                hold = {"dma": 70, "arr": 0}.get(nodes[j][3], cost)
+                iv = busy.setdefault(q, [])
+                lo, hi = 0, len(iv)
+                while lo < hi:
+                    mid = (lo + hi) // 2
+                    lo, hi = (mid + 1, hi) if iv[mid][1] <= s else (lo, mid)
+                while lo < len(iv) and iv[lo][0] < s + hold:
+                    s = max(s, iv[lo][1])
+                    lo += 1
+                e = s + cost + (BIAS * cost if q == "v" else 0)
+                if best is None or e < best[0]:
+                    best = (e, s, a, q, lo, hold, cost)
+            _, s, alt[j], q, lo, hold, cost = best
+            start[j], end[j] = s, s + cost
+            if hold:
+                busy[q].insert(lo, (s, s + hold))
+            for x in succ[j]:
+                left[x] -= 1
+                if not left[x]:
+                    ready.append(x)
+        return start, end, alt
+
+    def replay(seq, scale):
+        free, end, qof = {}, [0.0] * n, [None] * n
+        for _, j, a in seq:
+            q, cost = nodes[j][0][a][:2]
+            cost *= scale.get(q, 1.0)
+            s = max([end[p] + (SAME if qof[p] == q else CROSS) for p in pred[j]] + [free.get(q, 0.0)])
+            end[j], qof[j] = s + cost, q
+            free[q] = {"dma": s + 70, "arr": 0.0}.get(nodes[j][3], s + cost)
+        return max(end)
+
+    best, rng = None, np.random.default_rng(0)
+    for i in range(PASSES):
+        start, end, alt = place(pred, succ, prio)
+        seq = sorted((start[j], j, alt[j]) for j in range(n))
+        e = sum(replay(seq, x) for x in SCALES)
+        if best is None or e < best[0]:
+            best = (e, seq, end)
+        prio = place(succ, pred, [x + NOISE * float(y) for x, y in zip(best[2] if i % 4 == 3 else end, rng.random(n))])[1]
+    return best[1]
 
 
 def rank_program(g, core, T, topo):
@@ -149,145 +191,148 @@ def rank_program(g, core, T, topo):
         add([("v", cost, lambda: {"tt": g.vector.tensor_tensor, "ts": g.vector.tensor_scalar, "tc": g.vector.tensor_copy, "ms": g.vector.memset,
                                   "sc": g.vector.tensor_tensor_scan, "tr": g.vector.tensor_reduce}[meth](*a))], r, w)
 
-    def tt(out, a, b, op, r, w, c=128):
-        vop("tt", cv(c, 1), r, w, out, a, b, op)
+    def tt(out, a, b, op, r, w, k=1):
+        vop("tt", cv(out.shape[1], k), r, w, out, a, b, op)
 
-    def ts(out, a, s1, s2, o1, o2, r, w, c=64):
-        vop("ts", cv(c, 1), r, w, *((out, a, s1, s2, o1) if o2 is None else (out, a, s1, s2, o1, o2)))
+    def ts(out, a, s1, s2, o1, o2, r, w, k=1):
+        vop("ts", cv(out.shape[1], k), r, w, *((out, a, s1, s2, o1) if o2 is None else (out, a, s1, s2, o1, o2)))
 
-    def tc(out, a, r, w, c=128):
-        vop("tc", cv(c, 1), r, w, out, a)
+    def tc(out, a, r, w, k=1):
+        vop("tc", cv(out.shape[1], k), r, w, out, a)
 
-    def ms(ap, val, w, c=64):
-        vop("ms", cv(c, 1), [], w, ap, val)
+    def ms(ap, val, w, r=(), k=0.5):
+        vop("ms", cv(ap.shape[1], k), r, w, ap, val)
 
-    def scan(out, a, b, o1, r, w, n):
-        vop("sc", cv(n, 0.5), r, w, out, a, b, 0.0, OP.mult, o1)
+    def scan(out, a, b, o0, o1, r, w, k=1):
+        vop("sc", cv(out.shape[1], k), r, w, out, a, b, 0.0, o0, o1)
 
-    def act(out, in_, func, r, w, n=128, k=1, **kw):
-        add([("s", cs(n, k), lambda: g.scalar.activation(out, in_, func, **kw))], r, w)
+    def act(out, in_, func, r, w, k=1, **kw):
+        add([("s", cs(out.shape[1], k), lambda: g.scalar.activation(out, in_, func, **kw))], r, w)
 
-    def flex(out, in_, func, r, w, n, v, **kw):
-        add([("s", cs(n), lambda: g.scalar.activation(out, in_, func, **kw)),
-             ("v", cv(n, 1), lambda: g.vector.tensor_scalar(out, in_, *v) if v else g.vector.tensor_copy(out, in_))], r, w)
+    def flex(out, in_, func, r, w, v, k=1, kv=1, **kw):
+        add([("s", cs(out.shape[1], k), lambda: g.scalar.activation(out, in_, func, **kw)),
+             ("v", cv(out.shape[1], k * kv), lambda: g.vector.tensor_scalar(out, in_, *v) if v else g.vector.tensor_copy(out, in_))], r, w)
+
+    def lin(out, in_, f, o, r, w, kv=1):
+        flex(out, in_, AF.Identity, r, w, (f, o, OP.mult, OP.add), 1, kv, scale=f, bias=o)
 
     def gp(meth, r, w, *a, **kw):
-        add([("g", 350, lambda: {"iota": g.iota, "sel": g.affine_select}[meth](*a, **kw))], r, w)
+        add([("g", 400, lambda: {"iota": g.iota, "sel": g.affine_select}[meth](*a, **kw))], r, w)
 
-    def fill(nm, n, v, tag):
-        add([("g", 150 + n * 1.9, lambda: g.iota(T[nm][:], [[0, n]], v, 0, allow_small_or_imprecise_dtypes=True))], [], [tag])
+    def fill(nm, pat, v, n):
+        add([("g", 150 + n * 1.75, lambda: g.iota(T[nm][:], pat, v, 0, allow_small_or_imprecise_dtypes=True))], [], [nm + "0"])
 
     def cpy(out, in_, r, w):
-        add([("g", 420, lambda: g.affine_select(out, in_, [[0, 128]], OP.is_ge, 0.0, 1, 0))], r, w)
+        add([("g", 180 + 1.75 * out.shape[1], lambda: g.affine_select(out, in_, [[0, out.shape[1]]], OP.is_ge, 0.0, 1, 0))], r, w)
 
-    def MM(r, w, items, ns):
+    def MM(r, w, items):
         def f():
             for o, l, x, s0, s1 in items:
                 i = g.tensor.matmul(o, l, x, s0, s1)
             return i
-        add([("t", 60 + 0.45 * max(64, ns) * len(items), f)], r, w)
-
-    def grp(out, pairs):
-        return [(out, l, x, j == 0, j == len(pairs) - 1) for j, (l, x) in enumerate(pairs)]
+        add([("t", 10 + sum(MMF + PEC * max(64, x[0].shape[1]) for x in items), f)], r, w)
 
     def M(n):
         return T.mats[:, SLOT[n] * 128:SLOT[n] * 128 + 128]
 
+    def grp(out, pairs):
+        return [(out, M(l) if isinstance(l, str) else l, x, j == 0, j == len(pairs) - 1) for j, (l, x) in enumerate(pairs)]
+
+    def mm(r, w, *groups):
+        it = [x for o, pairs in groups for x in grp(o, pairs)]
+        MM(list(r) + sorted({l for _, pairs in groups for l, _ in pairs if isinstance(l, str)}), w, it)
+
     def WM(n, m):
         return T[n][:, 128 * m:128 * m + 128]
+
+    def ones(n):
+        return T.mats[:, SLOT["ON"] * 128:SLOT["ON"] * 128 + n]
 
     def dma(q, sem, out, in_, r, w, cost=2600):
         add([(q, cost, lambda: {"y": g.sync, "s": g.scalar}[q].dma_start(out, in_))], r, w, ("dma", sem, 16))
 
+    TAB = T.xt[:, 4096:8192]
     dma("s", "ld_st", T.sti[:], T.st[:], [], ["sti"])
-    dma("s", "ld_sp", T.rec0[:, 256:512], T.sp[:], [], ["l0a", "l0b"])
+    dma("s", "ld_sp", T.rec0[:, 256:512], T.sp[:], [], ["l0" + h for h in CH])
     dma("s", "ld_wt", T.wtb[:, 0:1], T.wt[:], [], ["wtb"])
-    dma("y", "ld_x", T.xt[:, 0:4096], T.x[:], [], ["x"], 8000)
-    dma("s", "ld_ch", T.rec0[:, 0:256], T.ch[:], [], ["c0a", "c0b"])
-    dma("s", "ld_fl", T.ff[:], T.fl[:], [], ["ffa", "ffb"])
-    ms(M("ON"), 1.0, ["ON"]); ms(T.onef[:], 1.0, ["onef"]); ms(T.wl[:], 0.0, ["wl0"], 1032)
-    for nm in ("h1a", "h1b", "h2a", "h2b"):
-        fill(nm, 2048, 1, nm)
-    fill("mk5", 5120, 1, "mk5"); fill("cl", 2064, 0, "cl0"); fill("mo", 2064, 0, "mo0")
-    for nm, st in (("jio", [[1, 16]]), ("c80", [[1280, 8]]), ("c16", [[256, 16]])):
-        gp("iota", [], [nm], T[nm][:], st, 0, 0, allow_small_or_imprecise_dtypes=True)
+    dma("y", "ld_x", TAB, T.x[:], [], ["x"], 8000)
+    dma("s", "ld_ch", T.rec0[:, 0:256], T.ch[:], [], ["c0" + h for h in CH])
+    dma("s", "ld_fl", T.ff[:], T.fl[:], [], ["ff" + h for h in CH])
+    ms(M("ON"), 1.0, ["ON"]); ms(T.onef[:], 1.0, ["onef"]); ms(T.wl[:], 0.0, ["wl0"]); ms(T.cl[:], 0.0, ["cl0"])
+    fill("mk4", [[0, 512], [256, 4]], 0, 2048)
+    for k in (4, 6, 7):
+        fill("q%d" % k, [[0, 128], [16384, k]], -26 * 2048, 128 * k)
+        ms(T["q%d" % k][:, 0:128 * k:k], -1e9, ["+q%d" % k], ["q%d0" % k], 1)
+        ms(T["q%d" % k][:, k - 1:128 * k:k], 2048.0 * (8 * k - 34) + sum(ROWS["CL"]), ["+q%d" % k], ["q%d0" % k], 1)
+    fill("q5", [[0, 128], [512, 5]], -2304, 640)
+    ms(T.q5[:, 0:640:5], -1e9, ["q5"], ["q50"], 1)
+    ms(T.q2[:, 0:256:2], 1048576.0, ["+q2"]); ms(T.q2[:, 1:256:2], 0.0, ["+q2"])
+    for nm, o, st in (("jio", T.jio[:], [[1, 16]]), ("ct", T.ct[:], [[256, 16]])):
+        gp("iota", [], [nm], o, st, 0, 0, allow_small_or_imprecise_dtypes=True)
     gp("sel", ["ON"], ["I"], M("I"), M("ON"), [[-1, 128]], OP.is_equal, 0.0, 0, 1)
     gp("sel", ["ON"], ["tmpm"], T.tmpm[:], M("ON"), [[-16, 8], [0, 16]], OP.is_ge, 0.0, 0, 1)
     gp("sel", ["tmpm"], ["B1"], M("B1"), T.tmpm[:], [[16, 8], [0, 16]], OP.is_ge, 0.0, 15, -1)
-    gp("sel", ["B1"], ["LT"], M("LT"), M("B1"), [[1, 128]], OP.is_gt, 0.0, 0, -1)
     gp("sel", ["B1"], ["LE"], M("LE"), M("B1"), [[1, 128]], OP.is_ge, 0.0, 0, -1)
     for d in (1, 2, 3, 4):
         gp("sel", ["B1"], ["S%d" % d], M("S%d" % d), M("B1"), [[-1, 128]], OP.is_equal, 0.0, -d, 1)
-    ts(T.tmi[:], T.sti[:], 6, None, OP.arith_shift_right, None, ["sti"], ["tmi"], 256)
-    ts(T.tmj[:], T.sti[:], 63, None, OP.bitwise_and, None, ["sti"], ["tmj"], 256)
-    tc(T.rec0[:, 512:768], T.tmi[:], ["tmi"], ["+s0"], 256)
-    tc(T.rec0[:, 768:1024], T.tmj[:], ["tmj"], ["+s0"], 256)
-    tt(T.junk[:, 0:64], T.mats[:, 0:64], T.mats[:, 64:128], OP.add, ["I"], ["f64"])
+    ts(T.tmi[:], T.sti[:], 6, None, OP.arith_shift_right, None, ["sti"], ["tmi"])
+    ts(T.tmj[:], T.sti[:], 63, None, OP.bitwise_and, None, ["sti"], ["tmj"])
+    tc(T.rec0[:, 512:768], T.tmi[:], ["tmi"], ["+s0"])
+    tc(T.rec0[:, 768:1024], T.tmj[:], ["tmj"], ["+s0"])
+    tt(T.junk[:, 0:64], T.mats[:, SLOT["I"] * 128:SLOT["I"] * 128 + 64], T.mats[:, SLOT["I"] * 128 + 64:SLOT["I"] * 128 + 128], OP.add, ["I"], ["f64"], 2)
     tt(T.junk[:, 64:96], T.junk[:, 0:32], T.junk[:, 32:64], OP.add, ["f64"], ["f32"])
     tt(T.e16[:], T.junk[:, 64:80], T.junk[:, 80:96], OP.add, ["f32"], ["e16"])
     tt(T.jt[:], T.e16[:], T.jio[:], OP.mult, ["e16", "jio"], ["jt"])
     co = lambda j: T.co[:, j:j + 1]
     vop("tr", 120, ["jt"], ["co0"], co(0), T.jt[:], AxisListType.X, OP.add)
-    for k in (1, 2, 3):
-        ts(co(k), co(0), float(-k), None, OP.add, None, ["co0"], ["co%d" % k])
-        ts(co(4 + k), co(0), -1.0, float(k), OP.mult, OP.add, ["co0"], ["co%d" % (4 + k)])
-    ts(co(4), co(0), 28.0, None, OP.add, None, ["co0"], ["co4"])
-    ts(co(8), co(0), 5.0, 4.0, OP.mult, OP.add, ["co0"], ["co8"])
-    ts(co(9), T.wtb[:, 0:1], 64.0, None, OP.mult, None, ["wtb"], ["co9"])
-    ts(co(10), co(0), 80.0, None, OP.mult, None, ["co0"], ["co10"])
-    ts(co(11), co(0), 16.0, None, OP.mult, None, ["co0"], ["co11"])
-    ts(co(12), T.e16[:, 0:1], 1.0, None, OP.mult, None, ["e16"], ["co12"])
-    ts(co(14), T.e16[:, 4:5], 0.03125, None, OP.mult, None, ["e16"], ["co14"])
-    ts(co(13), T.e16[:, 0:1], -1.0, 1.0, OP.mult, OP.add, ["e16"], ["co13"])
-    ts(T.c80[:], T.c80[:], co(10), None, OP.add, None, ["co10", "c80"], ["c80"])
-    ts(T.c16[:], T.c16[:], co(11), None, OP.add, None, ["co11", "c16"], ["c16"])
+    for j, f, o in ((1, 1, -7), (2, 1, -8), (3, 1, -9), (4, 1, 28), (5, -1, 0), (8, 4 / 4096, 3 / 4096), (10, -LN2, -80 * LN2), (11, 16, 0)):
+        ts(co(j), co(0), float(f), float(o), OP.mult, OP.add, ["co0"], ["co%d" % j])
+    tc(co(9), T.wtb[:, 0:1], ["wtb"], ["co9"])
+    tc(co(12), T.e16[:, 0:1], ["e16"], ["co12"])
+    for b, n in CH.values():
+        ts(T.c16[:, b // 8:b // 8 + n // 16], T.ct[:, b // 16:(b + n) // 16], co(11), None, OP.add, None, ["co11", "ct"], ["+c16"])
+        ts(T.c16[:, b // 8 + n // 16:(b + n) // 8], T.ct[:, 0:n // 16], co(11), 4.0, OP.add, OP.mult, ["co11", "ct"], ["+c16"])
     b8 = SLOT["B1"] * 128
     tc(T.b8f[:], T.mats[:, b8:b8 + 113:16], ["B1"], ["b8f"])
-    for gi in range(8):
-        colb = T.b8f[:, gi:gi + 1]
-        sl = slice(16 * gi, 16 * gi + 129 * 15 + 1, 129)
-        ts(T.wl[:, sl], T.onef[:], co(9), colb, OP.mult, OP.mult, ["onef", "co9", "b8f", "wl0"], ["+wl"])
-        ts(T.cl[:, sl], T.onef[:], colb, None, OP.mult, None, ["onef", "b8f", "cl0"], ["+cl"])
-        ts(T.mo[:, sl], T.onef[:], co(8), colb, OP.mult, OP.mult, ["onef", "co8", "b8f", "mo0"], ["+mo"])
-    tt(T.jt[:, 1:15], T.e16[:, 1:15], T.e16[:, 2:16], OP.subtract, ["e16", "co0"], ["+jd"])
-    tc(T.jt[:, 15:16], T.e16[:, 15:16], ["e16", "co0"], ["+jd"])
-    tc(T.jt[:, 0:1], T.e16[:, 0:1], ["e16", "co0"], ["+jd"])
-    ts(T.sd[:], T.jt[:], 0.03125, None, OP.mult, None, ["jd"], ["sd"])
+    for nm, src, f, r2 in (("wl", "bw8", co(9), "co9"), ("cl", "bc8", 4096.0, "b8f")):
+        ts(T[src][:], T.b8f[:], f, None, OP.mult, None, ["b8f", r2], [src])
+        for gi in range(8):
+            col = T[src][:, gi:gi + 1]
+            flex(T[nm][:, 16 * gi:16 * gi + 129 * 15 + 1:129], T.onef[:], AF.Copy, ["onef", src, nm + "0"], ["+" + nm], (col, None, OP.mult), scale=col)
+    ts(T.jt[:, 0:15], T.e16[:, 1:16], 512.0, None, OP.mult, None, ["e16", "co0"], ["jd"])
+    ms(T.jt[:, 15:16], 0.0, ["jd"])
+    tt(T.jio[:], T.jt[:], T.e16[:], OP.add, ["jd", "e16", "co0"], ["je"])
+    ts(T.sd[:], T.jio[:], 0.03125, None, OP.mult, None, ["je"], ["sd"])
 
     def mat(dst, src, f, r2=()):
-        add([("v", cv(64, 1), lambda: g.vector.tensor_scalar(M(dst), M(src), f, None, OP.mult)),
-             ("s", cs(128), lambda: g.scalar.activation(M(dst), M(src), AF.Copy, scale=f))], [src] + list(r2), [dst])
+        flex(M(dst), M(src), AF.Copy, [src] + list(r2), [dst], (f, None, OP.mult), 1, 0.5, scale=f)
 
-    for nm, f in (("I512", 512.0), ("I101", 101.0), ("I64", 64.0), ("I32", 32.0), ("mI", -1.0), ("I16", 16.0), ("mI4", -4.0)):
-        mat(nm, "I", f)
-    mat("T0", "B1", T.sd[:, 0:1], ["sd"])
-    for e in range(4):
-        nm = "T%d" % e
-        if e:
-            ms(M(nm), 0.0, [nm])
-        o = SLOT[nm] * 128
-        ts(T.mats[:, o:o + 113:16], T.mats[:, b8:b8 + 113:16], T.sd[:, e + 1:e + 2] if e < 3 else co(14), None, OP.mult, None, ["B1", "sd", "co14"], [nm])
-    mat("DG0", "I", co(13), ["co13"]); mat("DG3", "I", co(12), ["co12"])
-    for nm, v in (("kd", -215.0 / 64), ("k107", 107.5), ("km1", -1.0), ("kmh", -0.5)):
-        ms(T[nm][:], v, [nm])
-    for e in range(15):
-        mat("L%d" % e, "B1", T.sd[:, e + 1:e + 2], ["sd"])
-    for nm, f in (("mB1", -1.0), ("mB8", -8.0), ("BD32", 0.03125), ("B512", 512.0), ("BX32", 32.0)):
-        mat(nm, "B1", f)
+    for nm, f in DIAG.items():
+        if nm != "I":
+            mat(nm, "I", float(f))
+    for nm, f in BLOCK.items():
+        mat(nm, "B1", float(f))
+    for d in (1, 2, 3, 4):
+        mat("LE%d" % d, "LE", 512.0 * d)
+    for e in FIRST:
+        mat("W%d" % e, "B1", T.sd[:, e:e + 1], ["sd"])
     mat("BW", "B1", co(9), ["co9"])
-    for d in range(4):
-        s0 = "S%d" % d if d else "I"
-        tt(M("E%d" % d), M(s0), M("S%d" % (d + 1)), OP.subtract, [s0, "S%d" % (d + 1)], ["E%d" % d], 256)
+    mat("BR0", "B1", co(12), ["co12"]); mat("BR1", "B1", co(12), ["co12"])
+    o = SLOT["BR1"] * 128
+    ms(T.mats[:, o:o + 113:16], 0.0, ["BR1"])
     ms(M("BQ0"), 0.0, ["BQ0"])
     o = SLOT["BQ0"] * 128
     tc(T.mats[:, o:o + 113:16], T.mats[:, b8:b8 + 113:16], ["B1"], ["BQ0"])
-    ms(T.mk5[:, 0:5120:5], 0.0, ["mk5"], 1024)
+    for nm, vals in ROWS.items():
+        ms(M(nm), 0.0, [nm + "0"])
+        for j, v in enumerate(vals):
+            ms(T.mats[32 * j:32 * j + 1, SLOT[nm] * 128:SLOT[nm] * 128 + 128], float(v), ["+" + nm], [nm + "0"])
+    for nm, v in (("km1", -1.0), ("km6", -6.0), ("kmh", -0.5), ("kmx", -4096.0)):
+        ms(T[nm][:], v, [nm])
     ms(T.ac[:, 0:1], 0.0, ["ac0"])
-    for h in "ab":
-        ms(T["msk" + h][:], 0.0, ["mskz" + h], 128); ms(T["h0" + h][:], 0.0, ["h0z" + h], 256); ms(T["hn" + h][:], 0.0, ["hnz" + h], 320)
-        for k in (1, 2, 3):
-            for e in range(k):
-                ms(T["h%d%s" % (k, h)][:, e:2048:16], 0.0, ["h%d%s" % (k, h)])
+    ms(T.msk[:], 0.0, ["mskz"])
+    for b, n in CH.values():
+        ms(T.vs[:, SIZE["vs"] * b // 64 + 64 * n + 14:SIZE["vs"] * b // 64 + 64 * n + 15], 0.0, ["+vz"])
 
     sends = []
 
@@ -295,193 +340,196 @@ def rank_program(g, core, T, topo):
         def f():
             sends.append(("b_%s%d" % msg, put(msg, ap, via(msg, core, nxt, topo) or nxt)))
         add([("g", 1500, f)], tags, ["sent%s%d" % msg], ("send",))
-        tag = {"st": "s%d", "ca": "c%da", "cb": "c%db", "la": "l%da", "lb": "l%db"}[msg[0]] % msg[1]
-        add([("n", 3500, None)], ["sent%s%d" % msg], [tag], ("arr", "a_%s%d" % msg, nbits(topo.mask(via(msg, prv, core, topo) or prv, core))))
+        add([("n", ARR, None)], ["sent%s%d" % msg], ["%s%d%s" % (msg[0][0], msg[1], msg[0][1:])],
+            ("arr", "a_%s%d" % msg, nbits(topo.mask(via(msg, prv, core, topo) or prv, core))))
 
-    send(("st", 1), T.rec0[:, 512:1024], ["s0"])
-
-    def places(t, h):
-        R, b, pm = T["rec%d" % t], 128 * (h == "b"), T["pm" + h]
-        L = R[:, 256 + b:384 + b]
-        MM(["I512", "I101", "I64", "I", "l%d" % t + h, "s%d" % t], ["#pm" + h],
-           grp(pm[:, 384:512], [(M("I512"), L), (M("I101"), L), (M("I64"), R[:, 512 + b:640 + b]), (M("I"), R[:, 768 + b:896 + b])]), 128)
-        ts(T["s32" + h][:], pm[:, 384:512], T.ac[:, 4 * t:4 * t + 1], None, OP.add, None, ["#pm" + h, "ac%d" % t], ["s32" + h], 128)
-        ts(T["r32" + h][:], T["s32" + h][:], 4095, None, OP.bitwise_and, None, ["s32" + h], ["r32" + h], 128)
-        tc(T["offs" + h][:], T["r32" + h][:], ["r32" + h], ["off" + h])
-
-    def gather(k, h):
-        w = 64 if k == 4 else 128
-        for s in range(128 // w):
-            c0 = 128 * (h == "b") + w * s
-            act(T.zz[:, 80 * c0 + k:80 * (c0 + w) - 4 + k:5], T.xt[:, 0:4096].indirect(T["offs" + h][:, w * s:w * s + w]), AF.Copy,
-                ["x", "off" + h], ["z%d%s%d" % (k, h, s)], 16 * w, 1.5)
+    send(("s", 1), T.rec0[:, 512:1024], ["s0"])
+    gat = {}
 
     def stream(t, h):
-        b = 128 * (h == "b")
-        R = T["rec%d" % t]
-        C, L = R[:, b:b + 128], R[:, 256 + b:384 + b]
+        b, n = CH[h]
+        parts = range(n // 64)
+        R, NR, pd = T["rec%d" % t], T["nr%d" % t], T["pd" + h]
+        C, L = (R[:, 2 * b:2 * b + n], R[:, 2 * b + n:2 * b + 2 * n]) if t else (R[:, b:b + n], R[:, 256 + b:256 + b + n])
+        Cp = lambda s: R[:, (2 * b if t else b) + 64 * s:(2 * b if t else b) + 64 * s + 64]
+        NC, NL = (NR[:, 2 * b:2 * b + n], NR[:, 2 * b + n:2 * b + 2 * n]) if t < 2 else (NR[:, b:b + n], NR[:, 256 + b:256 + b + n])
+        F = T.ff[:, b:b + n]
         cg, lg = "c%d" % t + h, "l%d" % t + h
-        X = lambda nm: T[nm + h]
-        pu, pm, pd = X("pu"), X("pm"), X("pd")
-        PU, PM, D0, D1 = "#pu" + h, "#pm" + h, "#pd0" + h, "#pd1" + h
-        g_ = lambda *n: [x + h for x in n]
-        win, wx = X("win"), X("wx")
+        g_ = lambda *x: [y + h for y in x]
+        zt = lambda k: g_(*["z%d%d" % (k, s) for s in parts])
 
-        for e in range(4):
-            MM(["T%d" % e, "DG0", "DG3", "kd", cg], [D0],
-               grp(pd[:, e:509 + e:4], [(M("T%d" % e), C)] + ([(M("DG%d" % e), T.kd[:])] if e in (0, 3) else [])), 128)
-        flex(X("t0")[:], pd[:, 0:512], AF.Copy, [D0], g_("t0"), 512, None)
-        ppv = X("pp")[:, 1:256:2]
-        pts = [X("pt")[:, 256 * j + 1:256 * j + 256:2] for j in range(3)] + [X("pt")[:, 768:896]]
+        def X(nm, lo=0, hi=None, step=1):
+            o = SIZE[nm] * b // 64
+            return T[nm][:, o + lo:o + (SIZE[nm] * n // 64 if hi is None else hi):step]
+
+        P_ = lambda j, c=1: pd[:, n * j:n * (j + c)]
+        B_ = lambda j, c=1: ["#%s%d" % (h, x) for x in range(n * j // 512, (n * (j + c) + 511) // 512)]
+
+        def table(j, w):
+            o = n * j + (512 - 64 * w) * (n // 128)
+            return pd[:, o:o + n * w], lambda a, s: pd[:, o + 64 * w * s + a:o + 64 * w * (s + 1):w]
+
+        wx = lambda j, c=1: X("wx", n * j, n * (j + c))
+        win, y8, ppv = X("win", 0, n), X("y8"), X("pp", 1, 2 * n, 2)
+
+        def gather(k, s):
+            o = X("zz", 4096 * s + k, 4096 * s + 4096, 4) if k < 4 else X("vs", 4096 * s + 19, 4096 * s + 4112, 4)
+            i, w = TAB.indirect(X("offs", 64 * s, 64 * s + 64)), g_("z%d%d" % (k, s))
+            gat[t, k, h, s] = len(nodes)
+            if "%d%s%d" % (k, h, s) in VG:
+                tc(o, i, ["x", "off" + h], w, 1.5)
+            else:
+                act(o, i, AF.Copy, ["x", "off" + h], w, 1.5)
+
+        mm([lg, "s%d" % t], B_(7), (P_(7), [("I512", L), ("I101", L), ("I64", R[:, 512 + b:512 + b + n]), ("I", R[:, 768 + b:768 + b + n])]))
+        ts(X("s32"), P_(7), T.ac[:, 4 * t:4 * t + 1], None, OP.add, None, B_(7) + ["ac%d" % t], g_("s32"))
+        ts(X("r32"), X("s32"), 4095, None, OP.bitwise_and, None, g_("s32"), g_("r32"))
+        tc(X("offs"), X("r32"), g_("r32"), g_("off"))
+        mm([lg], B_(8), (P_(8), [("BR0", L)]))
+        flex(X("ax0"), P_(8), AF.Abs, B_(8) + ["co0", "co5"], g_("ax0"), (co(0), None, OP.not_equal), bias=co(5))
+        mm([cg] + g_("ax0"), B_(9), (P_(9), [("I", C), ("mI128", X("ax0"))]))
+        flex(X("sel"), P_(9), AF.Relu, B_(9), g_("sel"), (0.0, None, OP.max))
+        mm([cg] + g_("sel"), B_(10), (P_(10), [("BR1", C), ("BQ0", X("sel"))]))
+        lin(y8, P_(10), 0.25, 0.125, B_(10), g_("y8"))
+        lin(X("c8f"), P_(10), 8.0, 28.0, B_(10), g_("c8"))
+        pts = [X("pt", 2 * n * j + 1, 2 * n * (j + 1), 2) for j in range(3)] + [X("pt", 6 * n, 7 * n)]
         for j in range(3):
-            cpy(X("pt")[:, 256 * j:256 * j + 255:2], L, [lg], ["lp%d%s" % (j + 1, h)])
-        ts(ppv, L, -1.0, co(12), OP.add, OP.mult, [lg, "co12"], g_("pp"))
-        for e in (1, 2, 3):
-            ts(X("h0")[:, e:512:4], ppv, float(e), None, OP.is_lt, None, g_("pp", "h0z"), ["+h0" + h])
-        scan(X("sc")[:, 0:512], X("h0")[:], X("t0")[:], OP.add, g_("h0", "t0"), g_("sc"), 512)
+            cpy(X("pt", 2 * n * j, 2 * n * (j + 1) - 1, 2), L, [lg], g_("lp%d" % (j + 1)))
+        act(X("w3"), L, AF.Sigmoid, [lg, "co10"], g_("w3"), scale=16 * LN2, bias=co(10))
 
-        def c512(y, ys):
-            o, i = X("c5")[:], X("sc")[:, y:y + 127 * ys + 1:ys]
-            add([("s", cs(128), lambda: g.scalar.activation(o, i, AF.Identity, scale=16384.0, bias=55040.0)),
-                 ("v", cv(64, 1), lambda: g.vector.tensor_scalar(o, i, 16384.0, 55040.0, OP.mult, OP.add))], g_("sc"), g_("c5"))
-            return i
-
-        mv = c512(3, 4)
-        for n in (0, 1):
-            it = []
-            for hb in (0, 1):
-                r0 = b + 64 * n + 32 * hb
-                for e in range(16):
-                    it += grp(pd[:, 512 * hb + e:512 * hb + e + 497:16], [(M("L%d" % e), R[:, r0:r0 + 32]) if e < 15 else (M("I"), T.kd[:, 0:32])])
-            MM(["L%d" % e for e in range(15)] + ["I", "kd", cg], [D0, D1], it, 32)
-            for hb in (0, 1):
-                c0 = 1024 * n + 512 * hb
-                flex(X("dt")[:, c0:c0 + 512], pd[:, 512 * hb:512 * hb + 512], AF.Copy, [D1 if hb else D0], ["dt%d%s" % (2 * n + hb, h)], 512, None)
-        MM(["E0", "E1", "E2", "E3", "S4", cg], [D0, D1], [x for d in range(5) for x in grp(pd[:, 128 * d:128 * d + 128], [(M("E%d" % d if d < 4 else "S4"), C)])], 128)
-        for d in range(5):
-            flex(X("rd")[:, d:640:5], pd[:, 128 * d:128 * d + 128], AF.Copy, [D1 if d == 4 else D0], ["rd%d%s" % (d, h)], 128, None)
-        act(X("w3")[:], L, AF.Sigmoid, [lg], g_("w3"), scale=3.4657359027997265, bias=-41.58883083359672)
-
-        zb = 80 * b
         for k in range(4):
             kk = k + 1
-            gather(k, h)
-            U, U2 = pu[:, 0:128], pd[:, 0:128]
-            zt = ["wl", "z%d%s0" % (k, h)]
-            us = [(WM("wl", m), T.zz[:, zb + 5 * m + k:zb + 5 * m + k + 80 * 127 + 1:80]) for m in range(16)]
-            MM(zt, [PU], grp(U, us), 128)
-            tt(X("x32")[:], U, mv, OP.mult, [PU] + g_("sc"), g_("x32"))
-            tt(X("n32")[:], U, X("c5")[:], OP.add, [PU] + g_("c5"), g_("n32"))
-            MM(["I32", "I", "k107"] + zt + g_("sc"), [D0], grp(U2, [(M("I32"), mv), (M("I"), T.k107[:])] + us), 128)
-            ts(X("s32")[:], X("x32")[:], 3, 4095, OP.arith_shift_right, OP.bitwise_and, g_("x32"), g_("s32"), 128)
-            tt(X("r32")[:], X("s32")[:], U2, OP.add, [D0] + g_("s32"), g_("r32"))
-            ts(X("s32")[:], X("r32")[:], 4095, None, OP.bitwise_and, None, g_("r32"), g_("s32"), 128)
-            tc(X("offs")[:], X("s32")[:], g_("s32"), ["off" + h])
-            P = pts[k]
-            tp = "p%d%s" % (kk, h)
-            ts(X("nn")[:], X("n32")[:], 9, 3, OP.arith_shift_right, OP.bitwise_and, g_("n32"), g_("nn"), 128)
-            if k == 0:
-                tc(P, X("nn")[:], g_("nn"), [tp])
-            else:
-                tt(P, X("nn")[:], pm[:, 128:256], OP.add, [PM] + g_("nn"), [tp])
             if k < 3:
-                MM(["I", tp], [PM], grp(pm[:, 128:256], [(M("I"), P)]), 128)
-                ts(X("msk")[:, 1:256:2], P, co(kk), None, OP.is_ge, None, [tp, "co%d" % kk] + g_("mskz"), g_("msk"))
-                scan(X("pp")[:], X("msk")[:], X("pt")[:, 256 * k:256 * kk], OP.add, [tp, "lp%d%s" % (kk, h)] + g_("msk", "mskz"), g_("pp"), 256)
-                hn = "h%d" % kk
-                hts = []
-                for q in range(kk + 1, {1: 9, 2: 13, 3: 17}[kk]):
-                    hts.append("%s%s_%d" % (hn, h, q))
-
-                    def mk(o, i, d):
-                        return [("v", cv(64, 1), lambda: g.vector.tensor_scalar(o, i, float(d), None, OP.is_lt)),
-                                ("s", cs(128), lambda: g.scalar.activation(o, i, AF.Sigmoid, scale=-200.0, bias=200.0 * d - 100.0))]
-                    add(mk(X(hn)[:, q - 1:2048:16], ppv, q - kk), g_("pp", hn), [hts[-1]])
-                scan(X("sc")[:], X(hn)[:], X("dt")[:], OP.add, hts + g_(hn) + ["dt%d%s" % (n, h) for n in range(4)], g_("sc"), 2048)
-                mv = c512(15, 16)
-        gather(4, h)
+                nw = NW[kk]
+                tab, col = table(8, nw)
+                MM([cg, "ON", "CL"] + ["W%d" % (kk + 2 * a) for a in range(nw)], B_(8, 8),
+                   [(col(a, s), M("W%d" % (kk + 2 * a)), Cp(s), a == 0, False) for a in range(nw) for s in parts]
+                   + [(col(nw - 1, s), M("CL"), ones(64), False, False) for s in parts])
+            for s in parts:
+                gather(k, s)
+                mm(["wl", "ON"] + g_("z%d%d" % (k, s)), B_(0), (pd[:, 64 * s:64 * s + 64],
+                   [("CU", ones(64))] + [(WM("wl", m), X("zz", 4096 * s + 4 * m + k, 4096 * s + 4096, 64)) for m in range(16)]))
+            tt(X("x32"), P_(0), y8, OP.mult, B_(0) + g_("y8"), g_("x32"))
+            lin(P_(4), P_(0), 37.0, 3947.0, B_(0) + B_(4), g_("u37"))
+            tt(X("n32"), P_(0), X("c8" if k else "c8f"), OP.add, B_(0) + g_("c8"), g_("n32"))
+            tt(X("r32"), X("x32"), P_(4), OP.add, B_(4) + g_("x32", "u37"), g_("r32"))
+            ts(X("s32"), X("r32"), 4095, None, OP.bitwise_and, None, g_("r32"), g_("s32"))
+            tc(X("offs"), X("s32"), g_("s32"), g_("off"))
+            P, tp = pts[k], "p%d%s" % (kk, h)
+            ts(X("nn"), X("n32"), 3, 3, OP.arith_shift_right, OP.bitwise_and, g_("n32"), g_("nn"))
+            if k == 0:
+                ts(P, X("nn"), -6.0, None, OP.add, None, g_("nn"), [tp])
+            else:
+                tt(P, X("nn"), P_(6), OP.add, B_(6) + g_("nn"), [tp])
+            if k < 3:
+                mm([tp], B_(6), (P_(6), [("I", P)]))
+                ts(X("msk", 1, 2 * n, 2), P, co(kk), None, OP.is_ge, None, [tp, "co%d" % kk, "mskz"], g_("msk"), 0.5)
+                scan(X("pp"), X("msk"), X("pt", 2 * n * k, 2 * n * kk), OP.mult, OP.add, [tp, "mskz"] + g_("msk", "lp%d" % kk), g_("pp"), 0.5)
+                MM(["K%d" % a for a in range(nw)] + g_("pp"), B_(8, 8),
+                   [(col(a, s), M("K%d" % a), X("pp", 128 * s + 1, 128 * s + 128, 2), False, a == nw - 1) for a in range(nw) for s in parts])
+                lin(X("rr"), ppv, 0.5, 194.75, g_("pp"), g_("rr"), 0.5)
+                mm(["ON"] + g_("pp", "rr"), B_(5), (P_(5), [("CF", ones(n)), ("mI256", ppv), ("Ih", ppv), ("I512", X("rr")), ("mI", X("rr"))]))
+                scan(X("sc", 0, n * nw), T["q%d" % nw][:, 0:n * nw], tab, OP.add, OP.max, B_(8, 8) + ["q%d" % nw], g_("sc"))
+                tt(X("xi"), P_(5), X("sc", nw - 1, n * nw, nw), OP.mult, B_(5) + g_("sc"), g_("xi"))
+                ts(X("c8"), X("xi"), 2044, None, OP.bitwise_and, None, g_("xi"), g_("c8"))
+                ts(y8, X("c8"), 0.03125, -0.75, OP.mult, OP.add, g_("c8"), g_("y8"))
+        v1 = g_(*["v1%d" % j for j in range(n // SW)])
+        for j in range(n // SW):
+            o, s = 64 * SW * j, SW * j // 64
+            scan(X("vs", 14 + o, 14 + o + 64 * SW), T.mk4[:, 0:64 * SW], X("zz", o, o + 64 * SW), OP.min, OP.max,
+                 ["mk40"] + g_(*["z%d%d" % (k, s) for k in range(4)]), [v1[j]] + g_(*{"z4%d" % s, "z4%d" % (max(SW * j - 1, 0) // 64)}), 0.5)
+        cpy(X("zz", 0, 64 * n, 64), F, ["ff" + h] + v1, g_("fs"))
+        bk = lambda s: ["#%s%d" % (h, x) for x in ((2, 3) if n == 128 and s == 0 else (0, 1))]
+        vf = lambda s, m, c=1: pd[:, 1024 * (n == 128 and s == 0) + 64 * m:1024 * (n == 128 and s == 0) + 64 * (m + c)]
+        for s in parts:
+            MM(["mI", "ff" + h], bk(s), [(vf(s, m), M("mI"), T.ff[:, b + 64 * s:b + 64 * s + 64], m % 8 == 0, False) for m in range(16)])
+            gather(4, s)
         yield
-        for s in (0, 1):
-            o = zb + 5120 * s
-            scan(T.vs[:, o:o + 5120], T.mk5[:], T.zz[:, o:o + 5120], OP.max, ["mk5", "z4%s%d" % (h, s)] + ["z%d%s0" % (k, h) for k in range(4)], ["vs%d%s" % (s, h)], 5120)
-            it = []
-            for m in range(16):
-                it += grp(pd[:, 64 * m:64 * m + 64], [(M("I"), T.vs[:, o + 5 * m + 4:o + 5 * m + 4 + 80 * 63 + 1:80]), (M("mI"), T.ff[:, b + 64 * s:b + 64 * s + 64])])
-            MM(["I", "mI", "vs%d%s" % (s, h), "ff" + h], [D0, D1], it, 64)
-            act(X("gg")[:], pd[:], AF.Sign, [D0, D1], g_("gg"), 1024, bias=0.5)
-            MM(["cl"] + g_("gg"), [PM], grp(pm[:, 64 * s:64 * s + 64], [(WM("cl", m), X("gg")[:, 64 * m:64 * m + 64]) for m in range(16)]), 64)
-        cpy(T.vs[:, zb:zb + 10240:80], T.ff[:, b:b + 128], ["ff" + h, "vs0" + h, "vs1" + h], ["vs0" + h, "vs1" + h])
-        flex(X("fl")[:], pm[:, 0:128], AF.Sigmoid, [PM], g_("fl"), 128, (1.0, None, OP.is_ge), scale=200.0, bias=-100.0)
-        tt(X("fw")[:], X("fl")[:], X("w3")[:], OP.mult, g_("fl", "w3"), g_("fw"), 256)
-        MM(["BD32"] + g_("fw"), [PU], grp(pu[:, 0:128], [(M("BD32"), X("fw")[:])]), 128)
-        tt(X("cand")[:], X("fw")[:], pu[:, 0:128], OP.is_gt, [PU] + g_("fw"), g_("cand"))
-        MM(["LT"] + g_("cand"), [PU], grp(pu[:, 128:256], [(M("LT"), X("cand")[:])]), 128)
-        tt(win[:], X("cand")[:], pu[:, 128:256], OP.is_gt, [PU] + g_("cand"), g_("win"))
-        if h == "b" and t < 2:
-            MM(["ON", "wina", "winb"], [PM], grp(pm[:, 384:512], [(M("ON"), T.wina[:]), (M("ON"), T.winb[:])]), 128)
-            act(T.junk[:], pm[:, 384:512], AF.Copy, [PM], ["f64", "f32", "ac%d" % (t + 1)], accum_out=T.ac[:, 4 * t + 4:4 * t + 5])
-        MM(["mo"] + g_("win"), [PU], grp(pu[:, 0:8], [(WM("mo", a), win[:, a:128:16]) for a in range(16)]), 8)
-        tt(X("o32")[:], pu[:, 0:8], T.c80[:], OP.add, [PU, "c80"], g_("o32"))
-        ts(X("nk")[:], pu[:, 0:8], 1.0, 4096.0, OP.is_lt, OP.mult, [PU], g_("nk"))
-        tc(X("ofs")[:], X("o32")[:], g_("o32"), g_("ofs"), 64)
-        tc(X("vsel")[:], T.vs[:, zb:zb + 10240].indirect(X("ofs")[:]), ["vs0" + h, "vs1" + h] + g_("ofs"), g_("vsel"), 192)
-        MM(["wl"] + g_("vsel"), [PU], grp(pu[:, 8:16], [(WM("wl", a), X("vsel")[:, a:128:16]) for a in range(16)]), 8)
-        tt(X("nk")[:], X("nk")[:], T.c16[:, b // 16:b // 16 + 8], OP.add, ["c16"] + g_("nk"), g_("nk"))
-        tc(X("q32")[:], pu[:, 8:16], [PU], g_("q32"), 64)
-        ts(X("o32")[:], X("q32")[:], 6, 15, OP.arith_shift_right, OP.bitwise_and, g_("q32"), g_("o32"))
-        tt(X("q32")[:], X("o32")[:], X("nk")[:], OP.add, g_("o32", "nk"), g_("q32"))
-        tc(X("of2")[:], X("q32")[:], g_("q32"), g_("of2"), 64)
-        tc(T.xt[:].indirect(X("of2")[:]), X("vsel")[:], g_("of2", "vsel"), ["x"], 512)
-        MM(["I", "I16", lg, "p1" + h, "p2" + h, "p3" + h, "p4" + h] + g_("win"), [D0, D1],
-           [x for j in range(5) for x in grp(pd[:, 128 * j:128 * j + 128], [(M("I"), pts[j - 1] if j else L), (M("I16"), win[:])])], 128)
-        flex(wx[:], pd[:, 0:640], AF.Relu, [D0, D1], g_("wx"), 640, (-16.0, 0.0, OP.add, OP.max), bias=-16.0)
-        MM(["LE"] + g_("wx"), [PU], grp(pu[:, 128:256], [(M("LE"), wx[:, 0:128])]), 128)
-        for d in (1, 2, 3, 4):
-            flex(X("hn")[:, d:640:5], pu[:, 128:256], AF.Sigmoid, [PU, "hnz" + h], ["+hn" + h], 128, (float(d), None, OP.is_lt), scale=-200.0, bias=200.0 * d - 100.0)
-        scan(X("scn")[:], X("hn")[:], X("rd")[:], OP.add, g_("hn") + ["rd%d%s" % (d, h) for d in range(5)], g_("scn"), 640)
-        NRt = T["nr%d" % t]
-        flex(NRt[:, b:b + 128], X("scn")[:, 4:640:5], AF.Copy, g_("scn"), ["nc%d%s" % (t, h)], 64, None)
+        for s in parts:
+            for o in (4096 * s, 4096 * s + 2048):
+                scan(X("zz", o + 1, o + 2048, 2), T.mk4[:, 0:2048:2], X("vs", o + 17, o + 2064, 2), OP.min, OP.max,
+                     ["mk40"] + v1 + g_("z4%d" % s), ["+vt%d%s" % (s, h)], 0.5)
+            MM(["I"] + g_("vt%d" % s), bk(s), [(vf(s, m), M("I"), X("zz", 4096 * s + 4 * m + 3, 4096 * s + 4096, 64), False, m % 8 == 7) for m in range(16)])
+            act(X("gg", 1024 * s, 1024 * s + 1024), vf(s, 0, 16), AF.Sign, bk(s), g_("gg%d" % s), bias=0.5)
+        o = n * 8
+        for s in parts:
+            mm(["cl", "kmx"] + g_("gg%d" % s, "w3"), B_(8), (pd[:, o + 128 * s + 1:o + 128 * s + 128:2], [("I", X("w3", 64 * s, 64 * s + 64))]),
+               (pd[:, o + 128 * s:o + 128 * s + 128:2], [("I", T.kmx[:, 0:64])] + [(WM("cl", m), X("gg", 1024 * s + 64 * m, 1024 * s + 64 * m + 64)) for m in range(16)]))
+        scan(X("fw"), T.q2[:, 0:2 * n], P_(8, 2), OP.max, OP.min, B_(8) + ["q2"], g_("fw"))
+        fw = X("fw", 1, 2 * n, 2)
+        mm(g_("fw"), B_(8), (P_(10), [("BH", fw)]))
+        tt(win, fw, P_(10), OP.is_gt, B_(8) + g_("fw"), g_("win"))
+        if b + n == 256 and t < 2:
+            mm(["win" + x for x in CH], B_(12), (pd[:, 12 * n:12 * n + 64], [("ON", T.win[:, 2 * x + 64 * s:2 * x + 64 * s + 64]) for x, y in CH.values() for s in range(y // 64)]))
+            act(T.junk[:, 0:64], pd[:, 12 * n:12 * n + 64], AF.Copy, B_(12), ["f64", "f32", "ac%d" % (t + 1)], accum_out=T.ac[:, 4 * t + 4:4 * t + 5])
+        e = n // 16
+        pk, po, ph = (pd[:, 4 * n + e * j:4 * n + e * (j + 1)] for j in range(3))
+        ts(X("win", n, 2 * n), win, co(8), None, OP.mult, None, g_("win") + ["co8"], g_("wo"), 0.5)
+        mm(["cl", "c16"] + g_("win", "wo"), B_(4), (pd[:, 4 * n:4 * n + 2 * e], [("I", T.c16[:, b // 8:(b + n) // 8])] + [(WM("cl", a), X("win", a, 2 * n, 16)) for a in range(16)]))
+        tc(X("ofs"), po, B_(4), g_("ofs"))
+        flex(X("vsel"), X("zz").indirect(X("ofs")), AF.Copy, g_("ofs", "fs", *["vt%d" % s for s in parts]), g_("vsel"), None, 1.5)
+        mm(["wl"] + g_("vsel"), B_(4), (ph, [(WM("wl", a), X("vsel", a, n, 16)) for a in range(16)]))
+        tc(X("q32"), ph, B_(4), g_("q32"))
+        ts(X("o32"), X("q32"), 15, None, OP.bitwise_and, None, g_("q32"), g_("o32"))
+        tt(X("q32"), X("o32"), pk, OP.add, B_(4) + g_("o32"), g_("q32"))
+        tc(X("of2"), X("q32"), g_("q32"), g_("of2"))
+        vop("tc", cv(n, 4), g_("of2", "vsel"), ["x"], T.xt[:].indirect(X("of2")), X("vsel"))
+        w0 = 0 if n == 128 else 12
+        relu = dict(v=(-26.0, 0.0, OP.add, OP.max), bias=-26.0)
+        mm([lg, "km6"] + g_("win"), B_(11), (P_(11), [("I", L), ("I", T.km6[:, 0:n]), ("I32", win)]))
+        mm(g_("win", "p1", "p2", "p3", "p4"), B_(w0), *[(P_(w0 + j), [("I", pts[j]), ("I32", win)]) for j in range(4)])
+        if n == 128:
+            flex(wx(0), P_(11), AF.Relu, B_(11), g_("wx0"), **relu)
+            flex(wx(1, 4), P_(0, 4), AF.Relu, B_(0), g_("wx"), **relu)
+        else:
+            flex(X("wx"), P_(11, 5), AF.Relu, B_(11), g_("wx0", "wx"), **relu)
+        y0, l0 = (0, 8) if n == 128 else (8, 0)
+        mm(g_("wx", "win"), B_(y0), *[(P_(y0 + j - 1), [("B1", wx(j)), (("B1", "BX2", "BX3", "BX32")[j - 1], win)]) for j in (1, 2, 3, 4)])
+        act(X("ax"), P_(y0, 3), AF.Abs, B_(y0) + ["co5"], g_("ax"), bias=co(5))
+        ts(P_(7), P_(y0 + 3), co(4), None, OP.is_equal, None, B_(y0) + B_(7) + ["co4"], g_("m4"))
+        tab, col = table(l0, 5)
+        xq = l0 if n == 128 else 5
+        mm([cg] + g_("wx0"), B_(l0, 8), (P_(xq), [("LE", wx(0))]),
+           *[(col(4 - d, s), [("S%d" % d if d else "I", Cp(s))] + ([("LE%d" % d, X("wx", 64 * s, 64 * s + 64))] if d else [])) for d in range(5) for s in parts])
+        scan(X("sn"), T.q5[:, 0:5 * n], tab, OP.add, OP.max, B_(l0, 8) + ["q5"], g_("sn"))
+        act(P_(xq), P_(xq), AF.Square, B_(xq), g_("sq"), scale=16.0)
+        nc, nl = "nc%d%s" % (t, h), "nl%d%s" % (t, h)
+        tt(NC, X("sn", 4, 5 * n, 5), P_(xq), OP.subtract, B_(xq) + g_("sn", "sq"), [nc])
         if t < 2:
-            send(("c" + h, t + 1), NRt[:, b:b + 128], ["nc%d%s" % (t, h)])
-        MM(["B1", "BX32"] + g_("wx", "win"), [D0], [x for j in (1, 2, 3, 4) for x in grp(pd[:, 128 * j - 128:128 * j],
-           [(M("B1"), wx[:, 128 * j:128 * j + 128])] + ([(M("BX32"), win[:])] if j == 4 else []))], 128)
-        ts(X("m4")[:], pd[:, 384:512], co(4), None, OP.is_equal, None, [D0, "co4"], g_("m4"), 128)
-        for j in (1, 2, 3):
-            act(X("ax")[:, 128 * j - 128:128 * j], pd[:, 128 * j - 128:128 * j], AF.Abs, [D0, "co%d" % (4 + j)], ["+ax" + h], bias=co(4 + j))
-        tc(X("z4")[:], T.zz[:, zb:zb + 10240].indirect(X("ofs")[:]), g_("ofs") + ["z4%s1" % h] + ["z%d%s0" % (k, h) for k in range(5)], g_("z4"), 192)
-        tt(X("t4")[:], X("m4")[:], X("scn")[:, 4:640:5], OP.mult, g_("m4", "scn"), g_("t4"), 256)
-        MM(["BW", "B512"] + g_("z4", "t4"), [PU], grp(pu[:, 0:128], [(M("BW"), X("z4")[:]), (M("B512"), X("t4")[:])]), 128)
-        tc(X("n4")[:], pu[:, 0:128], [PU], g_("n4"))
-        ts(X("n5")[:], X("n4")[:], 9, 3, OP.arith_shift_right, OP.bitwise_and, g_("n4"), g_("n5"), 128)
-        tt(X("n4m")[:], X("n5")[:], X("m4")[:], OP.mult, g_("n5", "m4"), g_("n4m"), 256)
-        it = []
-        for j in (1, 2, 3):
-            it += grp(pd[:, 384 + 128 * j:512 + 128 * j], [(M("B1"), wx[:, 128 * j + 128:128 * j + 256]), (M("mB1"), wx[:, 128 * j:128 * j + 128]), (M("mI4"), X("ax")[:, 128 * j - 128:128 * j])])
-        it += grp(pd[:, 896:1024], [(M("I"), L), (M("mB8"), win[:]), (M("I"), T.km1[:])])
-        MM(["B1", "mB1", "mI4", "mB8", "I", "km1", lg] + g_("wx", "ax", "win"), [D1], it, 128)
-        flex(X("ex")[:], pd[:, 512:1024], AF.Relu, [D1], g_("ex"), 512, (0.0, None, OP.max))
-        MM(["BQ0", "I"] + g_("wx", "ex", "n4m"), [PU],
-           grp(pu[:, 256:384], [(M("BQ0"), wx[:, 128:256])] + [(M("I"), X("ex")[:, 128 * j:128 * j + 128]) for j in range(4)] + [(M("I"), X("n4m")[:])]), 128)
-        flex(NRt[:, 256 + b:384 + b], pu[:, 256:384], AF.Identity, [PU], ["nl%d%s" % (t, h)], 128, (1.0, None, OP.add), bias=1.0)
+            send(("c" + h, t + 1), NC, [nc])
+        e0 = 0 if n == 128 else 12
+        mm([lg, "km1"] + g_("wx", "ax", "win"), B_(e0), *([(P_(e0 + j - 1), [("B1", wx(j + 1)), ("mB1", wx(j)), ("mI4", X("ax", n * j - n, n * j))]) for j in (1, 2, 3)]
+                                                          + [(P_(e0 + 3), [("I", L), ("mB8", win), ("I", T.km1[:, 0:n])])]))
+        flex(X("ex"), P_(e0, 4), AF.Relu, B_(e0), g_("ex"), (0.0, None, OP.max))
+        flex(X("z4"), X("vs", 16, 16 + 64 * n).indirect(X("ofs")), AF.Copy, ["vz"] + g_("ofs") + zt(4) + v1, g_("zw"), None, 1.5)
+        tt(X("t4"), NC, P_(7), OP.mult, [nc] + B_(7) + g_("m4"), g_("t4"))
+        n0 = 12 if n == 128 else 0
+        mm(g_("zw", "t4"), B_(n0), (P_(n0), [("BW", X("z4")), ("B8", X("t4"))]))
+        tc(X("n4"), P_(n0), B_(n0), g_("n4"))
+        ts(X("n5"), X("n4"), 3, 3, OP.arith_shift_right, OP.bitwise_and, g_("n4"), g_("n5"))
+        tt(X("n4m"), X("n5"), P_(7), OP.mult, B_(7) + g_("n5", "m4"), g_("n4m"))
+        it = grp(P_(y0), [("BQ0", wx(1))] + [("I", X("ex", n * j, n * j + n)) for j in range(4)] + [("I", X("n4m"))])
+        MM(["BQ0", "I"] + g_("wx", "ex"), B_(y0), it[:-1])
+        MM(g_("n4m"), B_(y0), it[-1:])
+        lin(NL, P_(y0), 1.0, 1.0, B_(y0), [nl])
         if t < 2:
-            send(("l" + h, t + 1), NRt[:, 256 + b:384 + b], ["nl%d%s" % (t, h)])
-        MM(["I", "kmh", "ff" + h] + g_("vsel"), [PM], grp(pm[:, 384:512], [(M("I"), T.ff[:, b:b + 128]), (M("I"), X("vsel")[:]), (M("I"), T.kmh[:])]), 128)
-        act(X("f1")[:], pm[:, 384:512], AF.Identity, [PM], g_("f1"), scale=0.5, bias=12582912.0)
-        act(T.ff[:, b:b + 128], X("f1")[:], AF.Identity, g_("f1"), ["ff" + h], bias=-12582912.0)
+            send(("l" + h, t + 1), NL, [nl])
+        mm(["kmh", "ff" + h] + g_("vsel"), B_(6), (P_(6), [("I", F), ("I", X("vsel")), ("I", T.kmh[:, 0:n])]))
+        lin(X("f1"), P_(6), 0.5, 12582912.0, B_(6), g_("f1"))
+        lin(F, X("f1"), 1.0, -12582912.0, g_("f1"), ["ff" + h])
 
     for t in range(3):
-        for h in "ab":
-            places(t, h)
         if t == 1:
-            send(("st", 2), T.rec1[:, 512:1024], ["s1"])
-        for part in [stream(t, h) for h in "ab"] * 2:
+            send(("s", 2), T.rec1[:, 512:1024], ["s1"])
+        for part in [stream(t, h) for h in CH] * 2:
             next(part, None)
-    for hb in (0, 1):
-        MM(["I", "x"], ["#pu" + "ab"[hb]], grp(T["pu" + "ab"[hb]][:, 0:128], [(M("I"), T.xt[:, 2048 * hb + a:2048 * hb + 2048:16]) for a in range(16)]), 128)
-        act(T.ysb[:, 128 * hb:128 * hb + 128], T["pu" + "ab"[hb]][:, 0:128], AF.Copy, ["#pu" + "ab"[hb]], ["ysb%d" % hb])
-    dma("y", "o_c", T.yc[:], T.nr2[:, 0:256], ["nc2a", "nc2b"], [])
-    dma("y", "o_l", T.yl[:], T.nr2[:, 256:512], ["nl2a", "nl2b"], [])
-    dma("y", "o_f", T.yf[:], T.ff[:], ["ffa", "ffb"], [])
+    for j in (0, 1):
+        o = T.pda[:, 512 * j:512 * j + 128]
+        mm(["x"], ["#a%d" % j], (o, [("I", T.xt[:, 4096 + 2048 * j + a:6144 + 2048 * j:16]) for a in range(16)]))
+        flex(T.ysb[:, 128 * j:128 * j + 128], o, AF.Copy, ["#a%d" % j], ["ysb%d" % j], None)
+    dma("y", "o_c", T.yc[:], T.nr2[:, 0:256], ["nc2" + h for h in CH], [])
+    dma("y", "o_l", T.yl[:], T.nr2[:, 256:512], ["nl2" + h for h in CH], [])
+    dma("y", "o_f", T.yf[:], T.ff[:], ["ff" + h for h in CH], [])
     dma("y", "o_s", T.ys[:], T.ysb[:], ["ysb0", "ysb1"], [])
 
     Q = {"v": g.vector, "s": g.scalar, "t": g.tensor, "g": g, "y": g.sync}
@@ -489,7 +537,8 @@ def rank_program(g, core, T, topo):
     known = {q: {} for q in Q}
     lw, rd, bank = {}, {}, {}
     if not KEEP:
-        KEEP.append(order([(n[0], n[1], n[2], n[3][0]) for n in nodes]))
+        turn = sorted((t, k + LAG[h], -k, h, s, j) for (t, k, h, s), j in gat.items() if "%d%s%d" % (k, h, s) not in VG)
+        KEEP.append(order([(n[0], n[1], n[2], n[3][0]) for n in nodes], [(x[-1], y[-1]) for x, y in zip(turn, turn[1:])]))
     for _, j, a in KEEP[0]:
         (q, _, f), (_, r, w, kind) = nodes[j][0][a], nodes[j]
         if kind[0] == "arr":

@@ -4,24 +4,28 @@ from concourse.mybir import AluOpType as OP, AxisListType, ActivationFunctionTyp
 CH = {"a": (0, 128), "b": (128, 128)}
 NW = {1: 4, 2: 6, 3: 7}
 FIRST = sorted({k + 2 * a for k in NW for a in range(NW[k])})
-DIAG = {"I": 1, "mI": -1, "I512": 512, "I101": 101, "I64": 64, "I32": 32, "mI4": -4, "mI128": -128, "mI256": -256, "Ih": 0.5}
+DIAG = {"I": 1, "mI": -1, "I512": 512, "I101": 101, "I64": 64, "I32": 32, "mI4": -4, "mI128": -128, "mI256": -256, "Ih": 0.5, "Iq": 0.25}
 DIAG.update({"K%d" % a: (4 * a - 11) * 2048 for a in range(7)})
 BLOCK = {"mB1": -1, "mB8": -8, "BH": 0.5, "B8": 8, "BX32": 32, "BX2": 2, "BX3": 3}
 ROWS = {"CU": (-32768, 4, 2.0 ** -9), "CL": (2048, 56, 7 / 64), "CF": (-98304, -1024, -61)}
-SLOTS = ["B1", "ON", "LE", "S1", "S2", "S3", "S4", "BW", "BQ0", "BR0", "BR1"] + list(DIAG) + list(BLOCK) + list(ROWS)
+SLOTS = ["B1", "ON", "LE", "LEq", "S1", "S2", "S3", "S4", "BW", "BQ0", "BR0", "BR1"] + list(DIAG) + list(BLOCK) + list(ROWS)
 SLOTS += ["W%d" % e for e in FIRST] + ["LE%d" % d for d in (1, 2, 3, 4)]
 SLOT = {n: j for j, n in enumerate(SLOTS)}
-BUF = {"bfloat16": "xt_8192 mk4_2048 wl_2064 cl_2064 ff_256 wtb_16 onef_16 e16_16 tmpm_128 km1_128 km6_128 kmh_128 kmx_128 q2_256 junk_128 c16_32",
+BUF = {"bfloat16": "xt_8192 mk5_2560 wl_2064 cl_2064 ff_256 wtb_16 onef_16 e16_16 tmpm_128 km1_128 kmh_128 kmx_128 q2_256 junk_128 c16_32",
        "float32": "sd_16 jio_16 jt_16 co_24 b8f_8 bw8_8 bc8_8 ct_16 ac_16 ysb_256 q4_512 q5_640 q6_768 q7_896", "int32": "sti_256 tmi_256 tmj_256"}
-BUFH = {"bfloat16": "zz_4096 vs_4112 pt_448 pp_128 msk_128 y8_64 rr_64 ax0_64 sel_64 gg_1024 w3_64 fw_128 win_128 vsel_64 z4_64 wx_320 ax_192 ex_256 t4_64 n4m_64",
+BUFH = {"bfloat16": "zz_5120 vs_5120 pt_448 pp_128 msk_128 y8_64 rr_64 ax0_64 sel_64 gg_1024 w3_64 fw_128 win_128 vsel_64 z4_64 wx_384 l2_64 ax_192 ex_256 t4_64 n4m_64",
         "float32": "f1_64 c8f_64 sc_448 sn_320", "int32": "s32_64 x32_64 r32_64 n32_64 nn_64 xi_64 c8_64 n4_64 n5_64 o32_4 q32_4", "uint16": "offs_64 ofs_4 of2_4"}
 SIZE = {s.split("_")[0]: int(s.split("_")[1]) for names in BUFH.values() for s in names.split()}
-LAG = {"a": 0, "b": 0.5}
-VG = ["0b0"]
-SW = 32
-BIAS, PASSES = 0.3, 12
-ARR, MMF, PEC, CYC, FV, SAME, CROSS = 4000, 3, 0.38, 0.87, 30, 90, 220
-NOISE, SCALES = 1000, [{}, {"n": 1.8}, {"v": 1.1, "s": 1.2}]
+LAG = {"a": (0, 0, 0, 0), "b": (0.5, 0.5, 0.5, 0.5)}
+VG = ["0a1", "0b0", "0b0"]
+S5 = 32
+GW = 64
+ONS = ""
+AHEAD = {}
+TRIES, SHIFT, FS, GK = 7000, 400, 60, 1.62
+BIAS, PASSES = 0.3, 8
+ARR, MMF, PEC, CYC, FV, SAME, CROSS = 3300, 4, 0.36, 0.85, 30, 140, 230
+NOISE, SCALES = 300, [{}, {"n": 1.8}, {"v": 1.1}, {"s": 1.1, "t": 1.2}]
 
 
 def _bufs():
@@ -70,10 +74,10 @@ def cv(n, k):
 
 
 def cs(n, k=1):
-    return 65 + n * k * CYC
+    return FS + n * k * CYC
 
 
-def order(nodes, after):
+def order(nodes, after, ahead, names):
     n = len(nodes)
     pred, succ, lw, rd = [[] for _ in range(n)], [[] for _ in range(n)], {}, {}
     for j, (alts, r, w, _) in enumerate(nodes):
@@ -113,7 +117,7 @@ def order(nodes, after):
             j = max(ready, key=lambda x: prio[x])
             ready.remove(j)
             best = None
-            for a, (q, cost) in enumerate(x[:2] for x in nodes[j][0]):
+            for a, (q, cost) in enumerate(x[:2] for x in nodes[j][0][:1 if nodes[j][3] == "pin" else 2]):
                 s = max([end[p] + (SAME if nodes[p][0][alt[p]][0] == q else CROSS) for p in pred[j]] + [0.0])
                 hold = {"dma": 70, "arr": 0}.get(nodes[j][3], cost)
                 iv = busy.setdefault(q, [])
@@ -137,24 +141,73 @@ def order(nodes, after):
                     ready.append(x)
         return start, end, alt
 
-    def replay(seq, scale):
-        free, end, qof = {}, [0.0] * n, [None] * n
+    def replay(seq, scale, held=None):
+        free, end, qof, f = dict.fromkeys("vstgyn", 0.0), [0.0] * n, [None] * n, {q: scale.get(q, 1.0) for q in "vstgyn"}
         for _, j, a in seq:
-            q, cost = nodes[j][0][a][:2]
-            cost *= scale.get(q, 1.0)
-            s = max([end[p] + (SAME if qof[p] == q else CROSS) for p in pred[j]] + [free.get(q, 0.0)])
-            end[j], qof[j] = s + cost, q
-            free[q] = {"dma": s + 70, "arr": 0.0}.get(nodes[j][3], s + cost)
+            q, cost = short[j][a]
+            s = free[q]
+            for p in pred[j]:
+                x = end[p] + (SAME if qof[p] == q else CROSS)
+                if x > s:
+                    s = x
+            x = end[j] = s + cost * f[q]
+            qof[j] = q
+            free[q] = x if plain[j] else s + 70 if q != "n" else 0.0
+        if held is not None:
+            at, before, last = {}, {}, {}
+            for k, (_, j, a) in enumerate(seq):
+                at[j], before[j], last[qof[j]] = k, last.get(qof[j]), j
+            j = end.index(max(end))
+            while j is not None:
+                s = end[j] - short[j][seq[at[j]][2]][1] * f[qof[j]]
+                w = [p for p in pred[j] if end[p] + (SAME if qof[p] == qof[j] else CROSS) > s - 1e-3]
+                if not w and before[j] is not None:
+                    held.append((at[before[j]], at[j]))
+                j = w[0] if w else before[j]
         return max(end)
+
+    plain, short = [x[3] not in ("dma", "arr") for x in nodes], [[a[:2] for a in x[0]] for x in nodes]
 
     best, rng = None, np.random.default_rng(0)
     for i in range(PASSES):
-        start, end, alt = place(pred, succ, prio)
+        start, end, alt = place(pred, succ, [x + y for x, y in zip(prio, ahead)])
         seq = sorted((start[j], j, alt[j]) for j in range(n))
         e = sum(replay(seq, x) for x in SCALES)
         if best is None or e < best[0]:
             best = (e, seq, end)
         prio = place(succ, pred, [x + NOISE * float(y) for x, y in zip(best[2] if i % 4 == 3 else end, rng.random(n))])[1]
+    for p, j in after:
+        pred[j].discard(p)
+    e, seq, held = best[0], best[1], []
+    for i in range(TRIES):
+        if not held:
+            for s in SCALES:
+                replay(seq, s, held)
+            at = {c[1]: k for k, c in enumerate(seq)}
+        x, y = held[int(rng.integers(len(held)))]
+        j, k, move = seq[x][1], seq[y][1], int(rng.integers(4))
+        if move == 0:
+            z = max([at[p] for p in pred[k]] + [-1]) + 1
+            if z > x:
+                continue
+            z = x - int(rng.integers(min(x - z, 12) + 1))
+            new = seq[:z] + [seq[y]] + seq[z:y] + seq[y + 1:]
+        elif move == 1:
+            z = min([at[s] for s in succ[j] if j in pred[s]] + [n]) - 1
+            if z < y:
+                continue
+            z = y + int(rng.integers(min(z - y, 12) + 1))
+            new = seq[:x] + seq[x + 1:z + 1] + [seq[x]] + seq[z + 1:]
+        elif move > 1 and len(nodes[seq[(x, y)[move - 2]][1]][0]) > 1:
+            z = (x, y)[move - 2]
+            new = seq[:z] + [(seq[z][0], seq[z][1], 1 - seq[z][2])] + seq[z + 1:]
+        else:
+            continue
+        f = sum(replay(new, s) for s in SCALES)
+        if f <= e + SHIFT * (1 - i / TRIES):
+            e, seq, held = f, new, []
+            if e < best[0]:
+                best = (e, seq)
     return best[1]
 
 
@@ -182,10 +235,11 @@ def rank_program(g, core, T, topo):
         return
 
     nxt, prv = T.cores[(rank + 1) % N], T.cores[(rank - 1) % N]
-    nodes = []
+    nodes, parts_of, now = [], [], ["start"]
 
     def add(alts, r, w, kind="op"):
         nodes.append((alts, list(r), list(w), kind))
+        parts_of.append(now[0])
 
     def vop(meth, cost, r, w, *a):
         add([("v", cost, lambda: {"tt": g.vector.tensor_tensor, "ts": g.vector.tensor_scalar, "tc": g.vector.tensor_copy, "ms": g.vector.memset,
@@ -215,6 +269,12 @@ def rank_program(g, core, T, topo):
 
     def lin(out, in_, f, o, r, w, kv=1):
         flex(out, in_, AF.Identity, r, w, (f, o, OP.mult, OP.add), 1, kv, scale=f, bias=o)
+
+    def only(x):
+        if x in ONS:
+            del nodes[-1][0][1]
+        if x.upper() in ONS:
+            del nodes[-1][0][0]
 
     def gp(meth, r, w, *a, **kw):
         add([("g", 400, lambda: {"iota": g.iota, "sel": g.affine_select}[meth](*a, **kw))], r, w)
@@ -259,7 +319,7 @@ def rank_program(g, core, T, topo):
     dma("s", "ld_ch", T.rec0[:, 0:256], T.ch[:], [], ["c0" + h for h in CH])
     dma("s", "ld_fl", T.ff[:], T.fl[:], [], ["ff" + h for h in CH])
     ms(M("ON"), 1.0, ["ON"]); ms(T.onef[:], 1.0, ["onef"]); ms(T.wl[:], 0.0, ["wl0"]); ms(T.cl[:], 0.0, ["cl0"])
-    fill("mk4", [[0, 512], [256, 4]], 0, 2048)
+    fill("mk5", [[0, 512], [256, 5]], 0, 2560)
     for k in (4, 6, 7):
         fill("q%d" % k, [[0, 128], [16384, k]], -26 * 2048, 128 * k)
         ms(T["q%d" % k][:, 0:128 * k:k], -1e9, ["+q%d" % k], ["q%d0" % k], 1)
@@ -285,16 +345,17 @@ def rank_program(g, core, T, topo):
     tt(T.jt[:], T.e16[:], T.jio[:], OP.mult, ["e16", "jio"], ["jt"])
     co = lambda j: T.co[:, j:j + 1]
     vop("tr", 120, ["jt"], ["co0"], co(0), T.jt[:], AxisListType.X, OP.add)
-    for j, f, o in ((1, 1, -7), (2, 1, -8), (3, 1, -9), (4, 1, 28), (5, -1, 0), (8, 4 / 4096, 3 / 4096), (10, -LN2, -80 * LN2), (11, 16, 0)):
+    for j, f, o in ((1, 1, -7), (2, 1, -8), (3, 1, -9), (4, 1, 28), (5, -1, 0), (8, 5 / 4096, 4 / 4096), (13, -200, 1500), (14, -200, 1700), (15, -200, 1900), (10, -LN2, -80 * LN2), (11, 16, 0)):
         ts(co(j), co(0), float(f), float(o), OP.mult, OP.add, ["co0"], ["co%d" % j])
-    tc(co(9), T.wtb[:, 0:1], ["wtb"], ["co9"])
+    tc(co(7), T.wtb[:, 0:1], ["wtb"], ["co7"])
     tc(co(12), T.e16[:, 0:1], ["e16"], ["co12"])
     for b, n in CH.values():
-        ts(T.c16[:, b // 8:b // 8 + n // 16], T.ct[:, b // 16:(b + n) // 16], co(11), None, OP.add, None, ["co11", "ct"], ["+c16"])
-        ts(T.c16[:, b // 8 + n // 16:(b + n) // 8], T.ct[:, 0:n // 16], co(11), 4.0, OP.add, OP.mult, ["co11", "ct"], ["+c16"])
+        for j, (o, f) in enumerate(((b // 16, 1.0), (0, 4.0))):
+            c0 = (2 * b + j * n) // 16
+            ts(T.c16[:, c0:c0 + n // 16], T.ct[:, o:o + n // 16], co(11), f, OP.add, OP.mult, ["co11", "ct"], ["+c16"])
     b8 = SLOT["B1"] * 128
     tc(T.b8f[:], T.mats[:, b8:b8 + 113:16], ["B1"], ["b8f"])
-    for nm, src, f, r2 in (("wl", "bw8", co(9), "co9"), ("cl", "bc8", 4096.0, "b8f")):
+    for nm, src, f, r2 in (("wl", "bw8", co(7), "co7"), ("cl", "bc8", 4096.0, "b8f")):
         ts(T[src][:], T.b8f[:], f, None, OP.mult, None, ["b8f", r2], [src])
         for gi in range(8):
             col = T[src][:, gi:gi + 1]
@@ -314,9 +375,10 @@ def rank_program(g, core, T, topo):
         mat(nm, "B1", float(f))
     for d in (1, 2, 3, 4):
         mat("LE%d" % d, "LE", 512.0 * d)
+    mat("LEq", "LE", 256.0)
     for e in FIRST:
         mat("W%d" % e, "B1", T.sd[:, e:e + 1], ["sd"])
-    mat("BW", "B1", co(9), ["co9"])
+    mat("BW", "B1", co(7), ["co7"])
     mat("BR0", "B1", co(12), ["co12"]); mat("BR1", "B1", co(12), ["co12"])
     o = SLOT["BR1"] * 128
     ms(T.mats[:, o:o + 113:16], 0.0, ["BR1"])
@@ -327,12 +389,10 @@ def rank_program(g, core, T, topo):
         ms(M(nm), 0.0, [nm + "0"])
         for j, v in enumerate(vals):
             ms(T.mats[32 * j:32 * j + 1, SLOT[nm] * 128:SLOT[nm] * 128 + 128], float(v), ["+" + nm], [nm + "0"])
-    for nm, v in (("km1", -1.0), ("km6", -6.0), ("kmh", -0.5), ("kmx", -4096.0)):
+    for nm, v in (("km1", -1.0), ("kmh", -0.5), ("kmx", -34816.0)):
         ms(T[nm][:], v, [nm])
     ms(T.ac[:, 0:1], 0.0, ["ac0"])
     ms(T.msk[:], 0.0, ["mskz"])
-    for b, n in CH.values():
-        ms(T.vs[:, SIZE["vs"] * b // 64 + 64 * n + 14:SIZE["vs"] * b // 64 + 64 * n + 15], 0.0, ["+vz"])
 
     sends = []
 
@@ -369,18 +429,19 @@ def rank_program(g, core, T, topo):
             o = n * j + (512 - 64 * w) * (n // 128)
             return pd[:, o:o + n * w], lambda a, s: pd[:, o + 64 * w * s + a:o + 64 * w * (s + 1):w]
 
-        wx = lambda j, c=1: X("wx", n * j, n * (j + c))
+        wx = lambda j, c=1: X("wx", n * (j + 1), n * (j + 1 + c))
         win, y8, ppv = X("win", 0, n), X("y8"), X("pp", 1, 2 * n, 2)
 
         def gather(k, s):
-            o = X("zz", 4096 * s + k, 4096 * s + 4096, 4) if k < 4 else X("vs", 4096 * s + 19, 4096 * s + 4112, 4)
-            i, w = TAB.indirect(X("offs", 64 * s, 64 * s + 64)), g_("z%d%d" % (k, s))
-            gat[t, k, h, s] = len(nodes)
-            if "%d%s%d" % (k, h, s) in VG:
-                tc(o, i, ["x", "off" + h], w, 1.5)
-            else:
-                act(o, i, AF.Copy, ["x", "off" + h], w, 1.5)
+            for j in range(64 * s, 64 * s + 64, GW):
+                o, i, w = X("zz", 80 * j + k, 80 * (j + GW), 5), TAB.indirect(X("offs", j, j + GW)), ["+z%d%d%s" % (k, s, h)]
+                gat[t, k, h, s, j] = len(nodes)
+                flex(o, i, AF.Copy, ["x", "off" + h], w, None, GK)
+                if "%d%s%d" % (k, h, s) in VG[t]:
+                    nodes[-1][0].reverse()
+                nodes[-1] = nodes[-1][:3] + (("pin",),)
 
+        now[0] = "first" + h
         mm([lg, "s%d" % t], B_(7), (P_(7), [("I512", L), ("I101", L), ("I64", R[:, 512 + b:512 + b + n]), ("I", R[:, 768 + b:768 + b + n])]))
         ts(X("s32"), P_(7), T.ac[:, 4 * t:4 * t + 1], None, OP.add, None, B_(7) + ["ac%d" % t], g_("s32"))
         ts(X("r32"), X("s32"), 4095, None, OP.bitwise_and, None, g_("s32"), g_("r32"))
@@ -395,27 +456,34 @@ def rank_program(g, core, T, topo):
         pts = [X("pt", 2 * n * j + 1, 2 * n * (j + 1), 2) for j in range(3)] + [X("pt", 6 * n, 7 * n)]
         for j in range(3):
             cpy(X("pt", 2 * n * j, 2 * n * (j + 1) - 1, 2), L, [lg], g_("lp%d" % (j + 1)))
+        act(X("l2"), L, AF.Square, [lg], g_("l2"))
         act(X("w3"), L, AF.Sigmoid, [lg, "co10"], g_("w3"), scale=16 * LN2, bias=co(10))
 
         for k in range(4):
             kk = k + 1
+            now[0] = "place" + h
             if k < 3:
                 nw = NW[kk]
                 tab, col = table(8, nw)
                 MM([cg, "ON", "CL"] + ["W%d" % (kk + 2 * a) for a in range(nw)], B_(8, 8),
                    [(col(a, s), M("W%d" % (kk + 2 * a)), Cp(s), a == 0, False) for a in range(nw) for s in parts]
                    + [(col(nw - 1, s), M("CL"), ones(64), False, False) for s in parts])
+            if t == 2 and k == 1:
+                mm(["x"], B_(5), (P_(5), [("I", T.xt[:, 4096 + 16 * b + a:4096 + 16 * (b + n):16]) for a in range(16)]))
+                flex(T.ysb[:, b:b + n], P_(5), AF.Copy, B_(5), g_("ysb"), None)
             for s in parts:
                 gather(k, s)
                 mm(["wl", "ON"] + g_("z%d%d" % (k, s)), B_(0), (pd[:, 64 * s:64 * s + 64],
-                   [("CU", ones(64))] + [(WM("wl", m), X("zz", 4096 * s + 4 * m + k, 4096 * s + 4096, 64)) for m in range(16)]))
+                   [("CU", ones(64))] + [(WM("wl", m), X("zz", 5120 * s + 5 * m + k, 5120 * (s + 1), 80)) for m in range(16)]))
             tt(X("x32"), P_(0), y8, OP.mult, B_(0) + g_("y8"), g_("x32"))
             lin(P_(4), P_(0), 37.0, 3947.0, B_(0) + B_(4), g_("u37"))
+            only("u")
             tt(X("n32"), P_(0), X("c8" if k else "c8f"), OP.add, B_(0) + g_("c8"), g_("n32"))
             tt(X("r32"), X("x32"), P_(4), OP.add, B_(4) + g_("x32", "u37"), g_("r32"))
             ts(X("s32"), X("r32"), 4095, None, OP.bitwise_and, None, g_("r32"), g_("s32"))
             tc(X("offs"), X("s32"), g_("s32"), g_("off"))
             P, tp = pts[k], "p%d%s" % (kk, h)
+            now[0] = "pick" + h
             ts(X("nn"), X("n32"), 3, 3, OP.arith_shift_right, OP.bitwise_and, g_("n32"), g_("nn"))
             if k == 0:
                 ts(P, X("nn"), -6.0, None, OP.add, None, g_("nn"), [tp])
@@ -423,97 +491,109 @@ def rank_program(g, core, T, topo):
                 tt(P, X("nn"), P_(6), OP.add, B_(6) + g_("nn"), [tp])
             if k < 3:
                 mm([tp], B_(6), (P_(6), [("I", P)]))
-                ts(X("msk", 1, 2 * n, 2), P, co(kk), None, OP.is_ge, None, [tp, "co%d" % kk, "mskz"], g_("msk"), 0.5)
+                flex(X("msk", 1, 2 * n, 2), P, AF.Sigmoid, [tp, "co%d" % kk, "co%d" % (12 + kk), "mskz"], g_("msk"), (co(kk), None, OP.is_ge), 1, 0.5, scale=200.0, bias=co(12 + kk))
+                only("m")
                 scan(X("pp"), X("msk"), X("pt", 2 * n * k, 2 * n * kk), OP.mult, OP.add, [tp, "mskz"] + g_("msk", "lp%d" % kk), g_("pp"), 0.5)
                 MM(["K%d" % a for a in range(nw)] + g_("pp"), B_(8, 8),
                    [(col(a, s), M("K%d" % a), X("pp", 128 * s + 1, 128 * s + 128, 2), False, a == nw - 1) for a in range(nw) for s in parts])
                 lin(X("rr"), ppv, 0.5, 194.75, g_("pp"), g_("rr"), 0.5)
+                only("r")
                 mm(["ON"] + g_("pp", "rr"), B_(5), (P_(5), [("CF", ones(n)), ("mI256", ppv), ("Ih", ppv), ("I512", X("rr")), ("mI", X("rr"))]))
                 scan(X("sc", 0, n * nw), T["q%d" % nw][:, 0:n * nw], tab, OP.add, OP.max, B_(8, 8) + ["q%d" % nw], g_("sc"))
                 tt(X("xi"), P_(5), X("sc", nw - 1, n * nw, nw), OP.mult, B_(5) + g_("sc"), g_("xi"))
                 ts(X("c8"), X("xi"), 2044, None, OP.bitwise_and, None, g_("xi"), g_("c8"))
                 ts(y8, X("c8"), 0.03125, -0.75, OP.mult, OP.add, g_("c8"), g_("y8"))
-        v1 = g_(*["v1%d" % j for j in range(n // SW)])
-        for j in range(n // SW):
-            o, s = 64 * SW * j, SW * j // 64
-            scan(X("vs", 14 + o, 14 + o + 64 * SW), T.mk4[:, 0:64 * SW], X("zz", o, o + 64 * SW), OP.min, OP.max,
-                 ["mk40"] + g_(*["z%d%d" % (k, s) for k in range(4)]), [v1[j]] + g_(*{"z4%d" % s, "z4%d" % (max(SW * j - 1, 0) // 64)}), 0.5)
-        cpy(X("zz", 0, 64 * n, 64), F, ["ff" + h] + v1, g_("fs"))
+        now[0] = "four" + h
+        vt = g_(*["vt%d" % s for s in parts])
         bk = lambda s: ["#%s%d" % (h, x) for x in ((2, 3) if n == 128 and s == 0 else (0, 1))]
         vf = lambda s, m, c=1: pd[:, 1024 * (n == 128 and s == 0) + 64 * m:1024 * (n == 128 and s == 0) + 64 * (m + c)]
         for s in parts:
             MM(["mI", "ff" + h], bk(s), [(vf(s, m), M("mI"), T.ff[:, b + 64 * s:b + 64 * s + 64], m % 8 == 0, False) for m in range(16)])
             gather(4, s)
         yield
+        now[0] = "fail" + h
         for s in parts:
-            for o in (4096 * s, 4096 * s + 2048):
-                scan(X("zz", o + 1, o + 2048, 2), T.mk4[:, 0:2048:2], X("vs", o + 17, o + 2064, 2), OP.min, OP.max,
-                     ["mk40"] + v1 + g_("z4%d" % s), ["+vt%d%s" % (s, h)], 0.5)
-            MM(["I"] + g_("vt%d" % s), bk(s), [(vf(s, m), M("I"), X("zz", 4096 * s + 4 * m + 3, 4096 * s + 4096, 64), False, m % 8 == 7) for m in range(16)])
-            act(X("gg", 1024 * s, 1024 * s + 1024), vf(s, 0, 16), AF.Sign, bk(s), g_("gg%d" % s), bias=0.5)
+            for o in range(5120 * s, 5120 * (s + 1), 80 * S5):
+                scan(X("vs", o, o + 80 * S5), T.mk5[:, 0:80 * S5], X("zz", o, o + 80 * S5), OP.min, OP.max,
+                     ["mk50"] + g_(*["z%d%d" % (k, s) for k in range(5)]), ["+" + vt[s], "+fs" + h], 0.5)
+            for j in (0, 1):
+                MM(["I", vt[s]], [bk(s)[j]], [(vf(s, m), M("I"), X("vs", 5120 * s + 5 * m + 4, 5120 * (s + 1), 80), False, m % 8 == 7) for m in range(8 * j, 8 * j + 8)])
+                flex(X("gg", 1024 * s + 512 * j, 1024 * s + 512 * j + 512), vf(s, 8 * j, 8), AF.Sigmoid, [bk(s)[j]], g_("gg%d%d" % (s, j)), (0.0, None, OP.is_ge), scale=200.0, bias=100.0)
+        cpy(X("vs", 0, 80 * n, 80), F, ["ff" + h] + vt, g_("fs"))
         o = n * 8
         for s in parts:
-            mm(["cl", "kmx"] + g_("gg%d" % s, "w3"), B_(8), (pd[:, o + 128 * s + 1:o + 128 * s + 128:2], [("I", X("w3", 64 * s, 64 * s + 64))]),
-               (pd[:, o + 128 * s:o + 128 * s + 128:2], [("I", T.kmx[:, 0:64])] + [(WM("cl", m), X("gg", 1024 * s + 64 * m, 1024 * s + 64 * m + 64)) for m in range(16)]))
+            it = grp(pd[:, o + 128 * s + 1:o + 128 * s + 128:2], [("I", X("w3", 64 * s, 64 * s + 64))])
+            it += grp(pd[:, o + 128 * s:o + 128 * s + 128:2], [("I", T.kmx[:, 0:64])] + [(WM("cl", m), X("gg", 1024 * s + 64 * m, 1024 * s + 64 * m + 64)) for m in range(16)])
+            MM(["cl", "kmx", "I"] + g_("gg%d0" % s, "w3"), B_(8), it[:10])
+            MM(g_("gg%d1" % s), B_(8), it[10:])
         scan(X("fw"), T.q2[:, 0:2 * n], P_(8, 2), OP.max, OP.min, B_(8) + ["q2"], g_("fw"))
         fw = X("fw", 1, 2 * n, 2)
-        mm(g_("fw"), B_(8), (P_(10), [("BH", fw)]))
+        w0 = 0 if n == 128 else 12
+        MM(["BH", "I", lg] + g_("fw", "l2"), B_(8), grp(P_(10), [("BH", fw)]) + [(P_(8), M("I"), X("l2"), True, False), (P_(9), M("I"), L, False, False)])
+        MM(["I"] + g_("p1", "p2", "p3", "p4"), B_(w0), [(P_(w0 + j), M("I"), pts[j], j == 0 and n == 128, False) for j in range(4)])
         tt(win, fw, P_(10), OP.is_gt, B_(8) + g_("fw"), g_("win"))
         if b + n == 256 and t < 2:
-            mm(["win" + x for x in CH], B_(12), (pd[:, 12 * n:12 * n + 64], [("ON", T.win[:, 2 * x + 64 * s:2 * x + 64 * s + 64]) for x, y in CH.values() for s in range(y // 64)]))
-            act(T.junk[:, 0:64], pd[:, 12 * n:12 * n + 64], AF.Copy, B_(12), ["f64", "f32", "ac%d" % (t + 1)], accum_out=T.ac[:, 4 * t + 4:4 * t + 5])
+            j = 12 if n == 128 else 6
+            mm(["win" + x for x in CH], B_(j), (pd[:, j * n:j * n + 64], [("ON", T.win[:, 2 * x + 64 * s:2 * x + 64 * s + 64]) for x, y in CH.values() for s in range(y // 64)]))
+            act(T.junk[:, 0:64], pd[:, j * n:j * n + 64], AF.Copy, B_(j), ["f64", "f32", "ac%d" % (t + 1)], accum_out=T.ac[:, 4 * t + 4:4 * t + 5])
         e = n // 16
-        pk, po, ph = (pd[:, 4 * n + e * j:4 * n + e * (j + 1)] for j in range(3))
-        ts(X("win", n, 2 * n), win, co(8), None, OP.mult, None, g_("win") + ["co8"], g_("wo"), 0.5)
-        mm(["cl", "c16"] + g_("win", "wo"), B_(4), (pd[:, 4 * n:4 * n + 2 * e], [("I", T.c16[:, b // 8:(b + n) // 8])] + [(WM("cl", a), X("win", a, 2 * n, 16)) for a in range(16)]))
+        now[0] = "table" + h
+        pk, po, ph, c0 = *(pd[:, 4 * n + e * j:4 * n + e * (j + 1)] for j in range(3)), b // 8
+        flex(X("win", n, 2 * n), win, AF.Copy, g_("win") + ["co8"], g_("wo"), (co(8), None, OP.mult), 1, 0.5, scale=co(8))
+        it = grp(pd[:, 4 * n:4 * n + 2 * e], [("I", T.c16[:, c0:c0 + 2 * e])] + [(WM("cl", a), X("win", a, 2 * n, 16)) for a in range(16)])
+        MM(["cl", "c16", "I", "Iq"] + g_("win", "wo"), B_(4), it[:1] + [(po, M("Iq"), T.c16[:, c0 + e:c0 + 2 * e], False, False)] + it[1:])
         tc(X("ofs"), po, B_(4), g_("ofs"))
-        flex(X("vsel"), X("zz").indirect(X("ofs")), AF.Copy, g_("ofs", "fs", *["vt%d" % s for s in parts]), g_("vsel"), None, 1.5)
+        flex(X("vsel"), X("vs").indirect(X("ofs")), AF.Copy, g_("ofs", "fs") + vt, g_("vsel"), None, 1.5)
+        flex(X("z4"), X("zz").indirect(X("ofs")), AF.Copy, g_("ofs") + zt(4), g_("zw"), None, 1.5)
         mm(["wl"] + g_("vsel"), B_(4), (ph, [(WM("wl", a), X("vsel", a, n, 16)) for a in range(16)]))
         tc(X("q32"), ph, B_(4), g_("q32"))
         ts(X("o32"), X("q32"), 15, None, OP.bitwise_and, None, g_("q32"), g_("o32"))
-        tt(X("q32"), X("o32"), pk, OP.add, B_(4) + g_("o32"), g_("q32"))
-        tc(X("of2"), X("q32"), g_("q32"), g_("of2"))
-        vop("tc", cv(n, 4), g_("of2", "vsel"), ["x"], T.xt[:].indirect(X("of2")), X("vsel"))
-        w0 = 0 if n == 128 else 12
-        relu = dict(v=(-26.0, 0.0, OP.add, OP.max), bias=-26.0)
-        mm([lg, "km6"] + g_("win"), B_(11), (P_(11), [("I", L), ("I", T.km6[:, 0:n]), ("I32", win)]))
-        mm(g_("win", "p1", "p2", "p3", "p4"), B_(w0), *[(P_(w0 + j), [("I", pts[j]), ("I32", win)]) for j in range(4)])
-        if n == 128:
-            flex(wx(0), P_(11), AF.Relu, B_(11), g_("wx0"), **relu)
-            flex(wx(1, 4), P_(0, 4), AF.Relu, B_(0), g_("wx"), **relu)
+        if t < 2:
+            tt(X("q32"), X("o32"), pk, OP.add, B_(4) + g_("o32"), g_("q32"))
+            tc(X("of2"), X("q32"), g_("q32"), g_("of2"))
+            vop("tc", cv(n, 4), g_("of2", "vsel"), ["x"], T.xt[:].indirect(X("of2")), X("vsel"))
         else:
-            flex(X("wx"), P_(11, 5), AF.Relu, B_(11), g_("wx0", "wx"), **relu)
+            tt(X("q32"), X("o32"), T.c16[:, c0:c0 + e], OP.add, ["c16"] + g_("o32"), g_("q32"))
+            tc(X("of2"), X("q32"), g_("q32"), g_("of2"))
+            flex(X("sel"), TAB.indirect(X("of2")), AF.Copy, ["x"] + g_("of2"), g_("sel"), None, 1.5)
+            mm(g_("win"), B_(5), (P_(5), [("B1", win)]))
+            flex(X("ax0"), P_(5), AF.Copy, B_(5), g_("ax0"), None)
+            mm(g_("vsel", "sel"), B_(5), (P_(5), [("I", X("vsel")), ("mI", X("sel"))]))
+            tt(X("c8f"), P_(5), X("ax0"), OP.mult, B_(5) + g_("ax0"), g_("c8"))
+            tt(T.ysb[:, b:b + n], T.ysb[:, b:b + n], X("c8f"), OP.add, g_("c8", "ysb"), g_("ysb"), 2)
+        now[0] = "spans" + h
+        MM(["I32"] + g_("win"), B_(8), [(P_(8 + j), M("I32"), win, False, j == 1 and n == 128) for j in (0, 1)])
+        MM(["I32"] + g_("win"), B_(w0), [(P_(w0 + j), M("I32"), win, False, j == 3) for j in range(4)])
+        flex(wx(-1, 2), P_(8, 2), AF.Relu, B_(8), g_("wx0"), (-32.0, 0.0, OP.add, OP.max), bias=-32.0)
+        flex(wx(1, 4), P_(w0, 4), AF.Relu, B_(w0), g_("wx"), (-26.0, 0.0, OP.add, OP.max), bias=-26.0)
         y0, l0 = (0, 8) if n == 128 else (8, 0)
         mm(g_("wx", "win"), B_(y0), *[(P_(y0 + j - 1), [("B1", wx(j)), (("B1", "BX2", "BX3", "BX32")[j - 1], win)]) for j in (1, 2, 3, 4)])
         act(X("ax"), P_(y0, 3), AF.Abs, B_(y0) + ["co5"], g_("ax"), bias=co(5))
         ts(P_(7), P_(y0 + 3), co(4), None, OP.is_equal, None, B_(y0) + B_(7) + ["co4"], g_("m4"))
         tab, col = table(l0, 5)
         xq = l0 if n == 128 else 5
-        mm([cg] + g_("wx0"), B_(l0, 8), (P_(xq), [("LE", wx(0))]),
-           *[(col(4 - d, s), [("S%d" % d if d else "I", Cp(s))] + ([("LE%d" % d, X("wx", 64 * s, 64 * s + 64))] if d else [])) for d in range(5) for s in parts])
+        mm([cg] + g_("wx0"), B_(l0, 8), (P_(xq), [("LEq", wx(-1))]),
+           *[(col(4 - d, s), [("S%d" % d if d else "I", Cp(s))] + ([("LE%d" % d, X("wx", n + 64 * s, n + 64 * s + 64))] if d else [])) for d in range(5) for s in parts])
         scan(X("sn"), T.q5[:, 0:5 * n], tab, OP.add, OP.max, B_(l0, 8) + ["q5"], g_("sn"))
-        act(P_(xq), P_(xq), AF.Square, B_(xq), g_("sq"), scale=16.0)
         nc, nl = "nc%d%s" % (t, h), "nl%d%s" % (t, h)
-        tt(NC, X("sn", 4, 5 * n, 5), P_(xq), OP.subtract, B_(xq) + g_("sn", "sq"), [nc])
+        tt(NC, X("sn", 4, 5 * n, 5), P_(xq), OP.subtract, B_(xq) + g_("sn"), [nc])
         if t < 2:
             send(("c" + h, t + 1), NC, [nc])
         e0 = 0 if n == 128 else 12
         mm([lg, "km1"] + g_("wx", "ax", "win"), B_(e0), *([(P_(e0 + j - 1), [("B1", wx(j + 1)), ("mB1", wx(j)), ("mI4", X("ax", n * j - n, n * j))]) for j in (1, 2, 3)]
                                                           + [(P_(e0 + 3), [("I", L), ("mB8", win), ("I", T.km1[:, 0:n])])]))
         flex(X("ex"), P_(e0, 4), AF.Relu, B_(e0), g_("ex"), (0.0, None, OP.max))
-        flex(X("z4"), X("vs", 16, 16 + 64 * n).indirect(X("ofs")), AF.Copy, ["vz"] + g_("ofs") + zt(4) + v1, g_("zw"), None, 1.5)
         tt(X("t4"), NC, P_(7), OP.mult, [nc] + B_(7) + g_("m4"), g_("t4"))
         n0 = 12 if n == 128 else 0
         mm(g_("zw", "t4"), B_(n0), (P_(n0), [("BW", X("z4")), ("B8", X("t4"))]))
         tc(X("n4"), P_(n0), B_(n0), g_("n4"))
         ts(X("n5"), X("n4"), 3, 3, OP.arith_shift_right, OP.bitwise_and, g_("n4"), g_("n5"))
         tt(X("n4m"), X("n5"), P_(7), OP.mult, B_(7) + g_("n5", "m4"), g_("n4m"))
-        it = grp(P_(y0), [("BQ0", wx(1))] + [("I", X("ex", n * j, n * j + n)) for j in range(4)] + [("I", X("n4m"))])
-        MM(["BQ0", "I"] + g_("wx", "ex"), B_(y0), it[:-1])
-        MM(g_("n4m"), B_(y0), it[-1:])
-        lin(NL, P_(y0), 1.0, 1.0, B_(y0), [nl])
+        mm(["km1"] + g_("wx", "ex"), B_(y0), (P_(y0), [("BQ0", wx(1)), ("mI", T.km1[:, 0:n])] + [("I", X("ex", n * j, n * j + n)) for j in range(4)]))
+        tt(NL, X("n4m"), P_(y0), OP.add, B_(y0) + g_("n4m"), [nl])
         if t < 2:
             send(("l" + h, t + 1), NL, [nl])
+        now[0] = "end"
         mm(["kmh", "ff" + h] + g_("vsel"), B_(6), (P_(6), [("I", F), ("I", X("vsel")), ("I", T.kmh[:, 0:n])]))
         lin(X("f1"), P_(6), 0.5, 12582912.0, B_(6), g_("f1"))
         lin(F, X("f1"), 1.0, -12582912.0, g_("f1"), ["ff" + h])
@@ -523,22 +603,19 @@ def rank_program(g, core, T, topo):
             send(("s", 2), T.rec1[:, 512:1024], ["s1"])
         for part in [stream(t, h) for h in CH] * 2:
             next(part, None)
-    for j in (0, 1):
-        o = T.pda[:, 512 * j:512 * j + 128]
-        mm(["x"], ["#a%d" % j], (o, [("I", T.xt[:, 4096 + 2048 * j + a:6144 + 2048 * j:16]) for a in range(16)]))
-        flex(T.ysb[:, 128 * j:128 * j + 128], o, AF.Copy, ["#a%d" % j], ["ysb%d" % j], None)
     dma("y", "o_c", T.yc[:], T.nr2[:, 0:256], ["nc2" + h for h in CH], [])
     dma("y", "o_l", T.yl[:], T.nr2[:, 256:512], ["nl2" + h for h in CH], [])
     dma("y", "o_f", T.yf[:], T.ff[:], ["ff" + h for h in CH], [])
-    dma("y", "o_s", T.ys[:], T.ysb[:], ["ysb0", "ysb1"], [])
+    dma("y", "o_s", T.ys[:], T.ysb[:], ["ysb" + h for h in CH], [])
 
     Q = {"v": g.vector, "s": g.scalar, "t": g.tensor, "g": g, "y": g.sync}
     cnt = {"v": 0, "s": 0, "t": 0, "g": 0}
     known = {q: {} for q in Q}
     lw, rd, bank = {}, {}, {}
     if not KEEP:
-        turn = sorted((t, k + LAG[h], -k, h, s, j) for (t, k, h, s), j in gat.items() if "%d%s%d" % (k, h, s) not in VG)
-        KEEP.append(order([(n[0], n[1], n[2], n[3][0]) for n in nodes], [(x[-1], y[-1]) for x, y in zip(turn, turn[1:])]))
+        turn = sorted((t, k + LAG[h][t] + (LAG[h][t + 1] - LAG[h][t]) * k / 4, -k, h, i, j) for (t, k, h, s, i), j in gat.items() if "%d%s%d" % (k, h, s) not in VG[t])
+        KEEP.append(order([(n[0], n[1], n[2], n[3][0]) for n in nodes], [(x[-1], y[-1]) for x, y in zip(turn, turn[1:])],
+                          [AHEAD.get(x, 0) for x in parts_of], parts_of))
     for _, j, a in KEEP[0]:
         (q, _, f), (_, r, w, kind) = nodes[j][0][a], nodes[j]
         if kind[0] == "arr":

@@ -8,7 +8,7 @@ DIAG = {"I": 1, "mI": -1, "I512": 512, "I101": 101, "I64": 64, "I32": 32, "mI4":
 DIAG.update({"K%d" % a: (4 * a - 11) * 2048 for a in range(7)})
 BLOCK = {"mB1": -1, "mB8": -8, "BH": 0.5, "B8": 8, "BX32": 32, "BX2": 2, "BX3": 3}
 ROWS = {"CU": (-32768, 4, 2.0 ** -9), "CL": (2048, 56, 7 / 64), "CF": (-98304, -1024, -61)}
-SLOTS = ["B1", "ON", "LE", "LEq", "S1", "S2", "S3", "S4", "BW", "BQ0", "BR0", "BR1"] + list(DIAG) + list(BLOCK) + list(ROWS)
+SLOTS = ["M2", "M3", "B1", "ON", "LE", "LEq", "S1", "S2", "S3", "S4", "BW", "BQ0", "BR0", "BR1"] + list(DIAG) + list(BLOCK) + list(ROWS)
 SLOTS += ["W%d" % e for e in FIRST] + ["LE%d" % d for d in (1, 2, 3, 4)]
 SLOT = {n: j for j, n in enumerate(SLOTS)}
 BUF = {"bfloat16": "xt_8192 mk5_2560 wl_2064 cl_2064 ff_256 wtb_16 onef_16 e16_16 tmpm_128 km1_128 kmh_128 kmx_128 q2_256 junk_128 c16_32",
@@ -19,13 +19,12 @@ SIZE = {s.split("_")[0]: int(s.split("_")[1]) for names in BUFH.values() for s i
 LAG = {"a": (0, 0, 0, 0), "b": (0.5, 0.5, 0.5, 0.5)}
 VG = ["0a1", "0b0", "0b0"]
 S5 = 32
-GW = 64
 ONS = ""
 AHEAD = {}
-TRIES, SHIFT, FS, GK = 7000, 400, 60, 1.62
+TRIES, SHIFT, FS, GK = 8000, 300, 72, 1.65
 BIAS, PASSES = 0.3, 8
-ARR, MMF, PEC, CYC, FV, SAME, CROSS = 3300, 4, 0.36, 0.85, 30, 140, 230
-NOISE, SCALES = 300, [{}, {"n": 1.8}, {"v": 1.1}, {"s": 1.1, "t": 1.2}]
+ARR, MMF, PEC, CYC, FV, SAME, CROSS = 4300, 3.5, 0.38, 0.84, 24, 150, 225
+NOISE, SCALES = 310, [{}, {"n": 1.7, "s": 1.15}, {"s": 0.8}, {"t": 1.15, "v": 1.08}]
 
 
 def _bufs():
@@ -181,8 +180,8 @@ def order(nodes, after, ahead, names):
     e, seq, held = best[0], best[1], []
     for i in range(TRIES):
         if not held:
-            for s in SCALES:
-                replay(seq, s, held)
+            first = replay(seq, SCALES[0], held)
+            replay(seq, SCALES[1 + i % (len(SCALES) - 1)], held)
             at = {c[1]: k for k, c in enumerate(seq)}
         x, y = held[int(rng.integers(len(held)))]
         j, k, move = seq[x][1], seq[y][1], int(rng.integers(4))
@@ -203,7 +202,10 @@ def order(nodes, after, ahead, names):
             new = seq[:z] + [(seq[z][0], seq[z][1], 1 - seq[z][2])] + seq[z + 1:]
         else:
             continue
-        f = sum(replay(new, s) for s in SCALES)
+        f = replay(new, SCALES[0])
+        if f > first + SHIFT:
+            continue
+        f += sum(replay(new, s) for s in SCALES[1:])
         if f <= e + SHIFT * (1 - i / TRIES):
             e, seq, held = f, new, []
             if e < best[0]:
@@ -318,7 +320,8 @@ def rank_program(g, core, T, topo):
     dma("y", "ld_x", TAB, T.x[:], [], ["x"], 8000)
     dma("s", "ld_ch", T.rec0[:, 0:256], T.ch[:], [], ["c0" + h for h in CH])
     dma("s", "ld_fl", T.ff[:], T.fl[:], [], ["ff" + h for h in CH])
-    ms(M("ON"), 1.0, ["ON"]); ms(T.onef[:], 1.0, ["onef"]); ms(T.wl[:], 0.0, ["wl0"]); ms(T.cl[:], 0.0, ["cl0"])
+    ms(M("ON"), 1.0, ["ON"]); ms(T.onef[:], 1.0, ["onef"]); ms(T.wl[:], 0.0, ["wl0"])
+    fill("cl", [[0, 2064]], 0, 2064); fill("msk", [[0, 512]], 0, 512)
     fill("mk5", [[0, 512], [256, 5]], 0, 2560)
     for k in (4, 6, 7):
         fill("q%d" % k, [[0, 128], [16384, k]], -26 * 2048, 128 * k)
@@ -345,7 +348,7 @@ def rank_program(g, core, T, topo):
     tt(T.jt[:], T.e16[:], T.jio[:], OP.mult, ["e16", "jio"], ["jt"])
     co = lambda j: T.co[:, j:j + 1]
     vop("tr", 120, ["jt"], ["co0"], co(0), T.jt[:], AxisListType.X, OP.add)
-    for j, f, o in ((1, 1, -7), (2, 1, -8), (3, 1, -9), (4, 1, 28), (5, -1, 0), (8, 5 / 4096, 4 / 4096), (13, -200, 1500), (14, -200, 1700), (15, -200, 1900), (10, -LN2, -80 * LN2), (11, 16, 0)):
+    for j, f, o in ((1, 1, -1), (2, 1, -8), (3, 1, -9), (4, 1, 28), (5, -1, 0), (8, 5 / 4096, 4 / 4096), (10, -LN2, -80 * LN2), (11, 16, 0)):
         ts(co(j), co(0), float(f), float(o), OP.mult, OP.add, ["co0"], ["co%d" % j])
     tc(co(7), T.wtb[:, 0:1], ["wtb"], ["co7"])
     tc(co(12), T.e16[:, 0:1], ["e16"], ["co12"])
@@ -369,8 +372,11 @@ def rank_program(g, core, T, topo):
         flex(M(dst), M(src), AF.Copy, [src] + list(r2), [dst], (f, None, OP.mult), 1, 0.5, scale=f)
 
     for nm, f in DIAG.items():
-        if nm != "I":
+        if nm != "I" and nm[0] != "K":
             mat(nm, "I", float(f))
+    ko = T.mats[:, SLOT["K0"] * 128:SLOT["K6"] * 128 + 128]
+    add([("g", 1700, lambda: g.iota(ko, [[8192, 7], [0, 128]], -11 * 2048, 0, allow_small_or_imprecise_dtypes=True))], [], ["K"])
+    add([("g", 1700, lambda: g.affine_select(ko, ko, [[0, 7], [-1, 128]], OP.is_equal, 0.0, 0, 1))], [], ["K"] + ["K%d" % a for a in range(7)])
     for nm, f in BLOCK.items():
         mat(nm, "B1", float(f))
     for d in (1, 2, 3, 4):
@@ -378,7 +384,7 @@ def rank_program(g, core, T, topo):
     mat("LEq", "LE", 256.0)
     for e in FIRST:
         mat("W%d" % e, "B1", T.sd[:, e:e + 1], ["sd"])
-    mat("BW", "B1", co(7), ["co7"])
+    mat("BW", "B1", co(7), ["co7"]); mat("M2", "I", co(2), ["co2"]); mat("M3", "I", co(3), ["co3"])
     mat("BR0", "B1", co(12), ["co12"]); mat("BR1", "B1", co(12), ["co12"])
     o = SLOT["BR1"] * 128
     ms(T.mats[:, o:o + 113:16], 0.0, ["BR1"])
@@ -392,14 +398,13 @@ def rank_program(g, core, T, topo):
     for nm, v in (("km1", -1.0), ("kmh", -0.5), ("kmx", -34816.0)):
         ms(T[nm][:], v, [nm])
     ms(T.ac[:, 0:1], 0.0, ["ac0"])
-    ms(T.msk[:], 0.0, ["mskz"])
 
     sends = []
 
     def send(msg, ap, tags):
         def f():
             sends.append(("b_%s%d" % msg, put(msg, ap, via(msg, core, nxt, topo) or nxt)))
-        add([("g", 1500, f)], tags, ["sent%s%d" % msg], ("send",))
+        add([("g", 700, f)], tags, ["sent%s%d" % msg], ("send",))
         add([("n", ARR, None)], ["sent%s%d" % msg], ["%s%d%s" % (msg[0][0], msg[1], msg[0][1:])],
             ("arr", "a_%s%d" % msg, nbits(topo.mask(via(msg, prv, core, topo) or prv, core))))
 
@@ -433,8 +438,9 @@ def rank_program(g, core, T, topo):
         win, y8, ppv = X("win", 0, n), X("y8"), X("pp", 1, 2 * n, 2)
 
         def gather(k, s):
-            for j in range(64 * s, 64 * s + 64, GW):
-                o, i, w = X("zz", 80 * j + k, 80 * (j + GW), 5), TAB.indirect(X("offs", j, j + GW)), ["+z%d%d%s" % (k, s, h)]
+            gw = 64 if k < 4 else 32
+            for j in range(64 * s, 64 * s + 64, gw):
+                o, i, w = X("zz", 80 * j + k, 80 * (j + gw), 5), TAB.indirect(X("offs", j, j + gw)), ["+z%d%d%s" % (k, s, h)] + g_("y%d" % (j // 32))[:k // 4]
                 gat[t, k, h, s, j] = len(nodes)
                 flex(o, i, AF.Copy, ["x", "off" + h], w, None, GK)
                 if "%d%s%d" % (k, h, s) in VG[t]:
@@ -487,13 +493,18 @@ def rank_program(g, core, T, topo):
             ts(X("nn"), X("n32"), 3, 3, OP.arith_shift_right, OP.bitwise_and, g_("n32"), g_("nn"))
             if k == 0:
                 ts(P, X("nn"), -6.0, None, OP.add, None, g_("nn"), [tp])
-            else:
+            elif k < 3:
                 tt(P, X("nn"), P_(6), OP.add, B_(6) + g_("nn"), [tp])
+            else:
+                tt(P, X("nn"), pts[2], OP.add, g_("nn", "p3"), [tp], 2)
             if k < 3:
-                mm([tp], B_(6), (P_(6), [("I", P)]))
-                flex(X("msk", 1, 2 * n, 2), P, AF.Sigmoid, [tp, "co%d" % kk, "co%d" % (12 + kk), "mskz"], g_("msk"), (co(kk), None, OP.is_ge), 1, 0.5, scale=200.0, bias=co(12 + kk))
-                only("m")
-                scan(X("pp"), X("msk"), X("pt", 2 * n * k, 2 * n * kk), OP.mult, OP.add, [tp, "mskz"] + g_("msk", "lp%d" % kk), g_("pp"), 0.5)
+                if k:
+                    tt(X("msk", 1, 2 * n, 2), X("nn"), P_(7), OP.is_ge, B_(7) + g_("nn") + ["msk0"], g_("msk"))
+                else:
+                    ts(X("msk", 1, 2 * n, 2), X("nn"), co(1), None, OP.is_ge, None, g_("nn") + ["co1", "msk0"], g_("msk"))
+                scan(X("pp"), X("msk"), X("pt", 2 * n * k, 2 * n * kk), OP.mult, OP.add, [tp, "msk0"] + g_("msk", "lp%d" % kk), g_("pp"), 0.5)
+                if k < 2:
+                    mm([tp, "ON"], B_(6), (P_(6), [("I", P)]), (P_(7), [("mI", P), ("M%d" % (kk + 1), ones(n))]))
                 MM(["K%d" % a for a in range(nw)] + g_("pp"), B_(8, 8),
                    [(col(a, s), M("K%d" % a), X("pp", 128 * s + 1, 128 * s + 128, 2), False, a == nw - 1) for a in range(nw) for s in parts])
                 lin(X("rr"), ppv, 0.5, 194.75, g_("pp"), g_("rr"), 0.5)
@@ -515,7 +526,7 @@ def rank_program(g, core, T, topo):
         for s in parts:
             for o in range(5120 * s, 5120 * (s + 1), 80 * S5):
                 scan(X("vs", o, o + 80 * S5), T.mk5[:, 0:80 * S5], X("zz", o, o + 80 * S5), OP.min, OP.max,
-                     ["mk50"] + g_(*["z%d%d" % (k, s) for k in range(5)]), ["+" + vt[s], "+fs" + h], 0.5)
+                     ["mk50"] + g_("y%d" % (o // 2560), *["z%d%d" % (k, s) for k in range(4)]), ["+" + vt[s], "+fs" + h], 0.5)
             for j in (0, 1):
                 MM(["I", vt[s]], [bk(s)[j]], [(vf(s, m), M("I"), X("vs", 5120 * s + 5 * m + 4, 5120 * (s + 1), 80), False, m % 8 == 7) for m in range(8 * j, 8 * j + 8)])
                 flex(X("gg", 1024 * s + 512 * j, 1024 * s + 512 * j + 512), vf(s, 8 * j, 8), AF.Sigmoid, [bk(s)[j]], g_("gg%d%d" % (s, j)), (0.0, None, OP.is_ge), scale=200.0, bias=100.0)
@@ -532,10 +543,6 @@ def rank_program(g, core, T, topo):
         MM(["BH", "I", lg] + g_("fw", "l2"), B_(8), grp(P_(10), [("BH", fw)]) + [(P_(8), M("I"), X("l2"), True, False), (P_(9), M("I"), L, False, False)])
         MM(["I"] + g_("p1", "p2", "p3", "p4"), B_(w0), [(P_(w0 + j), M("I"), pts[j], j == 0 and n == 128, False) for j in range(4)])
         tt(win, fw, P_(10), OP.is_gt, B_(8) + g_("fw"), g_("win"))
-        if b + n == 256 and t < 2:
-            j = 12 if n == 128 else 6
-            mm(["win" + x for x in CH], B_(j), (pd[:, j * n:j * n + 64], [("ON", T.win[:, 2 * x + 64 * s:2 * x + 64 * s + 64]) for x, y in CH.values() for s in range(y // 64)]))
-            act(T.junk[:, 0:64], pd[:, j * n:j * n + 64], AF.Copy, B_(j), ["f64", "f32", "ac%d" % (t + 1)], accum_out=T.ac[:, 4 * t + 4:4 * t + 5])
         e = n // 16
         now[0] = "table" + h
         pk, po, ph, c0 = *(pd[:, 4 * n + e * j:4 * n + e * (j + 1)] for j in range(3)), b // 8
@@ -543,6 +550,11 @@ def rank_program(g, core, T, topo):
         it = grp(pd[:, 4 * n:4 * n + 2 * e], [("I", T.c16[:, c0:c0 + 2 * e])] + [(WM("cl", a), X("win", a, 2 * n, 16)) for a in range(16)])
         MM(["cl", "c16", "I", "Iq"] + g_("win", "wo"), B_(4), it[:1] + [(po, M("Iq"), T.c16[:, c0 + e:c0 + 2 * e], False, False)] + it[1:])
         tc(X("ofs"), po, B_(4), g_("ofs"))
+        mm([lg] + g_("win"), B_(7), (P_(7), [("I", L), ("mB8", win)]))
+        flex(X("ex", 3 * n, 4 * n), P_(7), AF.Relu, B_(7), g_("ex3"), (-1.0, 0.0, OP.add, OP.max), bias=-1.0)
+        if b + n == 256 and t < 2:
+            mm(["win" + x for x in CH], B_(5), (pd[:, 5 * n:5 * n + 64], [("ON", T.win[:, 2 * x + 64 * s:2 * x + 64 * s + 64]) for x, y in CH.values() for s in range(y // 64)]))
+            act(T.junk[:, 0:64], pd[:, 5 * n:5 * n + 64], AF.Copy, B_(5), ["f64", "f32", "ac%d" % (t + 1)], accum_out=T.ac[:, 4 * t + 4:4 * t + 5])
         flex(X("vsel"), X("vs").indirect(X("ofs")), AF.Copy, g_("ofs", "fs") + vt, g_("vsel"), None, 1.5)
         flex(X("z4"), X("zz").indirect(X("ofs")), AF.Copy, g_("ofs") + zt(4), g_("zw"), None, 1.5)
         mm(["wl"] + g_("vsel"), B_(4), (ph, [(WM("wl", a), X("vsel", a, n, 16)) for a in range(16)]))
@@ -567,29 +579,29 @@ def rank_program(g, core, T, topo):
         flex(wx(-1, 2), P_(8, 2), AF.Relu, B_(8), g_("wx0"), (-32.0, 0.0, OP.add, OP.max), bias=-32.0)
         flex(wx(1, 4), P_(w0, 4), AF.Relu, B_(w0), g_("wx"), (-26.0, 0.0, OP.add, OP.max), bias=-26.0)
         y0, l0 = (0, 8) if n == 128 else (8, 0)
-        mm(g_("wx", "win"), B_(y0), *[(P_(y0 + j - 1), [("B1", wx(j)), (("B1", "BX2", "BX3", "BX32")[j - 1], win)]) for j in (1, 2, 3, 4)])
+        mm(g_("wx", "win"), B_(y0), *[(P_(y0 + j - 1), [("B1", wx(j)), (("B1", "BX2", "BX3")[j - 1], win)]) for j in (1, 2, 3)])
         act(X("ax"), P_(y0, 3), AF.Abs, B_(y0) + ["co5"], g_("ax"), bias=co(5))
-        ts(P_(7), P_(y0 + 3), co(4), None, OP.is_equal, None, B_(y0) + B_(7) + ["co4"], g_("m4"))
         tab, col = table(l0, 5)
         xq = l0 if n == 128 else 5
         mm([cg] + g_("wx0"), B_(l0, 8), (P_(xq), [("LEq", wx(-1))]),
            *[(col(4 - d, s), [("S%d" % d if d else "I", Cp(s))] + ([("LE%d" % d, X("wx", n + 64 * s, n + 64 * s + 64))] if d else [])) for d in range(5) for s in parts])
         scan(X("sn"), T.q5[:, 0:5 * n], tab, OP.add, OP.max, B_(l0, 8) + ["q5"], g_("sn"))
+        mm(g_("wx", "win"), B_(15), (P_(15), [("B1", wx(4)), ("BX32", win)]))
+        ts(P_(15), P_(15), co(4), None, OP.is_equal, None, B_(15) + ["co4"], g_("m4"))
         nc, nl = "nc%d%s" % (t, h), "nl%d%s" % (t, h)
         tt(NC, X("sn", 4, 5 * n, 5), P_(xq), OP.subtract, B_(xq) + g_("sn"), [nc])
         if t < 2:
             send(("c" + h, t + 1), NC, [nc])
         e0 = 0 if n == 128 else 12
-        mm([lg, "km1"] + g_("wx", "ax", "win"), B_(e0), *([(P_(e0 + j - 1), [("B1", wx(j + 1)), ("mB1", wx(j)), ("mI4", X("ax", n * j - n, n * j))]) for j in (1, 2, 3)]
-                                                          + [(P_(e0 + 3), [("I", L), ("mB8", win), ("I", T.km1[:, 0:n])])]))
-        flex(X("ex"), P_(e0, 4), AF.Relu, B_(e0), g_("ex"), (0.0, None, OP.max))
-        tt(X("t4"), NC, P_(7), OP.mult, [nc] + B_(7) + g_("m4"), g_("t4"))
+        mm(g_("wx", "ax"), B_(e0), *[(P_(e0 + j - 1), [("B1", wx(j + 1)), ("mB1", wx(j)), ("mI4", X("ax", n * j - n, n * j))]) for j in (1, 2, 3)])
+        flex(X("ex", 0, 3 * n), P_(e0, 3), AF.Relu, B_(e0), g_("ex"), (0.0, None, OP.max))
+        tt(X("t4"), NC, P_(15), OP.mult, [nc] + B_(15) + g_("m4"), g_("t4"))
         n0 = 12 if n == 128 else 0
         mm(g_("zw", "t4"), B_(n0), (P_(n0), [("BW", X("z4")), ("B8", X("t4"))]))
         tc(X("n4"), P_(n0), B_(n0), g_("n4"))
         ts(X("n5"), X("n4"), 3, 3, OP.arith_shift_right, OP.bitwise_and, g_("n4"), g_("n5"))
-        tt(X("n4m"), X("n5"), P_(7), OP.mult, B_(7) + g_("n5", "m4"), g_("n4m"))
-        mm(["km1"] + g_("wx", "ex"), B_(y0), (P_(y0), [("BQ0", wx(1)), ("mI", T.km1[:, 0:n])] + [("I", X("ex", n * j, n * j + n)) for j in range(4)]))
+        tt(X("n4m"), X("n5"), P_(15), OP.mult, B_(15) + g_("n5", "m4"), g_("n4m"))
+        mm(["km1"] + g_("wx", "ex", "ex3"), B_(y0), (P_(y0), [("BQ0", wx(1)), ("mI", T.km1[:, 0:n])] + [("I", X("ex", n * j, n * j + n)) for j in range(4)]))
         tt(NL, X("n4m"), P_(y0), OP.add, B_(y0) + g_("n4m"), [nl])
         if t < 2:
             send(("l" + h, t + 1), NL, [nl])

import numpy as np
from concourse.mybir import AluOpType as OP, AxisListType, ActivationFunctionType as AF

CH = {"a": (0, 128), "b": (128, 128)}
NW = {1: 4, 2: 6, 3: 7}
FIRST = sorted({k + 2 * a for k in NW for a in range(NW[k])})
DIAG = {"I": 1, "mI": -1, "I512": 512, "I101": 101, "I64": 64, "I32": 32, "mI4": -4, "mI128": -128, "mI256": -256, "Ih": 0.5, "Iq": 0.25}
DIAG.update({"K%d" % a: (4 * a - 11) * 2048 for a in range(7)})
BLOCK = {"mB1": -1, "mB8": -8, "BH": 0.5, "B8": 8, "BX32": 32, "BX2": 2, "BX3": 3}
ROWS = {"CU": (-32768, 4, 2.0 ** -9), "CL": (2048, 56, 7 / 64), "CF": (-98304, -1024, -61)}
SLOTS = ["M2", "M3", "B1", "ON", "LE", "LEq", "S1", "S2", "S3", "S4", "BW", "BQ0", "BR0", "BR1"] + list(DIAG) + list(BLOCK) + list(ROWS)
SLOTS += ["W%d" % e for e in FIRST] + ["LE%d" % d for d in (1, 2, 3, 4)]
SLOT = {n: j for j, n in enumerate(SLOTS)}
BUF = {"bfloat16": "xt_8192 mk5_2560 wl_2064 cl_2064 ff_256 wtb_16 onef_16 e16_16 tmpm_128 km1_128 kmh_128 kmx_128 q2_256 junk_128 c16_32",
       "float32": "sd_16 jio_16 jt_16 co_24 b8f_8 bw8_8 bc8_8 ct_16 ac_16 ysb_256 q4_512 q5_640 q6_768 q7_896", "int32": "sti_256 tmi_256 tmj_256"}
BUFH = {"bfloat16": "zz_5120 vs_5120 pt_448 pp_128 msk_128 y8_64 rr_64 ax0_64 sel_64 gg_1024 w3_64 fw_128 win_128 vsel_64 z4_64 wx_384 l2_64 ax_192 ex_256 t4_64 n4m_64",
        "float32": "f1_64 c8f_64 sc_448 sn_320", "int32": "s32_64 x32_64 r32_64 n32_64 nn_64 xi_64 c8_64 n4_64 n5_64 o32_4 q32_4", "uint16": "offs_64 ofs_4 of2_4"}
SIZE = {s.split("_")[0]: int(s.split("_")[1]) for names in BUFH.values() for s in names.split()}
LAG = {"a": (0, 0, 0, 0), "b": (0.5, 0.5, 0.5, 0.5)}
VG = ["0a1", "0b0", "0b0"]
S5 = 32
ONS = ""
AHEAD = {}
TRIES, SHIFT, FS, GK = 8000, 300, 72, 1.65
BIAS, PASSES = 0.3, 8
ARR, MMF, PEC, CYC, FV, SAME, CROSS = 4300, 3.5, 0.38, 0.84, 24, 150, 225
NOISE, SCALES = 310, [{}, {"n": 1.7, "s": 1.15}, {"s": 0.8}, {"t": 1.15, "v": 1.08}]


def _bufs():
    out = {"mats": ("sbuf", [128, len(SLOTS) * 128], "bfloat16")}
    for table, k in ((BUF, 1), (BUFH, 4)):
        for dt, names in table.items():
            for s in names.split():
                nm, n = s.split("_")
                out[nm] = ("sbuf", [128, int(n) * k], dt)
    for t in range(3):
        out["rec%d" % t] = ("sbuf", [128, 1024], "bfloat16")
        out["nr%d" % t] = ("sbuf", [128, 512], "bfloat16")
    for h, (_, n) in CH.items():
        out["pd" + h] = ("psum", [128, 16 * n], "float32")
    return out


SCRATCH = _bufs()
MSG = [("s", 1), ("s", 2)] + [(k + h, t) for t in (1, 2) for h in CH for k in "cl"]
COLS = {k + h: (2 * b + n * j, 2 * b + n * j + n) for h, (b, n) in CH.items() for j, k in enumerate("cl")}
COLS["s"] = (512, 1024)
SEMAPHORES = ["e_v", "e_s", "e_t", "e_g"] + ["ld_" + n for n in ("st", "sp", "wt", "x", "ch", "fl")] + ["o_c", "o_l", "o_f", "o_s"]
SEMAPHORES += [p + "%s%d" % m for m in MSG for p in ("a_", "b_")]
KEEP = []
LN2 = 0.6931471805599453


def nbits(m):
    return bin(m).count("1")


def relays(src, dst, topo):
    if topo.may_write(src, dst):
        return []
    own = [c for c in topo.cores_of(src) if c != src and topo.may_write(c, dst)]
    return sorted(own, key=lambda c: (topo.die(c) != topo.die(src), c))


def via(msg, src, dst, topo):
    own = relays(src, dst, topo)
    return own[(msg[0][0] == "l") % len(own)] if own else None


def cv(n, k):
    return FV + max(64, n * k) * CYC


def cs(n, k=1):
    return FS + n * k * CYC


def order(nodes, after, ahead, names):
    n = len(nodes)
    pred, succ, lw, rd = [[] for _ in range(n)], [[] for _ in range(n)], {}, {}
    for j, (alts, r, w, _) in enumerate(nodes):
        ws = w + [t for t in r if t[0] == "#"]
        ps = set()
        for t in r + ws:
            ps.update(lw.get(t, []) if t[0] != "+" else rd.get(t[1:], []))
        for t in ws:
            ps.update(rd.get(t, []))
        for t in r:
            rd.setdefault(t, []).append(j)
        for t in ws:
            if t[0] == "+":
                lw.setdefault(t[1:], []).append(j)
            else:
                lw[t], rd[t] = [j], []
        pred[j] = ps - {j}
    for p, j in after:
        pred[j].add(p)
    for j in range(n):
        for p in pred[j]:
            succ[p].append(j)
    prio, left = [0.0] * n, [len(x) for x in succ]
    todo = [j for j in range(n) if not left[j]]
    for j in todo:
        prio[j] = nodes[j][0][0][1] + CROSS + max([prio[x] for x in succ[j]] + [0])
        for p in pred[j]:
            left[p] -= 1
            if not left[p]:
                todo.append(p)

    def place(pred, succ, prio):
        left = [len(p) for p in pred]
        ready = [j for j in range(n) if not left[j]]
        busy, start, end, alt = {}, [0.0] * n, [0.0] * n, [0] * n
        while ready:
            j = max(ready, key=lambda x: prio[x])
            ready.remove(j)
            best = None
            for a, (q, cost) in enumerate(x[:2] for x in nodes[j][0][:1 if nodes[j][3] == "pin" else 2]):
                s = max([end[p] + (SAME if nodes[p][0][alt[p]][0] == q else CROSS) for p in pred[j]] + [0.0])
                hold = {"dma": 70, "arr": 0}.get(nodes[j][3], cost)
                iv = busy.setdefault(q, [])
                lo, hi = 0, len(iv)
                while lo < hi:
                    mid = (lo + hi) // 2
                    lo, hi = (mid + 1, hi) if iv[mid][1] <= s else (lo, mid)
                while lo < len(iv) and iv[lo][0] < s + hold:
                    s = max(s, iv[lo][1])
                    lo += 1
                e = s + cost + (BIAS * cost if q == "v" else 0)
                if best is None or e < best[0]:
                    best = (e, s, a, q, lo, hold, cost)
            _, s, alt[j], q, lo, hold, cost = best
            start[j], end[j] = s, s + cost
            if hold:
                busy[q].insert(lo, (s, s + hold))
            for x in succ[j]:
                left[x] -= 1
                if not left[x]:
                    ready.append(x)
        return start, end, alt

    def replay(seq, scale, held=None):
        free, end, qof, f = dict.fromkeys("vstgyn", 0.0), [0.0] * n, [None] * n, {q: scale.get(q, 1.0) for q in "vstgyn"}
        for _, j, a in seq:
            q, cost = short[j][a]
            s = free[q]
            for p in pred[j]:
                x = end[p] + (SAME if qof[p] == q else CROSS)
                if x > s:
                    s = x
            x = end[j] = s + cost * f[q]
            qof[j] = q
            free[q] = x if plain[j] else s + 70 if q != "n" else 0.0
        if held is not None:
            at, before, last = {}, {}, {}
            for k, (_, j, a) in enumerate(seq):
                at[j], before[j], last[qof[j]] = k, last.get(qof[j]), j
            j = end.index(max(end))
            while j is not None:
                s = end[j] - short[j][seq[at[j]][2]][1] * f[qof[j]]
                w = [p for p in pred[j] if end[p] + (SAME if qof[p] == qof[j] else CROSS) > s - 1e-3]
                if not w and before[j] is not None:
                    held.append((at[before[j]], at[j]))
                j = w[0] if w else before[j]
        return max(end)

    plain, short = [x[3] not in ("dma", "arr") for x in nodes], [[a[:2] for a in x[0]] for x in nodes]

    best, rng = None, np.random.default_rng(0)
    for i in range(PASSES):
        start, end, alt = place(pred, succ, [x + y for x, y in zip(prio, ahead)])
        seq = sorted((start[j], j, alt[j]) for j in range(n))
        e = sum(replay(seq, x) for x in SCALES)
        if best is None or e < best[0]:
            best = (e, seq, end)
        prio = place(succ, pred, [x + NOISE * float(y) for x, y in zip(best[2] if i % 4 == 3 else end, rng.random(n))])[1]
    for p, j in after:
        pred[j].discard(p)
    e, seq, held = best[0], best[1], []
    for i in range(TRIES):
        if not held:
            first = replay(seq, SCALES[0], held)
            replay(seq, SCALES[1 + i % (len(SCALES) - 1)], held)
            at = {c[1]: k for k, c in enumerate(seq)}
        x, y = held[int(rng.integers(len(held)))]
        j, k, move = seq[x][1], seq[y][1], int(rng.integers(4))
        if move == 0:
            z = max([at[p] for p in pred[k]] + [-1]) + 1
            if z > x:
                continue
            z = x - int(rng.integers(min(x - z, 12) + 1))
            new = seq[:z] + [seq[y]] + seq[z:y] + seq[y + 1:]
        elif move == 1:
            z = min([at[s] for s in succ[j] if j in pred[s]] + [n]) - 1
            if z < y:
                continue
            z = y + int(rng.integers(min(z - y, 12) + 1))
            new = seq[:x] + seq[x + 1:z + 1] + [seq[x]] + seq[z + 1:]
        elif move > 1 and len(nodes[seq[(x, y)[move - 2]][1]][0]) > 1:
            z = (x, y)[move - 2]
            new = seq[:z] + [(seq[z][0], seq[z][1], 1 - seq[z][2])] + seq[z + 1:]
        else:
            continue
        f = replay(new, SCALES[0])
        if f > first + SHIFT:
            continue
        f += sum(replay(new, s) for s in SCALES[1:])
        if f <= e + SHIFT * (1 - i / TRIES):
            e, seq, held = f, new, []
            if e < best[0]:
                best = (e, seq)
    return best[1]


def rank_program(g, core, T, topo):
    N = len(T.cores)
    rank = T.rank_of(core)

    def put(msg, src_ap, dst):
        a, b = COLS[msg[0]]
        rid, pid = topo.addr(dst, core)
        m = topo.mask(core, dst)
        g.remote_dma(T["rec%d" % msg[1]][:, a:b], src_ap, T.sem["a_%s%d" % msg], T.sem["b_%s%d" % msg], pid, rid, m)
        return nbits(m)

    if rank is None:
        for r in range(N):
            src, dst = T.cores[r], T.cores[(r + 1) % N]
            sent = []
            for msg in [x for x in MSG if via(x, src, dst, topo) == core]:
                a, b = COLS[msg[0]]
                g.wait_ge(T.sem["a_%s%d" % msg], nbits(topo.mask(src, core)))
                sent.append((msg, put(msg, T["rec%d" % msg[1]][:, a:b], dst)))
            for msg, n in sent:
                g.wait_ge(T.sem["b_%s%d" % msg], n)
        return

    nxt, prv = T.cores[(rank + 1) % N], T.cores[(rank - 1) % N]
    nodes, parts_of, now = [], [], ["start"]

    def add(alts, r, w, kind="op"):
        nodes.append((alts, list(r), list(w), kind))
        parts_of.append(now[0])

    def vop(meth, cost, r, w, *a):
        add([("v", cost, lambda: {"tt": g.vector.tensor_tensor, "ts": g.vector.tensor_scalar, "tc": g.vector.tensor_copy, "ms": g.vector.memset,
                                  "sc": g.vector.tensor_tensor_scan, "tr": g.vector.tensor_reduce}[meth](*a))], r, w)

    def tt(out, a, b, op, r, w, k=1):
        vop("tt", cv(out.shape[1], k), r, w, out, a, b, op)

    def ts(out, a, s1, s2, o1, o2, r, w, k=1):
        vop("ts", cv(out.shape[1], k), r, w, *((out, a, s1, s2, o1) if o2 is None else (out, a, s1, s2, o1, o2)))

    def tc(out, a, r, w, k=1):
        vop("tc", cv(out.shape[1], k), r, w, out, a)

    def ms(ap, val, w, r=(), k=0.5):
        vop("ms", cv(ap.shape[1], k), r, w, ap, val)

    def scan(out, a, b, o0, o1, r, w, k=1):
        vop("sc", cv(out.shape[1], k), r, w, out, a, b, 0.0, o0, o1)

    def act(out, in_, func, r, w, k=1, **kw):
        add([("s", cs(out.shape[1], k), lambda: g.scalar.activation(out, in_, func, **kw))], r, w)

    def flex(out, in_, func, r, w, v, k=1, kv=1, **kw):
        add([("s", cs(out.shape[1], k), lambda: g.scalar.activation(out, in_, func, **kw)),
             ("v", cv(out.shape[1], k * kv), lambda: g.vector.tensor_scalar(out, in_, *v) if v else g.vector.tensor_copy(out, in_))], r, w)

    def lin(out, in_, f, o, r, w, kv=1):
        flex(out, in_, AF.Identity, r, w, (f, o, OP.mult, OP.add), 1, kv, scale=f, bias=o)

    def only(x):
        if x in ONS:
            del nodes[-1][0][1]
        if x.upper() in ONS:
            del nodes[-1][0][0]

    def gp(meth, r, w, *a, **kw):
        add([("g", 400, lambda: {"iota": g.iota, "sel": g.affine_select}[meth](*a, **kw))], r, w)

    def fill(nm, pat, v, n):
        add([("g", 150 + n * 1.75, lambda: g.iota(T[nm][:], pat, v, 0, allow_small_or_imprecise_dtypes=True))], [], [nm + "0"])

    def cpy(out, in_, r, w):
        add([("g", 180 + 1.75 * out.shape[1], lambda: g.affine_select(out, in_, [[0, out.shape[1]]], OP.is_ge, 0.0, 1, 0))], r, w)

    def MM(r, w, items):
        def f():
            for o, l, x, s0, s1 in items:
                i = g.tensor.matmul(o, l, x, s0, s1)
            return i
        add([("t", 10 + sum(MMF + PEC * max(64, x[0].shape[1]) for x in items), f)], r, w)

    def M(n):
        return T.mats[:, SLOT[n] * 128:SLOT[n] * 128 + 128]

    def grp(out, pairs):
        return [(out, M(l) if isinstance(l, str) else l, x, j == 0, j == len(pairs) - 1) for j, (l, x) in enumerate(pairs)]

    def mm(r, w, *groups):
        it = [x for o, pairs in groups for x in grp(o, pairs)]
        MM(list(r) + sorted({l for _, pairs in groups for l, _ in pairs if isinstance(l, str)}), w, it)

    def WM(n, m):
        return T[n][:, 128 * m:128 * m + 128]

    def ones(n):
        return T.mats[:, SLOT["ON"] * 128:SLOT["ON"] * 128 + n]

    def dma(q, sem, out, in_, r, w, cost=2600):
        add([(q, cost, lambda: {"y": g.sync, "s": g.scalar}[q].dma_start(out, in_))], r, w, ("dma", sem, 16))

    TAB = T.xt[:, 4096:8192]
    dma("s", "ld_st", T.sti[:], T.st[:], [], ["sti"])
    dma("s", "ld_sp", T.rec0[:, 256:512], T.sp[:], [], ["l0" + h for h in CH])
    dma("s", "ld_wt", T.wtb[:, 0:1], T.wt[:], [], ["wtb"])
    dma("y", "ld_x", TAB, T.x[:], [], ["x"], 8000)
    dma("s", "ld_ch", T.rec0[:, 0:256], T.ch[:], [], ["c0" + h for h in CH])
    dma("s", "ld_fl", T.ff[:], T.fl[:], [], ["ff" + h for h in CH])
    ms(M("ON"), 1.0, ["ON"]); ms(T.onef[:], 1.0, ["onef"]); ms(T.wl[:], 0.0, ["wl0"])
    fill("cl", [[0, 2064]], 0, 2064); fill("msk", [[0, 512]], 0, 512)
    fill("mk5", [[0, 512], [256, 5]], 0, 2560)
    for k in (4, 6, 7):
        fill("q%d" % k, [[0, 128], [16384, k]], -26 * 2048, 128 * k)
        ms(T["q%d" % k][:, 0:128 * k:k], -1e9, ["+q%d" % k], ["q%d0" % k], 1)
        ms(T["q%d" % k][:, k - 1:128 * k:k], 2048.0 * (8 * k - 34) + sum(ROWS["CL"]), ["+q%d" % k], ["q%d0" % k], 1)
    fill("q5", [[0, 128], [512, 5]], -2304, 640)
    ms(T.q5[:, 0:640:5], -1e9, ["q5"], ["q50"], 1)
    ms(T.q2[:, 0:256:2], 1048576.0, ["+q2"]); ms(T.q2[:, 1:256:2], 0.0, ["+q2"])
    for nm, o, st in (("jio", T.jio[:], [[1, 16]]), ("ct", T.ct[:], [[256, 16]])):
        gp("iota", [], [nm], o, st, 0, 0, allow_small_or_imprecise_dtypes=True)
    gp("sel", ["ON"], ["I"], M("I"), M("ON"), [[-1, 128]], OP.is_equal, 0.0, 0, 1)
    gp("sel", ["ON"], ["tmpm"], T.tmpm[:], M("ON"), [[-16, 8], [0, 16]], OP.is_ge, 0.0, 0, 1)
    gp("sel", ["tmpm"], ["B1"], M("B1"), T.tmpm[:], [[16, 8], [0, 16]], OP.is_ge, 0.0, 15, -1)
    gp("sel", ["B1"], ["LE"], M("LE"), M("B1"), [[1, 128]], OP.is_ge, 0.0, 0, -1)
    for d in (1, 2, 3, 4):
        gp("sel", ["B1"], ["S%d" % d], M("S%d" % d), M("B1"), [[-1, 128]], OP.is_equal, 0.0, -d, 1)
    ts(T.tmi[:], T.sti[:], 6, None, OP.arith_shift_right, None, ["sti"], ["tmi"])
    ts(T.tmj[:], T.sti[:], 63, None, OP.bitwise_and, None, ["sti"], ["tmj"])
    tc(T.rec0[:, 512:768], T.tmi[:], ["tmi"], ["+s0"])
    tc(T.rec0[:, 768:1024], T.tmj[:], ["tmj"], ["+s0"])
    tt(T.junk[:, 0:64], T.mats[:, SLOT["I"] * 128:SLOT["I"] * 128 + 64], T.mats[:, SLOT["I"] * 128 + 64:SLOT["I"] * 128 + 128], OP.add, ["I"], ["f64"], 2)
    tt(T.junk[:, 64:96], T.junk[:, 0:32], T.junk[:, 32:64], OP.add, ["f64"], ["f32"])
    tt(T.e16[:], T.junk[:, 64:80], T.junk[:, 80:96], OP.add, ["f32"], ["e16"])
    tt(T.jt[:], T.e16[:], T.jio[:], OP.mult, ["e16", "jio"], ["jt"])
    co = lambda j: T.co[:, j:j + 1]
    vop("tr", 120, ["jt"], ["co0"], co(0), T.jt[:], AxisListType.X, OP.add)
    for j, f, o in ((1, 1, -1), (2, 1, -8), (3, 1, -9), (4, 1, 28), (5, -1, 0), (8, 5 / 4096, 4 / 4096), (10, -LN2, -80 * LN2), (11, 16, 0)):
        ts(co(j), co(0), float(f), float(o), OP.mult, OP.add, ["co0"], ["co%d" % j])
    tc(co(7), T.wtb[:, 0:1], ["wtb"], ["co7"])
    tc(co(12), T.e16[:, 0:1], ["e16"], ["co12"])
    for b, n in CH.values():
        for j, (o, f) in enumerate(((b // 16, 1.0), (0, 4.0))):
            c0 = (2 * b + j * n) // 16
            ts(T.c16[:, c0:c0 + n // 16], T.ct[:, o:o + n // 16], co(11), f, OP.add, OP.mult, ["co11", "ct"], ["+c16"])
    b8 = SLOT["B1"] * 128
    tc(T.b8f[:], T.mats[:, b8:b8 + 113:16], ["B1"], ["b8f"])
    for nm, src, f, r2 in (("wl", "bw8", co(7), "co7"), ("cl", "bc8", 4096.0, "b8f")):
        ts(T[src][:], T.b8f[:], f, None, OP.mult, None, ["b8f", r2], [src])
        for gi in range(8):
            col = T[src][:, gi:gi + 1]
            flex(T[nm][:, 16 * gi:16 * gi + 129 * 15 + 1:129], T.onef[:], AF.Copy, ["onef", src, nm + "0"], ["+" + nm], (col, None, OP.mult), scale=col)
    ts(T.jt[:, 0:15], T.e16[:, 1:16], 512.0, None, OP.mult, None, ["e16", "co0"], ["jd"])
    ms(T.jt[:, 15:16], 0.0, ["jd"])
    tt(T.jio[:], T.jt[:], T.e16[:], OP.add, ["jd", "e16", "co0"], ["je"])
    ts(T.sd[:], T.jio[:], 0.03125, None, OP.mult, None, ["je"], ["sd"])

    def mat(dst, src, f, r2=()):
        flex(M(dst), M(src), AF.Copy, [src] + list(r2), [dst], (f, None, OP.mult), 1, 0.5, scale=f)

    for nm, f in DIAG.items():
        if nm != "I" and nm[0] != "K":
            mat(nm, "I", float(f))
    ko = T.mats[:, SLOT["K0"] * 128:SLOT["K6"] * 128 + 128]
    add([("g", 1700, lambda: g.iota(ko, [[8192, 7], [0, 128]], -11 * 2048, 0, allow_small_or_imprecise_dtypes=True))], [], ["K"])
    add([("g", 1700, lambda: g.affine_select(ko, ko, [[0, 7], [-1, 128]], OP.is_equal, 0.0, 0, 1))], [], ["K"] + ["K%d" % a for a in range(7)])
    for nm, f in BLOCK.items():
        mat(nm, "B1", float(f))
    for d in (1, 2, 3, 4):
        mat("LE%d" % d, "LE", 512.0 * d)
    mat("LEq", "LE", 256.0)
    for e in FIRST:
        mat("W%d" % e, "B1", T.sd[:, e:e + 1], ["sd"])
    mat("BW", "B1", co(7), ["co7"]); mat("M2", "I", co(2), ["co2"]); mat("M3", "I", co(3), ["co3"])
    mat("BR0", "B1", co(12), ["co12"]); mat("BR1", "B1", co(12), ["co12"])
    o = SLOT["BR1"] * 128
    ms(T.mats[:, o:o + 113:16], 0.0, ["BR1"])
    ms(M("BQ0"), 0.0, ["BQ0"])
    o = SLOT["BQ0"] * 128
    tc(T.mats[:, o:o + 113:16], T.mats[:, b8:b8 + 113:16], ["B1"], ["BQ0"])
    for nm, vals in ROWS.items():
        ms(M(nm), 0.0, [nm + "0"])
        for j, v in enumerate(vals):
            ms(T.mats[32 * j:32 * j + 1, SLOT[nm] * 128:SLOT[nm] * 128 + 128], float(v), ["+" + nm], [nm + "0"])
    for nm, v in (("km1", -1.0), ("kmh", -0.5), ("kmx", -34816.0)):
        ms(T[nm][:], v, [nm])
    ms(T.ac[:, 0:1], 0.0, ["ac0"])

    sends = []

    def send(msg, ap, tags):
        def f():
            sends.append(("b_%s%d" % msg, put(msg, ap, via(msg, core, nxt, topo) or nxt)))
        add([("g", 700, f)], tags, ["sent%s%d" % msg], ("send",))
        add([("n", ARR, None)], ["sent%s%d" % msg], ["%s%d%s" % (msg[0][0], msg[1], msg[0][1:])],
            ("arr", "a_%s%d" % msg, nbits(topo.mask(via(msg, prv, core, topo) or prv, core))))

    send(("s", 1), T.rec0[:, 512:1024], ["s0"])
    gat = {}

    def stream(t, h):
        b, n = CH[h]
        parts = range(n // 64)
        R, NR, pd = T["rec%d" % t], T["nr%d" % t], T["pd" + h]
        C, L = (R[:, 2 * b:2 * b + n], R[:, 2 * b + n:2 * b + 2 * n]) if t else (R[:, b:b + n], R[:, 256 + b:256 + b + n])
        Cp = lambda s: R[:, (2 * b if t else b) + 64 * s:(2 * b if t else b) + 64 * s + 64]
        NC, NL = (NR[:, 2 * b:2 * b + n], NR[:, 2 * b + n:2 * b + 2 * n]) if t < 2 else (NR[:, b:b + n], NR[:, 256 + b:256 + b + n])
        F = T.ff[:, b:b + n]
        cg, lg = "c%d" % t + h, "l%d" % t + h
        g_ = lambda *x: [y + h for y in x]
        zt = lambda k: g_(*["z%d%d" % (k, s) for s in parts])

        def X(nm, lo=0, hi=None, step=1):
            o = SIZE[nm] * b // 64
            return T[nm][:, o + lo:o + (SIZE[nm] * n // 64 if hi is None else hi):step]

        P_ = lambda j, c=1: pd[:, n * j:n * (j + c)]
        B_ = lambda j, c=1: ["#%s%d" % (h, x) for x in range(n * j // 512, (n * (j + c) + 511) // 512)]

        def table(j, w):
            o = n * j + (512 - 64 * w) * (n // 128)
            return pd[:, o:o + n * w], lambda a, s: pd[:, o + 64 * w * s + a:o + 64 * w * (s + 1):w]

        wx = lambda j, c=1: X("wx", n * (j + 1), n * (j + 1 + c))
        win, y8, ppv = X("win", 0, n), X("y8"), X("pp", 1, 2 * n, 2)

        def gather(k, s):
            gw = 64 if k < 4 else 32
            for j in range(64 * s, 64 * s + 64, gw):
                o, i, w = X("zz", 80 * j + k, 80 * (j + gw), 5), TAB.indirect(X("offs", j, j + gw)), ["+z%d%d%s" % (k, s, h)] + g_("y%d" % (j // 32))[:k // 4]
                gat[t, k, h, s, j] = len(nodes)
                flex(o, i, AF.Copy, ["x", "off" + h], w, None, GK)
                if "%d%s%d" % (k, h, s) in VG[t]:
                    nodes[-1][0].reverse()
                nodes[-1] = nodes[-1][:3] + (("pin",),)

        now[0] = "first" + h
        mm([lg, "s%d" % t], B_(7), (P_(7), [("I512", L), ("I101", L), ("I64", R[:, 512 + b:512 + b + n]), ("I", R[:, 768 + b:768 + b + n])]))
        ts(X("s32"), P_(7), T.ac[:, 4 * t:4 * t + 1], None, OP.add, None, B_(7) + ["ac%d" % t], g_("s32"))
        ts(X("r32"), X("s32"), 4095, None, OP.bitwise_and, None, g_("s32"), g_("r32"))
        tc(X("offs"), X("r32"), g_("r32"), g_("off"))
        mm([lg], B_(8), (P_(8), [("BR0", L)]))
        flex(X("ax0"), P_(8), AF.Abs, B_(8) + ["co0", "co5"], g_("ax0"), (co(0), None, OP.not_equal), bias=co(5))
        mm([cg] + g_("ax0"), B_(9), (P_(9), [("I", C), ("mI128", X("ax0"))]))
        flex(X("sel"), P_(9), AF.Relu, B_(9), g_("sel"), (0.0, None, OP.max))
        mm([cg] + g_("sel"), B_(10), (P_(10), [("BR1", C), ("BQ0", X("sel"))]))
        lin(y8, P_(10), 0.25, 0.125, B_(10), g_("y8"))
        lin(X("c8f"), P_(10), 8.0, 28.0, B_(10), g_("c8"))
        pts = [X("pt", 2 * n * j + 1, 2 * n * (j + 1), 2) for j in range(3)] + [X("pt", 6 * n, 7 * n)]
        for j in range(3):
            cpy(X("pt", 2 * n * j, 2 * n * (j + 1) - 1, 2), L, [lg], g_("lp%d" % (j + 1)))
        act(X("l2"), L, AF.Square, [lg], g_("l2"))
        act(X("w3"), L, AF.Sigmoid, [lg, "co10"], g_("w3"), scale=16 * LN2, bias=co(10))

        for k in range(4):
            kk = k + 1
            now[0] = "place" + h
            if k < 3:
                nw = NW[kk]
                tab, col = table(8, nw)
                MM([cg, "ON", "CL"] + ["W%d" % (kk + 2 * a) for a in range(nw)], B_(8, 8),
                   [(col(a, s), M("W%d" % (kk + 2 * a)), Cp(s), a == 0, False) for a in range(nw) for s in parts]
                   + [(col(nw - 1, s), M("CL"), ones(64), False, False) for s in parts])
            if t == 2 and k == 1:
                mm(["x"], B_(5), (P_(5), [("I", T.xt[:, 4096 + 16 * b + a:4096 + 16 * (b + n):16]) for a in range(16)]))
                flex(T.ysb[:, b:b + n], P_(5), AF.Copy, B_(5), g_("ysb"), None)
            for s in parts:
                gather(k, s)
                mm(["wl", "ON"] + g_("z%d%d" % (k, s)), B_(0), (pd[:, 64 * s:64 * s + 64],
                   [("CU", ones(64))] + [(WM("wl", m), X("zz", 5120 * s + 5 * m + k, 5120 * (s + 1), 80)) for m in range(16)]))
            tt(X("x32"), P_(0), y8, OP.mult, B_(0) + g_("y8"), g_("x32"))
            lin(P_(4), P_(0), 37.0, 3947.0, B_(0) + B_(4), g_("u37"))
            only("u")
            tt(X("n32"), P_(0), X("c8" if k else "c8f"), OP.add, B_(0) + g_("c8"), g_("n32"))
            tt(X("r32"), X("x32"), P_(4), OP.add, B_(4) + g_("x32", "u37"), g_("r32"))
            ts(X("s32"), X("r32"), 4095, None, OP.bitwise_and, None, g_("r32"), g_("s32"))
            tc(X("offs"), X("s32"), g_("s32"), g_("off"))
            P, tp = pts[k], "p%d%s" % (kk, h)
            now[0] = "pick" + h
            ts(X("nn"), X("n32"), 3, 3, OP.arith_shift_right, OP.bitwise_and, g_("n32"), g_("nn"))
            if k == 0:
                ts(P, X("nn"), -6.0, None, OP.add, None, g_("nn"), [tp])
            elif k < 3:
                tt(P, X("nn"), P_(6), OP.add, B_(6) + g_("nn"), [tp])
            else:
                tt(P, X("nn"), pts[2], OP.add, g_("nn", "p3"), [tp], 2)
            if k < 3:
                if k:
                    tt(X("msk", 1, 2 * n, 2), X("nn"), P_(7), OP.is_ge, B_(7) + g_("nn") + ["msk0"], g_("msk"))
                else:
                    ts(X("msk", 1, 2 * n, 2), X("nn"), co(1), None, OP.is_ge, None, g_("nn") + ["co1", "msk0"], g_("msk"))
                scan(X("pp"), X("msk"), X("pt", 2 * n * k, 2 * n * kk), OP.mult, OP.add, [tp, "msk0"] + g_("msk", "lp%d" % kk), g_("pp"), 0.5)
                if k < 2:
                    mm([tp, "ON"], B_(6), (P_(6), [("I", P)]), (P_(7), [("mI", P), ("M%d" % (kk + 1), ones(n))]))
                MM(["K%d" % a for a in range(nw)] + g_("pp"), B_(8, 8),
                   [(col(a, s), M("K%d" % a), X("pp", 128 * s + 1, 128 * s + 128, 2), False, a == nw - 1) for a in range(nw) for s in parts])
                lin(X("rr"), ppv, 0.5, 194.75, g_("pp"), g_("rr"), 0.5)
                only("r")
                mm(["ON"] + g_("pp", "rr"), B_(5), (P_(5), [("CF", ones(n)), ("mI256", ppv), ("Ih", ppv), ("I512", X("rr")), ("mI", X("rr"))]))
                scan(X("sc", 0, n * nw), T["q%d" % nw][:, 0:n * nw], tab, OP.add, OP.max, B_(8, 8) + ["q%d" % nw], g_("sc"))
                tt(X("xi"), P_(5), X("sc", nw - 1, n * nw, nw), OP.mult, B_(5) + g_("sc"), g_("xi"))
                ts(X("c8"), X("xi"), 2044, None, OP.bitwise_and, None, g_("xi"), g_("c8"))
                ts(y8, X("c8"), 0.03125, -0.75, OP.mult, OP.add, g_("c8"), g_("y8"))
        now[0] = "four" + h
        vt = g_(*["vt%d" % s for s in parts])
        bk = lambda s: ["#%s%d" % (h, x) for x in ((2, 3) if n == 128 and s == 0 else (0, 1))]
        vf = lambda s, m, c=1: pd[:, 1024 * (n == 128 and s == 0) + 64 * m:1024 * (n == 128 and s == 0) + 64 * (m + c)]
        for s in parts:
            MM(["mI", "ff" + h], bk(s), [(vf(s, m), M("mI"), T.ff[:, b + 64 * s:b + 64 * s + 64], m % 8 == 0, False) for m in range(16)])
            gather(4, s)
        yield
        now[0] = "fail" + h
        for s in parts:
            for o in range(5120 * s, 5120 * (s + 1), 80 * S5):
                scan(X("vs", o, o + 80 * S5), T.mk5[:, 0:80 * S5], X("zz", o, o + 80 * S5), OP.min, OP.max,
                     ["mk50"] + g_("y%d" % (o // 2560), *["z%d%d" % (k, s) for k in range(4)]), ["+" + vt[s], "+fs" + h], 0.5)
            for j in (0, 1):
                MM(["I", vt[s]], [bk(s)[j]], [(vf(s, m), M("I"), X("vs", 5120 * s + 5 * m + 4, 5120 * (s + 1), 80), False, m % 8 == 7) for m in range(8 * j, 8 * j + 8)])
                flex(X("gg", 1024 * s + 512 * j, 1024 * s + 512 * j + 512), vf(s, 8 * j, 8), AF.Sigmoid, [bk(s)[j]], g_("gg%d%d" % (s, j)), (0.0, None, OP.is_ge), scale=200.0, bias=100.0)
        cpy(X("vs", 0, 80 * n, 80), F, ["ff" + h] + vt, g_("fs"))
        o = n * 8
        for s in parts:
            it = grp(pd[:, o + 128 * s + 1:o + 128 * s + 128:2], [("I", X("w3", 64 * s, 64 * s + 64))])
            it += grp(pd[:, o + 128 * s:o + 128 * s + 128:2], [("I", T.kmx[:, 0:64])] + [(WM("cl", m), X("gg", 1024 * s + 64 * m, 1024 * s + 64 * m + 64)) for m in range(16)])
            MM(["cl", "kmx", "I"] + g_("gg%d0" % s, "w3"), B_(8), it[:10])
            MM(g_("gg%d1" % s), B_(8), it[10:])
        scan(X("fw"), T.q2[:, 0:2 * n], P_(8, 2), OP.max, OP.min, B_(8) + ["q2"], g_("fw"))
        fw = X("fw", 1, 2 * n, 2)
        w0 = 0 if n == 128 else 12
        MM(["BH", "I", lg] + g_("fw", "l2"), B_(8), grp(P_(10), [("BH", fw)]) + [(P_(8), M("I"), X("l2"), True, False), (P_(9), M("I"), L, False, False)])
        MM(["I"] + g_("p1", "p2", "p3", "p4"), B_(w0), [(P_(w0 + j), M("I"), pts[j], j == 0 and n == 128, False) for j in range(4)])
        tt(win, fw, P_(10), OP.is_gt, B_(8) + g_("fw"), g_("win"))
        e = n // 16
        now[0] = "table" + h
        pk, po, ph, c0 = *(pd[:, 4 * n + e * j:4 * n + e * (j + 1)] for j in range(3)), b // 8
        flex(X("win", n, 2 * n), win, AF.Copy, g_("win") + ["co8"], g_("wo"), (co(8), None, OP.mult), 1, 0.5, scale=co(8))
        it = grp(pd[:, 4 * n:4 * n + 2 * e], [("I", T.c16[:, c0:c0 + 2 * e])] + [(WM("cl", a), X("win", a, 2 * n, 16)) for a in range(16)])
        MM(["cl", "c16", "I", "Iq"] + g_("win", "wo"), B_(4), it[:1] + [(po, M("Iq"), T.c16[:, c0 + e:c0 + 2 * e], False, False)] + it[1:])
        tc(X("ofs"), po, B_(4), g_("ofs"))
        mm([lg] + g_("win"), B_(7), (P_(7), [("I", L), ("mB8", win)]))
        flex(X("ex", 3 * n, 4 * n), P_(7), AF.Relu, B_(7), g_("ex3"), (-1.0, 0.0, OP.add, OP.max), bias=-1.0)
        if b + n == 256 and t < 2:
            mm(["win" + x for x in CH], B_(5), (pd[:, 5 * n:5 * n + 64], [("ON", T.win[:, 2 * x + 64 * s:2 * x + 64 * s + 64]) for x, y in CH.values() for s in range(y // 64)]))
            act(T.junk[:, 0:64], pd[:, 5 * n:5 * n + 64], AF.Copy, B_(5), ["f64", "f32", "ac%d" % (t + 1)], accum_out=T.ac[:, 4 * t + 4:4 * t + 5])
        flex(X("vsel"), X("vs").indirect(X("ofs")), AF.Copy, g_("ofs", "fs") + vt, g_("vsel"), None, 1.5)
        flex(X("z4"), X("zz").indirect(X("ofs")), AF.Copy, g_("ofs") + zt(4), g_("zw"), None, 1.5)
        mm(["wl"] + g_("vsel"), B_(4), (ph, [(WM("wl", a), X("vsel", a, n, 16)) for a in range(16)]))
        tc(X("q32"), ph, B_(4), g_("q32"))
        ts(X("o32"), X("q32"), 15, None, OP.bitwise_and, None, g_("q32"), g_("o32"))
        if t < 2:
            tt(X("q32"), X("o32"), pk, OP.add, B_(4) + g_("o32"), g_("q32"))
            tc(X("of2"), X("q32"), g_("q32"), g_("of2"))
            vop("tc", cv(n, 4), g_("of2", "vsel"), ["x"], T.xt[:].indirect(X("of2")), X("vsel"))
        else:
            tt(X("q32"), X("o32"), T.c16[:, c0:c0 + e], OP.add, ["c16"] + g_("o32"), g_("q32"))
            tc(X("of2"), X("q32"), g_("q32"), g_("of2"))
            flex(X("sel"), TAB.indirect(X("of2")), AF.Copy, ["x"] + g_("of2"), g_("sel"), None, 1.5)
            mm(g_("win"), B_(5), (P_(5), [("B1", win)]))
            flex(X("ax0"), P_(5), AF.Copy, B_(5), g_("ax0"), None)
            mm(g_("vsel", "sel"), B_(5), (P_(5), [("I", X("vsel")), ("mI", X("sel"))]))
            tt(X("c8f"), P_(5), X("ax0"), OP.mult, B_(5) + g_("ax0"), g_("c8"))
            tt(T.ysb[:, b:b + n], T.ysb[:, b:b + n], X("c8f"), OP.add, g_("c8", "ysb"), g_("ysb"), 2)
        now[0] = "spans" + h
        MM(["I32"] + g_("win"), B_(8), [(P_(8 + j), M("I32"), win, False, j == 1 and n == 128) for j in (0, 1)])
        MM(["I32"] + g_("win"), B_(w0), [(P_(w0 + j), M("I32"), win, False, j == 3) for j in range(4)])
        flex(wx(-1, 2), P_(8, 2), AF.Relu, B_(8), g_("wx0"), (-32.0, 0.0, OP.add, OP.max), bias=-32.0)
        flex(wx(1, 4), P_(w0, 4), AF.Relu, B_(w0), g_("wx"), (-26.0, 0.0, OP.add, OP.max), bias=-26.0)
        y0, l0 = (0, 8) if n == 128 else (8, 0)
        mm(g_("wx", "win"), B_(y0), *[(P_(y0 + j - 1), [("B1", wx(j)), (("B1", "BX2", "BX3")[j - 1], win)]) for j in (1, 2, 3)])
        act(X("ax"), P_(y0, 3), AF.Abs, B_(y0) + ["co5"], g_("ax"), bias=co(5))
        tab, col = table(l0, 5)
        xq = l0 if n == 128 else 5
        mm([cg] + g_("wx0"), B_(l0, 8), (P_(xq), [("LEq", wx(-1))]),
           *[(col(4 - d, s), [("S%d" % d if d else "I", Cp(s))] + ([("LE%d" % d, X("wx", n + 64 * s, n + 64 * s + 64))] if d else [])) for d in range(5) for s in parts])
        scan(X("sn"), T.q5[:, 0:5 * n], tab, OP.add, OP.max, B_(l0, 8) + ["q5"], g_("sn"))
        mm(g_("wx", "win"), B_(15), (P_(15), [("B1", wx(4)), ("BX32", win)]))
        ts(P_(15), P_(15), co(4), None, OP.is_equal, None, B_(15) + ["co4"], g_("m4"))
        nc, nl = "nc%d%s" % (t, h), "nl%d%s" % (t, h)
        tt(NC, X("sn", 4, 5 * n, 5), P_(xq), OP.subtract, B_(xq) + g_("sn"), [nc])
        if t < 2:
            send(("c" + h, t + 1), NC, [nc])
        e0 = 0 if n == 128 else 12
        mm(g_("wx", "ax"), B_(e0), *[(P_(e0 + j - 1), [("B1", wx(j + 1)), ("mB1", wx(j)), ("mI4", X("ax", n * j - n, n * j))]) for j in (1, 2, 3)])
        flex(X("ex", 0, 3 * n), P_(e0, 3), AF.Relu, B_(e0), g_("ex"), (0.0, None, OP.max))
        tt(X("t4"), NC, P_(15), OP.mult, [nc] + B_(15) + g_("m4"), g_("t4"))
        n0 = 12 if n == 128 else 0
        mm(g_("zw", "t4"), B_(n0), (P_(n0), [("BW", X("z4")), ("B8", X("t4"))]))
        tc(X("n4"), P_(n0), B_(n0), g_("n4"))
        ts(X("n5"), X("n4"), 3, 3, OP.arith_shift_right, OP.bitwise_and, g_("n4"), g_("n5"))
        tt(X("n4m"), X("n5"), P_(15), OP.mult, B_(15) + g_("n5", "m4"), g_("n4m"))
        mm(["km1"] + g_("wx", "ex", "ex3"), B_(y0), (P_(y0), [("BQ0", wx(1)), ("mI", T.km1[:, 0:n])] + [("I", X("ex", n * j, n * j + n)) for j in range(4)]))
        tt(NL, X("n4m"), P_(y0), OP.add, B_(y0) + g_("n4m"), [nl])
        if t < 2:
            send(("l" + h, t + 1), NL, [nl])
        now[0] = "end"
        mm(["kmh", "ff" + h] + g_("vsel"), B_(6), (P_(6), [("I", F), ("I", X("vsel")), ("I", T.kmh[:, 0:n])]))
        lin(X("f1"), P_(6), 0.5, 12582912.0, B_(6), g_("f1"))
        lin(F, X("f1"), 1.0, -12582912.0, g_("f1"), ["ff" + h])

    for t in range(3):
        if t == 1:
            send(("s", 2), T.rec1[:, 512:1024], ["s1"])
        for part in [stream(t, h) for h in CH] * 2:
            next(part, None)
    dma("y", "o_c", T.yc[:], T.nr2[:, 0:256], ["nc2" + h for h in CH], [])
    dma("y", "o_l", T.yl[:], T.nr2[:, 256:512], ["nl2" + h for h in CH], [])
    dma("y", "o_f", T.yf[:], T.ff[:], ["ff" + h for h in CH], [])
    dma("y", "o_s", T.ys[:], T.ysb[:], ["ysb" + h for h in CH], [])

    Q = {"v": g.vector, "s": g.scalar, "t": g.tensor, "g": g, "y": g.sync}
    cnt = {"v": 0, "s": 0, "t": 0, "g": 0}
    known = {q: {} for q in Q}
    lw, rd, bank = {}, {}, {}
    if not KEEP:
        turn = sorted((t, k + LAG[h][t] + (LAG[h][t + 1] - LAG[h][t]) * k / 4, -k, h, i, j) for (t, k, h, s, i), j in gat.items() if "%d%s%d" % (k, h, s) not in VG[t])
        KEEP.append(order([(n[0], n[1], n[2], n[3][0]) for n in nodes], [(x[-1], y[-1]) for x, y in zip(turn, turn[1:])],
                          [AHEAD.get(x, 0) for x in parts_of], parts_of))
    for _, j, a in KEEP[0]:
        (q, _, f), (_, r, w, kind) = nodes[j][0][a], nodes[j]
        if kind[0] == "arr":
            for t in w:
                lw[t], rd[t] = [(kind[1], kind[2], {})], []
            continue
        own, evs = "e_" + q, []
        for t in r + w:
            if t[0] == "#":
                evs += [e for e in bank.get(t, {}).values() if e[0] != own]
            elif t[0] == "+":
                evs += rd.get(t[1:], [])
            else:
                evs += lw.get(t, []) + (rd.get(t, []) if t in w else [])
        best = {}
        for sem, val, clk in evs:
            if known[q].get(sem, 0) < val and (sem not in best or best[sem][0] < val):
                best[sem] = (val, clk)
        for sem, (val, clk) in best.items():
            if not any(o != sem and best[o][1].get(sem, 0) >= val for o in best):
                Q[q].wait_ge(T.sem[sem], val)
        for sem, (val, clk) in best.items():
            for k, x in list(clk.items()) + [(sem, val)]:
                known[q][k] = max(known[q].get(k, 0), x)
        if kind[0] == "send":
            f()
            ev = (sends[-1][0], sends[-1][1], dict(known[q]))
        elif kind[0] == "dma":
            f().then_inc(T.sem[kind[1]], 16)
            ev = (kind[1], 16, dict(known[q]))
        else:
            cnt[q] += 1
            f().then_inc(T.sem[own], 1)
            ev = (own, cnt[q], dict(known[q]))
            ev[2][own] = cnt[q]
        for t in set(r + w):
            if t[0] == "#":
                bank.setdefault(t, {})[ev[0]] = ev
            elif t[0] == "+":
                lw.setdefault(t[1:], []).append(ev)
            elif t in w:
                lw[t], rd[t] = [ev], []
            else:
                rd[t] = [e for e in rd.get(t, []) if e[0] != ev[0]] + [ev]
    for q in ("v", "s", "t", "g"):
        g.wait_ge(T.sem["e_" + q], cnt[q])
    for s in ("o_c", "o_l", "o_f", "o_s"):
        g.wait_ge(T.sem[s], 16)
    for s, n in sends:
        g.wait_ge(T.sem[s], n)
